import numpy as np, ml_dtypes
CORES = [16,18,20,22]
N = 4
BF = ml_dtypes.bfloat16
W, L, RO, PX, LIM = 4096, 256, 5, 1, 10
def parts(rng):
    X = rng.integers(0, 64, (N, 8, 16, W)); H = rng.integers(0, 2 * W, (N, 8, 16, L)); c = rng.integers(0, W, (N, 8, L)); z = rng.integers(0, 64, (N, 8, 16, L))
    return X, H, c, z, np.argsort(rng.random((N, 8, W)), axis=-1).astype(np.int64)
def pack(X, H, c, z, nx):
    return {"xt": np.ascontiguousarray(X.reshape(N, 128, W)).astype(np.float32).astype(BF), "mem": np.ascontiguousarray(H.reshape(N, 128, L)).astype(np.int32),
            "plc": np.ascontiguousarray(c).astype(np.int32), "zt": np.ascontiguousarray(z.reshape(N, 128, L)).astype(np.float32).astype(BF), "nxt": np.ascontiguousarray(nx).astype(np.int32)}
def choose(X, H, c, z, pen):
    e = H >> 1; d = np.where((H & 1) == 1, -e, e); cc = c[:, :, None, :]
    pl = np.concatenate([(cc + d) % W, (cc - d) % W], axis=2); co = []
    for h in (0, 1):
        v = np.take_along_axis(X, np.ascontiguousarray(pl[:, :, 16 * h:16 * h + 16]).reshape(N, 8, 1, 16 * L), 3).reshape(N, 8, 16, 16, L)
        co.append(np.add.reduce(np.abs(v - z[:, :, :, None, :]), axis=2) + 4 * np.arange(16)[:, None] + h * pen[:, None, None, None])
    return pl, np.argmin(np.concatenate(co, axis=2), axis=2)
def setup_inputs(rng):
    return pack(*parts(rng))
def setup_inputs_corners(rng):
    X, H, c, z, nx = parts(rng); far = np.array([0, 1, W // 2 - 1, W // 2, W // 2 + 1, W - 1]); spots = np.array([0, 1, W // 2, W - 1])
    for p in range(N):
        for g in range(8):
            k = (p + g) % 8
            if k == 0: H[p, g] = 2 * rng.choice(far, (16, L)) + rng.integers(0, 2, (16, L)); c[p, g] = rng.choice(spots, L)
            if k == 1: H[p, g] = H[p, g, :1].copy()
            if k == 2: H[p, g] = 2 * (H[p, g, :1] >> 1) + (np.arange(16) % 2)[:, None]
            if k == 3: nx[p, g] = np.arange(W); c[p, g] = rng.choice(spots, L)
            if k == 4: nx[p, g] = rng.choice(np.array([0, W - 1]), W)
            if k == 5: nx[p, g] = (np.arange(W) + 1) % W; H[p, g] = rng.integers(0, 4, (16, L))
            if k == 6: H[p, g] = np.where(rng.random((1, L)) < 0.5, 0, 2 * W - 1)
            if k == 7: c[p, g] = rng.choice(spots, L); X[p, g] = rng.integers(0, 64, (16, 3))[:, rng.integers(0, 3, W)]
    return pack(X, H, c, z, nx)
def setup_inputs_crowd(rng):
    X, H, c, z, nx = parts(rng); few = int(rng.integers(1, 4))
    for p in range(N):
        for g in range(8):
            P = rng.permutation(np.arange(1, W - 1))[:3]; k = (p + g) % 5
            if g % 4 == 0: P[0] = 0
            if g % 4 == 3: P[0] = W - 1
            near = p >= N - 2 and g == (-p) % 5
            if near:
                x0 = np.full(16, 32) if p == N - 2 else X[p, g][:, P[0]].copy()
                far = np.full(16, 62) if p == N - 2 else np.minimum((x0 + 32) % 64, 62)
                X[p, g] = far[:, None] + rng.integers(0, 2, (16, W)) * (np.arange(16) < 4)[:, None]; X[p, g, :, P[0]] = x0
            to = np.full(L, P[0])
            if k == 1: to[0] = P[1]
            if k == 2: to[L - 1] = P[1]
            if k == 3: to = P[rng.integers(0, 3, L)]
            if k == 4: to = rng.permutation(W)[:L]
            if p == N - 2:
                H[p, g] = rng.integers(0, 2, (16, L)); c[p, g] = to; z[p, g] = np.where(X[p, g][:, to] < 32, 63, 0)
                if near:
                    for i in (L - 1, 0, L // 2)[:few]:
                        e = int(rng.integers(1, W // 2)); s = int(rng.integers(0, 2))
                        H[p, g, 0, i] = 2 * e + s; c[p, g, i] = (P[0] + (-e if s == 1 else e)) % W
                continue
            rev = np.full(L, 1) if p in (0, N - 1) else (rng.permutation(L) < L // 2 - int(g == 7)).astype(np.int64)
            if p == N - 1 and g == 7: rev[L - 1] = 0
            e = rng.integers(1, W // 2, L); s = rng.integers(0, 2, L); d = np.where(s == 1, -e, e)
            c[p, g] = (to + np.where(rev == 1, d, -d)) % W; H[p, g, 0] = 2 * e + s
            z[p, g] = np.clip(X[p, g][:, to] + rng.integers(-2, 3, (16, L)), 0, 63)
    return pack(X, H, c, z, nx)
def setup_inputs_ends(rng):
    X = np.where(rng.random((N, 8, 1, W)) < 0.5, 63 * rng.integers(0, 2, (N, 8, 1, W)), 63 * rng.integers(0, 2, (N, 8, 16, W)))
    z = np.where(rng.random((N, 8, 1, L)) < 0.5, 63 * rng.integers(0, 2, (N, 8, 1, L)), 63 * rng.integers(0, 2, (N, 8, 16, L)))
    H = (2 * W - 1) * rng.integers(0, 2, (N, 8, 16, L)); c = (W - 1) * rng.integers(0, 2, (N, 8, L)); nx = (W - 1) * rng.integers(0, 2, (N, 8, W))
    o = rng.integers(0, 2, (N, 8)); o[:, 7] = 1; nx[:, :, 0] = (W - 1) * o; nx[:, :, W - 1] = (W - 1) * (1 - o)
    for q in (0, 1, W - 2, W - 1):
        X[:, 1, :, q] = 63; X[:, 6, :, q] = 0; X[:, 7, :, q] = 0 if q < 2 else 63
    z[:, 1] = 63 * rng.integers(0, 2, (N, 1, L)); z[:, 6] = 63 * rng.integers(0, 2, (N, 1, L))
    for i in (0, 1, L - 1): z[:, 1, :, i] = 0; z[:, 6, :, i] = 63
    rest = np.add.reduce((choose(X, H, c, z, np.zeros(N, np.int64))[1] >> 4)[:, :7].reshape(N, -1), axis=1)
    for p in range(N):
        n = 32 + ((0 if p == 1 else 31) - int(rest[p])) % 32
        m = np.zeros(L, bool); m[0] = True; m[L - 1] = True; m[rng.permutation(np.arange(1, L - 1))[:n - 2]] = True
        cc = (W - 1) * rng.integers(0, 2, L); cc[m] = 0; zz = 63 * rng.integers(0, 2, L); zz[m] = 63; zz[(~m) & (cc == 0)] = 0
        c[p, 7] = cc; z[p, 7] = zz[None, :]; H[p, 7, 0] = np.where(m | (zz == 0), 2 * W - 1, 0)
        for i in (0, L - 1): H[p, 7, 12:, i] = 2 * W - 1
    return pack(X, H, c, z, nx)
def setup_inputs_spread(rng):
    X = np.minimum((np.exp2(6 * rng.random((N, 8, 1, W))) * rng.random((N, 8, 16, W))).astype(np.int64), 63)
    z = np.minimum((np.exp2(6 * rng.random((N, 8, 1, L))) * rng.random((N, 8, 16, L))).astype(np.int64), 63)
    e = np.clip(np.power(float(W), rng.random((N, 8, 16, L))).astype(np.int64) - 1, 0, W - 1)
    H = 2 * e + (rng.random((N, 8, 16, L)) < rng.random((N, 8, 1, 1))).astype(np.int64)
    c = np.minimum((W * rng.random((N, 8, L)) ** 3).astype(np.int64), W - 1); nx = np.minimum((W * rng.random((N, 8, W)) ** 2).astype(np.int64), W - 1)
    return pack(X, H, c, z, nx)
def setup_inputs_ties(rng):
    X, H, c, z, nx = parts(rng)
    X[:, 2:7] = 4 * rng.integers(0, 12, (N, 1, 16, 1)) + 4 * rng.integers(0, 3, (N, 5, 16, W)) * (np.arange(16) < 2)[:, None]
    z[:, 2:7] = 4 * rng.integers(0, 16, (N, 5, 16, L)); X[:, 7] = rng.integers(0, 64, (N, 16, 1)); X[:, :2] = 0
    X[:, 6] = 63 - (np.argsort(rng.random((N, 16, W)), axis=1) < rng.integers(0, 9, (N, 1, W))).astype(np.int64); z[:, 6] = 0
    o = N - 1 if PX < N - 1 else PX - 1
    X[o, 6] = 63 - X[o, 6]
    for p in range(N):
        if p < (p ^ PX):
            lo = rng.integers(0, 63 - LIM, (2, 16, L)); n = rng.choice(np.array([0, 7, 8, 9, 10, 16]), (2, 1, L))
            hi = lo + np.where(np.argsort(rng.random((2, 16, L)), axis=1) < n, LIM, LIM + 1); sw = rng.random((2, 1, L)) < 0.5
            z[p, :2] = np.where(sw, hi, lo); z[p ^ PX, :2] = np.where(sw, lo, hi)
    return pack(X, H, c, z, nx)
def check_inputs(d):
    bad = []
    for k, hi in (("xt", 63), ("mem", 2 * W - 1), ("plc", W - 1), ("zt", 63), ("nxt", W - 1)):
        v = np.asarray(d[k]).astype(np.float64)
        if not (np.min(v) >= 0 and np.max(v) <= hi): bad.append("range of " + k)
        elif np.any(v != np.floor(v)): bad.append("whole numbers in " + k)
    return bad
def reference(xt, mem, plc, zt, nxt):
    X = xt.astype(np.float32).astype(np.int64).reshape(N, 8, 16, W); nx = nxt.astype(np.int64)
    H = mem.astype(np.int64).reshape(N, 8, 16, L); c = plc.astype(np.int64); z = zt.astype(np.float32).astype(np.int64).reshape(N, 8, 16, L)
    A = np.zeros(N, np.int64); par = np.arange(N) ^ PX
    for t in range(RO):
        if t > 0: H = np.roll(H, 1, axis=0); c = np.roll(c, 1, axis=0); z = np.roll(z, 1, axis=0)
        pl, w = choose(X, H, c, z, A & 31); rev = w >> 4
        q = np.take_along_axis(pl, w[:, :, None, :], 2)[:, :, 0]
        step = np.take_along_axis(H, (w & 15)[:, :, None, :], 2) ^ rev[:, :, None, :]
        A = np.add.reduce(rev.reshape(N, -1), axis=1)
        xq = np.take_along_axis(X, q[:, :, None, :], 3); half = (xq + z) >> 1
        u, first = np.unique((np.arange(N * 8).reshape(N, 8, 1) * W + q).reshape(-1), return_index=True)
        X[u // (8 * W), (u // W) % 8, :, u % W] = half.transpose(0, 1, 3, 2).reshape(-1, 16)[first]
        z = np.abs(z - xq); c = np.take_along_axis(nx, q, 2)
        H = np.concatenate([step, H[:, :, :15]], axis=2)
        alike = np.add.reduce((np.abs(z - z[par]) <= LIM).astype(np.int64), axis=2) >= 9
        H = np.concatenate([H[:, :, :8], np.where(alike[:, :, None, :], H[par][:, :, 8:], H[:, :, 8:])], axis=2)
    return {"yx": X.reshape(N, 128, W).astype(np.float32).astype(BF), "yh": H.reshape(N, 128, L).astype(np.float32), "yc": c.astype(np.float32), "yz": z.reshape(N, 128, L).astype(np.float32).astype(BF)}

@@ -1,0 +1,567 @@
+from concourse.bass import DstId, RemoteDMATransfer
+from concourse.mybir import AluOpType as ALU, AxisListType as AX, ActivationFunctionType as AF
+
+RO = 5
+SLOT = 144
+ROUTE = ("SSSVSVSV", "VVVVVVVV")
+SAME_QUEUE_WAW = True
+
+SCRATCH = {
+    "tab": ("sbuf", [128, 4112], "bfloat16"), "nxb": ("sbuf", [128, 4112], "bfloat16"),
+    "gb": ("sbuf", [128, 8192], "bfloat16"), "ab": ("sbuf", [128, 8192], "bfloat16"),
+    "msg": ("sbuf", [128, SLOT * 10], "float32"), "pmsg": ("sbuf", [128, SLOT * 12], "float32"),
+    "zin": ("sbuf", [128, 5120], "bfloat16"), "zout": ("sbuf", [128, 1280], "bfloat16"),
+    "pz": ("sbuf", [128, 1536], "bfloat16"),
+    "t32": ("sbuf", [128, 512], "int32"), "o32": ("sbuf", [128, 512], "int32"), "o16": ("sbuf", [128, 512], "uint16"),
+    "kf": ("sbuf", [128, 16], "float32"), "ki": ("sbuf", [128, 16], "int32"), "kc": ("sbuf", [128, 16], "int32"),
+    "pt32": ("sbuf", [128, 16], "int32"),
+    "pt16": ("sbuf", [128, 16], "uint16"), "pd16": ("sbuf", [128, 16], "uint16"), "q16": ("sbuf", [128, 16], "uint16"),
+    "off16": ("sbuf", [128, 32], "uint16"), "kind": ("sbuf", [128, 16], "bfloat16"),
+    "xx": ("sbuf", [128, 256], "float32"), "ff": ("sbuf", [128, 256], "float32"), "ne": ("sbuf", [128, 256], "float32"),
+    "rr": ("sbuf", [128, 256], "float32"), "x2": ("sbuf", [128, 256], "float32"), "f2": ("sbuf", [128, 256], "float32"),
+    "zm": ("sbuf", [128, 128], "bfloat16"), "gq": ("sbuf", [128, 256], "bfloat16"), "hv": ("sbuf", [128, 256], "bfloat16"),
+    "nxg": ("sbuf", [128, 256], "bfloat16"), "al1": ("sbuf", [128, 256], "bfloat16"), "al2": ("sbuf", [128, 256], "bfloat16"),
+    "alk": ("sbuf", [128, 16], "float32"), "dif": ("sbuf", [128, 128], "float32"), "tmp": ("sbuf", [128, 128], "float32"),
+    "cnj": ("sbuf", [128, 16], "float32"), "cnt": ("sbuf", [128, 1], "float32"), "cni": ("sbuf", [128, 2], "int32"),
+    "pnf": ("sbuf", [128, 1], "float32"), "pend": ("sbuf", [128, 128], "bfloat16"),
+    "pi": ("sbuf", [128, 1], "int32"), "pb": ("sbuf", [128, 8], "int32"), "pc": ("sbuf", [128, 16], "float32"),
+    "ci": ("sbuf", [128, 144], "float32"), "c16": ("sbuf", [128, 128], "float32"), "cg": ("sbuf", [128, 128], "float32"),
+    "lio": ("sbuf", [128, 176], "float32"), "lst": ("sbuf", [128, 184], "uint16"),
+    "idn": ("sbuf", [128, 128], "bfloat16"), "nid": ("sbuf", [128, 128], "bfloat16"), "wd": ("sbuf", [128, 144], "bfloat16"),
+    "nwd": ("sbuf", [128, 144], "bfloat16"),
+    "blk": ("sbuf", [128, 128], "float32"), "dia": ("sbuf", [128, 128], "float32"), "rst": ("sbuf", [128, 128], "float32"),
+    "b1": ("sbuf", [128, 256], "bfloat16"), "b2": ("sbuf", [128, 256], "bfloat16"), "kbig": ("sbuf", [128, 64], "bfloat16"),
+    "one": ("sbuf", [128, 128], "bfloat16"), "m160": ("sbuf", [128, 16], "bfloat16"),
+    "inb": ("sbuf", [128, 272], "int32"), "sb": ("sbuf", [128, 256], "int32"), "sg": ("sbuf", [128, 256], "float32"),
+    "ya": ("sbuf", [128, 256], "float32"), "yf": ("sbuf", [128, 272], "float32"), "dup": ("sbuf", [128, 544], "float32"),
+    "trp": ("sbuf", [128, 544], "float32"), "ztb": ("sbuf", [128, 256], "bfloat16"),
+    "nxi": ("sbuf", [128, 256], "int32"), "nxj": ("sbuf", [128, 512], "int32"), "nxh": ("sbuf", [128, 512], "bfloat16"),
+    "fin": ("sbuf", [128, 272], "float32"), "oh1": ("sbuf", [128, 256], "float32"), "oh": ("sbuf", [128, 256], "float32"),
+    "oc": ("sbuf", [128, 16], "float32"), "oz": ("sbuf", [128, 256], "bfloat16"),
+    "key0": ("psum", [128, 512], "float32"), "key1": ("psum", [128, 512], "float32"),
+    "pd0": ("psum", [128, 512], "float32"), "pd1": ("psum", [128, 512], "float32"),
+    "pq": ("psum", [128, 512], "float32"), "ps": ("psum", [128, 512], "float32"),
+    "pa": ("psum", [128, 512], "float32"), "pn": ("psum", [128, 512], "float32"),
+}
+LOADS = ["ld_mem", "ld_plc", "ld_z", "ld_tab", "ld_nx", "nx_hi", "nx_lo", "st_x", "st_h", "st_c", "st_z"]
+SEMAPHORES = (["cV", "cS", "cP", "cG", "sent"] + LOADS
+              + ["%s%d%d" % (k, t, h) for k in ("az", "af", "bz", "bf", "du") for t in range(1, RO + 1) for h in range(2)])
+
+L1, L2, LZ, LF1, LF2, LR, LJ = 0, 34, 54, 118, 152, 54, 170
+PAR = dict(cyc=1.04e-3, gat=1.56, sca=3.8, pec=0.55e-3, hop=0.10, remote=2.6, local=2.0, route=ROUTE)
+
+
+def A(name, lo=0, hi=None, step=1):
+    return (name, lo, SCRATCH[name][1][1] if hi is None else hi, step)
+
+
+def IND(win, off):
+    return ("*", win, off)
+
+
+def build(T, topo, rank):
+    ops = []
+    visit = [None]
+    CYC, GAT, SCA, PEC, REMOTE, LOCAL, ROUTE = [PAR[k] for k in ("cyc", "gat", "sca", "pec", "remote", "local", "route")]
+    N = len(T.cores)
+    me = T.cores[rank]
+
+    def ap(a):
+        if not isinstance(a, tuple):
+            return a
+        if a[0] == "*":
+            return ap(a[1]).indirect(ap(a[2]))
+        return T[a[0]][:, a[1]:a[2]:a[3]] if a[3] != 1 else T[a[0]][:, a[1]:a[2]]
+
+    def regs(xs):
+        out = []
+        for a in xs:
+            if isinstance(a, tuple):
+                out += [a[1], a[2]] if a[0] == "*" else [a]
+        return out
+
+    def width(a):
+        return 16 * width(a[2]) if a[0] == "*" else len(range(a[1], a[2], a[3]))
+
+    def two(a):
+        return SCRATCH[a[0]][2] in ("bfloat16", "uint16")
+
+    def add(q, name, fn, rd, wr, cost, lat=0.0, sem=None, val=0, after=None):
+        r = regs(rd)
+        w = []
+        for a in wr:
+            if a[0] == "*":
+                w.append(a[1]); r.append(a[2])
+            else:
+                w.append(a)
+        t = visit[0]
+        ops.append(dict(t=t or 0, cls=name if t is None else name[:2] + name[3:], q=q, name=name, fn=fn, rd=r, wr=w, cost=cost, lat=lat, sem=sem, val=val, after=after))
+
+    def vcost(out, ins, both=False):
+        if out[0] == "*":
+            return 0.05 + width(out) * SCA * CYC
+        if ins[0][0] == "*":
+            return 0.05 + width(out) * GAT * CYC
+        f = 2.0 if both else (0.5 if two(out) and all(two(a) for a in ins) else 1.0)
+        return max(64, width(ins[0]) * f) * CYC
+
+    def tt(name, out, a, b, op):
+        both = a[0] == "*" or (SCRATCH[a[0]][0] == "sbuf" and SCRATCH[b[0]][0] == "sbuf")
+        add("V", name, lambda g: [g.vector.tensor_tensor(ap(out), ap(a), ap(b), op)], [a, b], [out], vcost(out, [a, b], both))
+
+    def ts(name, out, a, s1, op0, s2=None, op1=None):
+        if op1 is None:
+            fn = lambda g: [g.vector.tensor_scalar(ap(out), ap(a), ap(s1), None, op0)]
+        else:
+            fn = lambda g: [g.vector.tensor_scalar(ap(out), ap(a), ap(s1), ap(s2), op0, op1)]
+        add("V", name, fn, [a, s1, s2], [out], vcost(out, [a]))
+
+    def cp(name, out, a):
+        add("V", name, lambda g: [g.vector.tensor_copy(ap(out), ap(a))], [a], [out], vcost(out, [a]))
+
+    def scan(name, out, a, b):
+        add("V", name, lambda g: [g.vector.tensor_tensor_scan(ap(out), ap(a), ap(b), 0.0, ALU.mult, ALU.add)], [a, b], [out], vcost(out, [a]))
+
+    def fill(name, out, v):
+        add("V", name, lambda g: [g.vector.memset(ap(out), v)], [], [out], vcost(out, [out]))
+
+    def act(name, out, a, func, bias=0.0, scale=1.0, acc=None):
+        c = 0.065 + width(out) * GAT * CYC if a[0] == "*" else max(64, width(out)) * CYC + 0.03
+        if acc is not None:
+            fn = lambda g: [g.scalar.activation(ap(out), ap(a), func, accum_out=ap(acc))]
+        elif bias == 0.0 and scale == 1.0:
+            fn = lambda g: [g.scalar.activation(ap(out), ap(a), func)]
+        else:
+            fn = lambda g: [g.scalar.activation(ap(out), ap(a), func, bias=bias, scale=scale)]
+        add("S", name, fn, [a], [out] + ([acc] if acc else []), c)
+
+    def mm(name, items):
+        c = sum(max(64, width(i[2])) * (1 if two(i[2]) else 4) for i in items) * PEC
+        add("P", name, lambda g: [g.tensor.matmul(ap(o), ap(l), ap(r), s, e) for o, l, r, s, e in items],
+            [x for i in items for x in i[1:3]], [i[0] for i in items], c, lat=0.1)
+
+    def iota(name, out, pat, base, ch=0):
+        if SCRATCH[out[0]][2] == "int32":
+            fn = lambda g: [g.iota(ap(out), pat, base, ch)]
+        else:
+            fn = lambda g: [g.iota(ap(out), pat, base, ch, allow_small_or_imprecise_dtypes=True)]
+        add("G", name, fn, [], [out], 0.13 + 2 * width(out) * CYC)
+
+    def dma(q, name, out, a, rd, wr, lat, sem=None, val=16):
+        eng = (lambda g: g.sync) if q == "Y" else (lambda g: g.scalar)
+        add(q, name, lambda g: [eng(g).dma_start(out, a)], rd, wr, 0.06, lat=lat, sem=sem or name, val=val)
+
+    def sel16(name, out, src):
+        mm(name, [(out, A("wd", 15 - p, 143 - p), A(src[0], src[1] + p, src[2], 16), p == 0, p == 15) for p in range(16)])
+
+    def send(name, src, dsts):
+        def fn(g):
+            trs = []
+            for i, (r, land, sem) in enumerate(dsts):
+                es = topo.engines(me, T.cores[r])
+                k = len(es) // len(dsts)
+                rid, pid, _ = topo.addr(T.cores[r])
+                trs.append((rid, pid, sum(1 << e for e in es[i * k:(i + 1) * k]), land, sem))
+            if len(trs) == 1:
+                rid, pid, m, land, sem = trs[0]
+                g.remote_dma(ap(land), ap(src), T.sem[sem], T.sem.sent, pid, rid, m)
+            else:
+                g.remote_dma_fused([RemoteDMATransfer(dst_ids=[DstId(rid=rid, pnc=pid)], dma_engine_mask=m, remote_sem=T.sem[sem],
+                                                      src=ap(src), dst=ap(land)) for rid, pid, m, land, sem in trs], local_sem=T.sem.sent)
+            return []
+        k = len(topo.engines(me, T.cores[dsts[0][0]])) // len(dsts)
+        add("G", name, fn, [src], [], 0.5, sem="sent", val=k * len(dsts))
+
+    def recv(name, land, src_rank, nwrites, after):
+        k = len(topo.engines(T.cores[src_rank], me)) // nwrites
+        add(None, name, None, [], [land], 0.0, lat=REMOTE, sem=name, val=k, after=after)
+
+    def lst(lo, n):
+        return A("lst", lo, lo + n)
+
+    def pc(i):
+        return A("pc", i, i + 1)
+
+    dma("Y", "ld_mem", T.inb[:, 0:256], T.mem[:], [], [A("inb", 0, 256)], LOCAL)
+    dma("Y", "ld_plc", T.inb[:, 256:272], T.plc[:], [], [A("inb", 256, 272)], LOCAL)
+    dma("S", "ld_z", T.ztb[:], T.zt[:], [], [A("ztb")], LOCAL)
+    dma("S", "ld_tab", T.tab[:, 16:4112], T.xt[:], [], [A("tab", 16, 4112)], LOCAL + 4.0)
+    dma("Y", "ld_nx", T.nxi[:], T.nxt[:], [], [A("nxi")], LOCAL + 4.5)
+
+    iota("i_p", A("pi"), [[0, 1]], 0, 1)
+    iota("i_l1", A("lio", L1, L1 + 32), [[-16, 16], [0, 2]], 255)
+    iota("i_l1c", A("lio", L1 + 32, L1 + 34), [[0, 2]], 271)
+    iota("i_lz", A("lio", LZ, LZ + 64), [[-128, 2], [0, 4], [-16, 8]], 255)
+    iota("i_l2", A("lio", L2, L2 + 20), [[256, 2], [2, 10]], -2)
+    iota("i_ci", A("ci"), [[1, 144]], 0)
+    iota("i_b2", A("b2"), [[1, 256]], 0)
+    for b in range(2):
+        iota("i_b1%d" % b, A("b1", 128 * b, 128 * b + 128), [[256, 2], [2048, 8], [0, 8]], 16384 * b)
+    iota("i_c16", A("c16"), [[0, 8], [1, 16]], 0)
+    iota("i_cg", A("cg"), [[16, 8], [0, 16]], 0)
+    iota("i_lf1", A("lio", LF1, LF1 + 32), [[136, 2], [1, 8], [0, 2]], 8)
+    iota("i_lf2", A("lio", LF2, LF2 + 16), [[-32, 16]], 495)
+    iota("i_lf2c", A("lio", LF2 + 16, LF2 + 18), [[0, 2]], 527)
+    iota("i_nx0", A("nxb"), [[0, 4112]], 0)
+    ts("p0", A("pb", 0, 1), A("pi"), 7, ALU.bitwise_and)
+    ts("p1", A("pb", 1, 2), A("pi"), 3, ALU.logical_shift_right, 1, ALU.bitwise_and)
+    ts("p2", A("pb", 2, 3), A("pi"), 16, ALU.bitwise_and)
+    ts("p3", A("pb", 3, 4), A("pi"), 15, ALU.bitwise_and)
+    ts("p4", A("pb", 4, 5), A("pi"), 112, ALU.bitwise_and)
+    ts("p5", A("pb", 5, 6), A("pi"), 127, ALU.bitwise_and)
+    cp("pc", A("pc", 0, 6), A("pb", 0, 6))
+    ts("l1", lst(L1, 34), A("lio", L1, L1 + 34), pc(3), ALU.subtract)
+    ts("lz", lst(LZ, 64), A("lio", LZ, LZ + 64), pc(3), ALU.subtract)
+    ts("p6", pc(6), pc(0), 32.0, ALU.mult, pc(2), ALU.add)
+    ts("l2", lst(L2, 20), A("lio", L2, L2 + 20), pc(6), ALU.add, pc(1), ALU.add)
+    ts("p7", pc(7), pc(2), pc(0), ALU.subtract)
+    for h in range(2):
+        ts("l2c%d" % h, lst(L2 + 10 * h, 1), pc(7), 527.0 - 8 * h, ALU.add)
+    ts("lj", lst(LJ, 8), A("ci", 0, 8), 0.0, ALU.mult, pc(0), ALU.add)
+    ts("idn", A("idn"), A("ci", 0, 128), pc(5), ALU.is_equal)
+    ts("nid", A("nid"), A("idn"), -1.0, ALU.mult)
+    ts("p8", pc(8), pc(4), 15.0, ALU.add)
+    ts("wd", A("wd"), A("ci"), pc(8), ALU.is_equal, 512.0, ALU.mult)
+    ts("nwd", A("nwd"), A("wd"), -1.0, ALU.mult)
+    ts("blk", A("blk"), A("cg"), pc(4), ALU.is_equal)
+    ts("dia", A("dia"), A("c16"), pc(3), ALU.is_equal)
+    ts("rst", A("rst"), A("c16"), pc(3), ALU.not_equal)
+    fill("spare", A("tab", 0, 16), 0.0)
+    fill("kbig", A("kbig"), 512.0)
+    fill("one", A("one"), 1.0)
+    fill("m160", A("m160"), -160.0)
+    ts("p9", pc(9), pc(3), 8.0, ALU.mult)
+    ts("lf1", lst(LF1, 32), A("lio", LF1, LF1 + 32), pc(9), ALU.add)
+    ts("p10", pc(10), pc(1), -128.0, ALU.mult, pc(3), ALU.subtract)
+    ts("p11", pc(11), pc(10), 143.0, ALU.add)
+    ts("lf1d", lst(LF1 + 32, 2), A("ci", 0, 2), 0.0, ALU.mult, pc(11), ALU.add)
+    ts("p12", pc(12), pc(2), pc(3), ALU.subtract)
+    ts("lf2", lst(LF2, 18), A("lio", LF2, LF2 + 18), pc(12), ALU.add)
+
+    ts("y_s", A("sb"), A("inb", 0, 256), 1, ALU.bitwise_and)
+    ts("y_g", A("sg"), A("sb"), 24577.0, ALU.mult)
+    tt("y_m", A("yf", 0, 256), A("sg"), A("inb", 0, 256), ALU.subtract)
+    ts("y_c", A("yf", 256, 272), A("inb", 256, 272), 28672.0, ALU.add, 2.0, ALU.mult)
+    act("y_d", A("dup"), IND(A("yf"), lst(L1, 34)), AF.Abs, scale=0.5)
+    add("V", "y_t", lambda g: [g.vector.transpose(ap(A("trp")), ap(A("dup")))], [A("dup")], [A("trp")], 544 * CYC)
+    for h in range(2):
+        act("y_l%d" % h, A("msg", SLOT * h, SLOT * h + SLOT), IND(A("trp"), lst(L2 + 10 * h, 9)), AF.Identity, bias=-6144.0)
+        act("z_l%d" % h, A("zin", 512 * h, 512 * h + 512), IND(A("ztb"), lst(LZ + 32 * h, 32)), AF.Copy)
+    ts("nx1", A("nxj", 0, 256), A("nxi"), 4032, ALU.bitwise_and)
+    ts("nx2", A("nxj", 256, 512), A("nxi"), 63, ALU.bitwise_and)
+    cp("nx3", A("nxh"), A("nxj"))
+    dma("Y", "nx_hi", T.nxb[0:128:16, 16:4112], T.nxh[:, 0:256], [A("nxh")], [A("nxb", 0, 2056)], LOCAL + 0.5)
+    dma("Y", "nx_lo", T.nxb[1:128:16, 16:4112], T.nxh[:, 256:512], [A("nxh")], [A("nxb", 2056, 4112)], LOCAL + 0.5)
+
+    prev, part = (rank - 1) % N, rank ^ 1
+
+    def exchange(t, h, zown, own, out):
+        n = "%d%d" % (t, h)
+        src = part if t == RO else prev ^ 1
+        if src == rank:
+            zp, yp = A("zout", 128 * (2 * t - 2 + h), 128 * (2 * t - 1 + h)), A("msg", SLOT * (2 * t - 2 + h) + 72, SLOT * (2 * t - 2 + h) + 136)
+        else:
+            s = 2 * t + h
+            zp, yp = A("pz", 128 * s, 128 * s + 128), A("pmsg", SLOT * s + 72, SLOT * s + 136)
+            w = 1 if t == RO else 2
+            recv("bz" + n, zp, src, w, "sz%d%d" % (t - 1, h))
+            recv("bf" + n, A("pmsg", SLOT * s, SLOT * s + 136), src, w, "sf%d%d" % (t - 1, h))
+        H = lambda b, k=128: A(b, k * h, k * h + k)
+        mm("ad" + n, [(A("pa", 0, 128), A("idn"), zown, True, False), (A("pa", 0, 128), A("nid"), zp, False, True)])
+        act("a1" + n, H("al1"), A("pa", 0, 128), AF.Abs)
+        act("a2" + n, H("al2"), H("al1"), AF.Sign, bias=10.5, scale=-1.0)
+        sel16("as" + n, A("pa", 128, 136), H("al2"))
+        ts("ak" + n, H("alk", 8), A("pa", 128, 136), 512.0, ALU.is_ge)
+        tt("df" + n, H("dif", 64), yp, own, ALU.subtract)
+        tt("dm" + n, H("tmp", 64), IND(H("alk", 8), lst(LJ, 4)), H("dif", 64), ALU.mult)
+        tt("sw" + n, out, own, H("tmp", 64), ALU.add)
+
+    def prep(t, h):
+        n, s = "%d%d" % (t, h), 2 * t + h
+        m0, z0 = SLOT * s, 512 * s
+        if t > 0:
+            w = 1 if ((prev ^ 1) + 1) % N == prev else 2
+            recv("az" + n, A("zin", z0, z0 + 128), prev, w, "sz%d%d" % (t - 1, h))
+            recv("af" + n, A("msg", m0 + 8, m0 + SLOT), prev, w, "sf%d%d" % (t - 1, h))
+            add("Y", "du" + n, lambda g: [g.sync.dma_start(T.zin[:, z0 + 128 * r:z0 + 128 * r + 128], T.zin[:, z0:z0 + 128]) for r in (1, 2, 3)],
+                [A("zin", z0, z0 + 128)], [A("zin", z0 + 128, z0 + 512)], 0.2, lat=LOCAL, sem="du" + n, val=48)
+        c = IND(A("msg", m0 + 8, m0 + 16), lst(LJ, 4))
+        for b in range(2):
+            if b and t > 0:
+                exchange(t, h, A("zin", z0, z0 + 128), A("msg", m0 + 80, m0 + SLOT), A("msg", m0 + 80, m0 + SLOT))
+            y, o, nb = A("msg", m0 + 16 + 64 * b, m0 + 80 + 64 * b), 256 * h + 128 * b, n + str(b)
+            tt("ta" + nb, A("t32", o, o + 64), c, y, ALU.add)
+            tt("tb" + nb, A("t32", o + 64, o + 128), c, y, ALU.subtract)
+            ts("to" + nb, A("o32", o, o + 128), A("t32", o, o + 128), 16384 | 4095, ALU.bitwise_and)
+            ts("tu" + nb, A("o16", o, o + 128), A("o32", o, o + 128), -16368.0, ALU.add)
+
+    nr2 = [0]
+
+    def main(t, h):
+        n, s = "%d%d" % (t, h), 2 * t + h
+        z4 = A("zin", 512 * s, 512 * s + 512)
+        key = "key%d" % h
+        mm("kb" + n, [(A(key, 0, 256), A("idn"), A("b1"), True, False), (A(key, 0, 256), A("idn"), A("b2"), False, False)])
+        neg = []
+        for u in range(8):
+            o = 4096 * h + 512 * u
+            gath = IND(A("tab"), A("o16", 256 * h + 32 * u, 256 * h + 32 * u + 32))
+            gu, au = A("gb", o, o + 512), A("ab", o, o + 512)
+            if ROUTE[h][u] != "S":
+                tt("mg%s%d" % (n, u), gu, gath, z4, ALU.subtract)
+                if ROUTE[h][u] == "V":
+                    act("ma%s%d" % (n, u), au, gu, AF.Abs)
+                else:
+                    ts("ma%s%d" % (n, u), au, gu, 0.0, ALU.max, 2.0, ALU.mult)
+                    if u % 2 == 0 or ROUTE[h][u - 1] != "W":
+                        wide = 2 if u % 2 == 0 and ROUTE[h][u + 1] == "W" else 1
+                        neg.append((u, wide))
+            else:
+                pd = A("pd%d" % (nr2[0] % 2)); nr2[0] += 1
+                act("mg%s%d" % (n, u), gu, gath, AF.Copy)
+                mm("md%s%d" % (n, u), [(pd, A("idn"), gu, True, False), (pd, A("nid"), z4, False, True)])
+                act("ma%s%d" % (n, u), au, pd, AF.Abs)
+            if u % 2:
+                w = u // 2
+                for u0, wide in neg:
+                    o0 = 4096 * h + 512 * u0
+                    mm("mw%s%d" % (n, u0), [(A(key, 32 * u0, 32 * (u0 + wide)), A("nwd", 15 - p, 143 - p),
+                                             A("gb", o0 + p, o0 + 512 * wide, 16), False, False) for p in range(16)])
+                neg.clear()
+                if w == 3 and t > 0:
+                    mm("kp" + n, [(A(key, o1, o1 + 64), A("pend"), A("kbig"), False, False) for o1 in (64, 192)])
+                mm("ms%s%d" % (n, w), [(A(key, 64 * w, 64 * w + 64), A("wd", 15 - p, 143 - p),
+                                        A("ab", o - 512 + p, o + 512, 16), False, w == 3 and p == 15) for p in range(16)])
+
+    def tail(t, h):
+        n, s = "%d%d" % (t, h), 2 * t + h
+        m0 = SLOT * s
+        H = lambda b, k=128: A(b, k * h, k * h + k)
+        last = lambda b: A(b, 128 * h + 15, 128 * h + 128, 16)
+        key = "key%d" % h
+        add("V", "mn" + n, lambda g: [g.vector.tensor_reduce(ap(A("kf", 8 * h + j, 8 * h + j + 1)), ap(A(key, j, 256, 8)), AX.X, ALU.min) for j in range(8)],
+            [A(key)], [H("kf", 8)], 8 * 64 * CYC)
+        cp("ki" + n, H("ki", 8), H("kf", 8))
+        ts("pt" + n, H("pt32", 8), H("ki", 8), 255, ALU.bitwise_and)
+        cp("pu" + n, H("pt16", 8), H("pt32", 8))
+        tt("xx" + n, H("xx"), IND(H("o32", 256), H("pt16", 8)), A("dia"), ALU.mult)
+        scan("ff" + n, H("ff"), A("rst"), H("xx"))
+        mm("qr" + n, [(A("pq", 0, 128), A("blk"), H("xx"), True, True)])
+        tt("ne" + n, H("ne"), A("pq", 0, 128), H("ff"), ALU.not_equal)
+        scan("rr" + n, H("rr"), H("ne"), H("xx"))
+        ts("of" + n, A("off16", 16 * h, 16 * h + 16, 2), last("rr"), -16368.0, ALU.add, pc(3), ALU.max)
+        zo = A("zout", 128 * s, 128 * s + 128)
+        z1 = A("zin", 512 * s, 512 * s + 128)
+        ts("qq" + n, H("q16", 8), last("ff"), -16368.0, ALU.add)
+        if h == 0:
+            dd = A("ps", 128, 256)
+            act("gq" + n, H("gq"), IND(A("tab"), H("q16", 8)), AF.Copy)
+            mm("xz" + n, [(dd, A("idn"), H("gq"), True, False), (dd, A("nid"), z1, False, True),
+                          (A("ps", 0, 128), A("idn"), H("gq"), True, False), (A("ps", 0, 128), A("idn"), z1, False, True)])
+            act("zn" + n, zo, dd, AF.Abs)
+            act("hv" + n, H("hv"), A("ps", 0, 128), AF.Identity, bias=159.75, scale=0.5)
+            plus = lambda j: A("m160")
+        else:
+            ts("pv" + n, H("pd16", 8), H("pt32", 8), 16.0, ALU.mult, pc(3), ALU.add)
+            act("zm" + n, A("zm"), z1, AF.Identity, bias=-192.0)
+            act("zn" + n, zo, IND(H("gb", 4096), H("pd16", 8)), AF.Abs)
+            act("hv" + n, H("hv"), IND(H("gb", 4096), H("pd16", 8)), AF.Identity, bias=191.75, scale=0.5)
+            plus = lambda j: A("zm", 16 * j, 16 * j + 16)
+        act("ng" + n, H("nxg"), IND(A("nxb"), H("q16", 8)), AF.Copy)
+        sel16("cs" + n, A("pn", 0, 8), H("nxg"))
+        act("cn" + n, A("msg", m0, m0 + 8), A("pn", 0, 8), AF.Identity, bias=22528.0, scale=1.0 / 512)
+        tt("x2" + n, H("x2"), IND(H("t32", 256), H("pt16", 8)), A("dia"), ALU.mult)
+        scan("f2" + n, H("f2"), A("rst"), H("x2"))
+        tt("vn" + n, A("msg", m0 + 8, m0 + 16), last("f2"), A("msg", m0 + 8, m0 + 16), ALU.subtract)
+        s1, n1 = s + 2, "%d%d" % (t + 1, h)
+        dz, df = [], []
+        if t + 1 < RO:
+            dz.append(((rank + 1) % N, A("zin", 512 * s1, 512 * s1 + 128), "az" + n1))
+            df.append(((rank + 1) % N, A("msg", SLOT * s1 + 8, SLOT * s1 + SLOT), "af" + n1))
+        other = part if t + 1 == RO else (part + 1) % N
+        if other != rank:
+            dz.append((other, A("pz", 128 * s1, 128 * s1 + 128), "bz" + n1))
+            df.append((other, A("pmsg", SLOT * s1, SLOT * s1 + 136), "bf" + n1))
+        send("sz" + n, zo, dz)
+        send("sf" + n, A("msg", m0, m0 + 136), df)
+        for j in range(8):
+            tt("sc%s%d" % (n, j), IND(A("tab"), A("off16", 16 * h + 2 * j, 16 * h + 2 * j + 1)),
+               A("hv", 128 * h + 16 * j, 128 * h + 16 * j + 16), plus(j), ALU.add)
+
+    def penalty(t):
+        n = str(t)
+        ts("kc" + n, A("kc"), A("ki"), 64, ALU.bitwise_and)
+        ts("kd" + n, A("kind"), A("kc"), 1.0, ALU.is_ge)
+        mm("c1" + n, [(A("pn", 16, 32), A("one"), A("kind"), True, True)])
+        act("c2" + n, A("cnj"), A("pn", 16, 32), AF.Identity, acc=A("cnt"))
+        cp("c3" + n, A("cni", 0, 1), A("cnt"))
+        ts("c4" + n, A("cni", 1, 2), A("cni", 0, 1), 31, ALU.bitwise_and)
+        cp("c5" + n, A("pnf"), A("cni", 1, 2))
+        add("S", "c6" + n, lambda g: [g.scalar.activation(ap(A("pend")), ap(A("idn")), AF.Identity, scale=ap(A("pnf")))],
+            [A("idn"), A("pnf")], [A("pend")], 128 * CYC + 0.03)
+
+    for t in range(RO):
+        visit[0] = t
+        prep(t, 0); main(t, 0); prep(t, 1); main(t, 1); tail(t, 0); tail(t, 1)
+        if t + 1 < RO:
+            penalty(t)
+    visit[0] = None
+
+    dma("Y", "st_x", T.yx[:], T.tab[:, 16:4112], [A("tab")], [], LOCAL + 4.0)
+    for h in range(2):
+        s = 2 * (RO - 1) + h
+        act("fc%d" % h, A("fin", 136 * h, 136 * h + 72), A("msg", SLOT * s, SLOT * s + 72), AF.Copy)
+        exchange(RO, h, A("zout", 128 * s, 128 * s + 128), A("msg", SLOT * s + 72, SLOT * s + 136), A("fin", 136 * h + 72, 136 * h + 136))
+    for h in range(2):
+        act("oz%d" % h, A("oz", 128 * h, 128 * h + 128), IND(A("zout", 1024, 1280), lst(LZ + 32 * h, 8)), AF.Copy)
+    dma("Y", "st_z", T.yz[:], T.oz[:], [A("oz")], [], LOCAL)
+    cp("o_d", A("dup"), IND(A("fin"), lst(LF1, 34)))
+    add("V", "o_t", lambda g: [g.vector.transpose(ap(A("trp")), ap(A("dup")))], [A("dup")], [A("trp")], 544 * CYC)
+    act("o_h", A("oh1"), IND(A("trp"), lst(LF2, 16)), AF.Abs, bias=-0.5, scale=2.0)
+    ts("o_c", A("oc"), IND(A("trp"), lst(LF2 + 16, 1)), -22528.0, ALU.add)
+    ts("o_m", A("oh"), A("oh1"), -1.0, ALU.mult, 12288.5, ALU.add)
+    dma("Y", "st_c", T.yc[:], T.oc[:], [A("oc")], [], LOCAL)
+    dma("S", "st_h", T.yh[:], T.oh[:], [A("oh")], [], LOCAL)
+    return ops
+
+
+def hazards(ops):
+    hist = {}
+    deps = []
+    for i, o in enumerate(ops):
+        d = {}
+        for kind, regs in (("r", o["rd"]), ("w", o["wr"])):
+            for b, lo, hi, _ in regs:
+                psum = SCRATCH[b][0] == "psum"
+                for j, k2, l2, h2 in hist.get(b, ()):
+                    same = ops[j]["q"] == o["q"] and o["q"] in ("V", "S", "P", "G") and ops[j]["sem"] is None
+                    if psum:
+                        d[j] = d.get(j, False) or not same
+                    elif l2 < hi and lo < h2 and (kind == "w" or k2 == "w"):
+                        raw = kind == "r"
+                        d[j] = d.get(j, False) or raw or not same or (SAME_QUEUE_WAW and o["q"] != "P")
+        for kind, regs in (("r", o["rd"]), ("w", o["wr"])):
+            for b, lo, hi, _ in regs:
+                hh = hist.setdefault(b, [])
+                if kind == "w" or SCRATCH[b][0] == "psum":
+                    q = o["q"]
+                    if SCRATCH[b][0] == "psum":
+                        hh[:] = [e for e in hh if ops[e[0]]["q"] == q]
+                    else:
+                        hh[:] = [e for e in hh if not (lo <= e[2] and e[3] <= hi) or e[0] == i]
+                hh.append((i, kind, lo, hi))
+        d.pop(i, None)
+        deps.append(d)
+    return deps
+
+
+def schedule(ops):
+    deps = hazards(ops)
+    idx = {o["name"]: i for i, o in enumerate(ops)}
+    n = len(ops)
+    pre = [dict(d) for d in deps]
+    for i, o in enumerate(ops):
+        if o["after"]:
+            pre[i][idx[o["after"]]] = True
+    succ = [[] for _ in ops]
+    for i in range(n):
+        for j in pre[i]:
+            succ[j].append(i)
+    cost = [max(o["cost"], 1e-4) for o in ops]
+    lag = [o["lat"] + PAR["hop"] for o in ops]
+
+    def place(key, back):
+        before, behind = (succ, pre) if back else (pre, succ)
+        left = [len(b) for b in before]
+        ready = [ops[i]["lat"] if back else 0.0 for i in range(n)]
+        start = [0.0] * n
+        busy = {}
+        avail = {i: key[i] for i in range(n) if left[i] == 0}
+        while avail:
+            i = min(avail, key=avail.get)
+            del avail[i]
+            st = ready[i]
+            if ops[i]["q"]:
+                b = busy.setdefault(ops[i]["q"], [])
+                k = len(b)
+                while k > 0 and b[k - 1][1] > st:
+                    k -= 1
+                while k < len(b) and b[k][0] < st + cost[i]:
+                    st = max(st, b[k][1])
+                    k += 1
+                b.insert(k, (st, st + cost[i]))
+            start[i] = st
+            for k in behind[i]:
+                gap = (lag[k] if pre[i][k] else 0.0) if back else (lag[i] if pre[k][i] else 0.0)
+                ready[k] = max(ready[k], st + cost[i] + gap)
+                left[k] -= 1
+                if left[k] == 0:
+                    avail[k] = key[k]
+        return start, max(start[i] + cost[i] + (0.0 if back else ops[i]["lat"]) for i in range(n))
+
+    def run(plan):
+        if isinstance(plan, str):
+            names = ["period"] + [o["cls"] for o in ops if o["cls"] == o["name"] or o["t"] == 2]
+            plan = dict(zip(names, [0.1 * int(x) for x in plan.split()]))
+        start, total = place([plan.get(o["cls"], 0.0) + plan["period"] * o["t"] for o in ops], False)
+        order = sorted(range(n), key=lambda i: (start[i], i))
+        return {ops[i]["name"]: k for k, i in enumerate(order)}, total, start
+
+    return run, place
+
+
+PLAN = """233 -8 23 -128 87 5 -204 -327 -103 -103 52 -25 -108 -46 -86 216 214 135 -63 154 268 -145 27 -229 -201 -98 32 -154 -381 -263 -146 -79 -446 -218 -166 -13 -424 -204 -64 4 -86 214 87 117 90 174 -168 148 81 143 -63 -292 -158 24 18 -346 -207 -197 -134 -214 -116 -304 -98 54 159 130 128 178 193 204 45 -108 65 25 -33 55 58 -101 62 71 10 -10 -34 -232 23 22 -24 32 -128 57 83 -234 54 102 -171 77 92 103 118 79 40 127 -32 100 226 100 -93 148 99 119 189 140 173 159 110 164 115 190 -11 75 172 -6 -68 84 103 -35 -5 -60 -99 22 52 83 -12 99 105 97 63 115 200 165 -92 121 147 109 99 108 194 68 174 172 -87 151 46 226 -51 174 226 152 236 -7 78 -112 40 -385 -95 -119 -140 -89 -147 -25 125 163 126 61 72 26 186 131 233 94 -62 274 67 209 211 56 241 249 138 161 255 275 105 224 109 129 234 244 94 81 255 279 250 248 20 -47 -9 149 164 151 102 259 298 281 285 20 267 179 144 134 186 278 289 278 389 369 162 138 438 366 434 1053 834 1346 1177 1289 880 905 1346 1099 931 989 1089 1061 834 962 1202 1402 1280 1289 1206 1536 1250 1157 1337 1247 1600 1415 1128 1081 1170 1199 1184 1181"""
+ORDER = {}
+
+
+def rank_program(g, core, T, topo):
+    rank = T.rank_of(core)
+    if rank is None:
+        return
+    if not ORDER:
+        ORDER.update(schedule(build(T, topo, 0))[0](PLAN)[0])
+    ops = build(T, topo, rank)
+    deps = hazards(ops)
+    queue = {"V": g.vector, "S": g.scalar, "P": g.tensor, "G": g, "Y": g.sync}
+    count = {"V": 0, "S": 0, "P": 0, "G": 0}
+    known = {q: {} for q in queue}
+    done = {}
+    sent = 0
+    for i in sorted(range(len(ops)), key=lambda i: ORDER[ops[i]["name"]]):
+        o = ops[i]
+        q = o["q"]
+        if q is None:
+            done[i] = (o["sem"], o["val"], {o["sem"]: o["val"]})
+            continue
+        kn = known[q]
+        need = sorted((done[j] for j, w in deps[i].items() if w), key=lambda d: -len(d[2]))
+        want = {}
+        for sem, val, clock in need:
+            if kn.get(sem, 0) < val:
+                want[sem] = max(want.get(sem, 0), val)
+        for sem, val, clock in need:
+            if want.get(sem) == val and kn.get(sem, 0) < val:
+                queue[q].wait_ge(T.sem[sem], val)
+                for s2, v2 in clock.items():
+                    kn[s2] = max(kn.get(s2, 0), v2)
+        ins = o["fn"](g)
+        if o["sem"] == "sent":
+            sent += o["val"]
+            continue
+        if o["sem"]:
+            for x in ins:
+                x.then_inc(T.sem[o["sem"]], 16)
+            sem, val = o["sem"], o["val"]
+        else:
+            for x in ins:
+                x.then_inc(T.sem["c" + q], 1)
+            count[q] += len(ins)
+            sem, val = "c" + q, count[q]
+        clock = dict(kn)
+        clock[sem] = val
+        done[i] = (sem, val, clock)
+    g.wait_ge(T.sem.sent, sent)
+    for q in count:
+        g.wait_ge(T.sem["c" + q], count[q])
+    for s in ("st_z", "st_c", "st_h", "st_x"):
+        g.wait_ge(T.sem[s], 16)

@@ -1,54 +1,62 @@
 from concourse.bass import DstId, RemoteDMATransfer
-from concourse.mybir import AluOpType as ALU, AxisListType as AX, ActivationFunctionType as AF
+from concourse.mybir import AluOpType as ALU, ActivationFunctionType as AF
 
 RO = 5
 SLOT = 144
-ROUTE = ("SSSVSVSV", "VVVVVVVV")
-SAME_QUEUE_WAW = True
+SPARE = 32
+CFG = dict(route=("CCAACCAA", "DDADDDDB"), first=("CCAACCAA", "DDADDDDB"), last=("CCAACCAA", "DDADDDDB"),
+           dup="VV", merge=False, zq="V", passes=6, xs="VV", cs="SS", wide="12",
+           cyc=0.95e-3, gat=1.56, sca=3.8, pec=0.5e-3, hop=0.18, call=0.5, remote=2.6, local=2.0, table=3.2)
 
 SCRATCH = {
-    "tab": ("sbuf", [128, 4112], "bfloat16"), "nxb": ("sbuf", [128, 4112], "bfloat16"),
+    "tab": ("sbuf", [128, 4096 + SPARE], "bfloat16"), "nxb": ("sbuf", [128, 4096 + SPARE], "bfloat16"),
     "gb": ("sbuf", [128, 8192], "bfloat16"), "ab": ("sbuf", [128, 8192], "bfloat16"),
-    "msg": ("sbuf", [128, SLOT * 10], "float32"), "pmsg": ("sbuf", [128, SLOT * 12], "float32"),
-    "zin": ("sbuf", [128, 5120], "bfloat16"), "zout": ("sbuf", [128, 1280], "bfloat16"),
-    "pz": ("sbuf", [128, 1536], "bfloat16"),
+    "msg": ("sbuf", [128, SLOT * 10], "float32"), "pmsg": ("sbuf", [128, 72 * 10], "float32"),
+    "nz": ("sbuf", [128, 5120], "bfloat16"), "crp": ("sbuf", [128, 128], "float32"),
+    "zin": ("sbuf", [128, 1280], "bfloat16"), "zout": ("sbuf", [128, 1280], "bfloat16"),
+    "pz": ("sbuf", [128, 1536], "bfloat16"), "zb": ("sbuf", [128, 1280], "bfloat16"),
     "t32": ("sbuf", [128, 512], "int32"), "o32": ("sbuf", [128, 512], "int32"), "o16": ("sbuf", [128, 512], "uint16"),
-    "kf": ("sbuf", [128, 16], "float32"), "ki": ("sbuf", [128, 16], "int32"), "kc": ("sbuf", [128, 16], "int32"),
-    "pt32": ("sbuf", [128, 16], "int32"),
+    "kf": ("sbuf", [128, 512], "float32"), "ki": ("sbuf", [128, 16], "int32"), "pt32": ("sbuf", [128, 16], "int32"),
     "pt16": ("sbuf", [128, 16], "uint16"), "pd16": ("sbuf", [128, 16], "uint16"), "q16": ("sbuf", [128, 16], "uint16"),
-    "off16": ("sbuf", [128, 32], "uint16"), "kind": ("sbuf", [128, 16], "bfloat16"),
+    "bx": ("sbuf", [128, 256], "bfloat16"), "off16": ("sbuf", [128, 32], "uint16"), "kind": ("sbuf", [128, 16], "bfloat16"),
     "xx": ("sbuf", [128, 256], "float32"), "ff": ("sbuf", [128, 256], "float32"), "ne": ("sbuf", [128, 256], "float32"),
     "rr": ("sbuf", [128, 256], "float32"), "x2": ("sbuf", [128, 256], "float32"), "f2": ("sbuf", [128, 256], "float32"),
-    "zm": ("sbuf", [128, 128], "bfloat16"), "gq": ("sbuf", [128, 256], "bfloat16"), "hv": ("sbuf", [128, 256], "bfloat16"),
+    "xe": ("sbuf", [128, 256], "float32"), "fe": ("sbuf", [128, 256], "float32"), "nf": ("sbuf", [128, 256], "float32"),
+    "rf": ("sbuf", [128, 256], "float32"),
+    "gq": ("sbuf", [128, 256], "bfloat16"), "hv": ("sbuf", [128, 256], "bfloat16"),
     "nxg": ("sbuf", [128, 256], "bfloat16"), "al1": ("sbuf", [128, 256], "bfloat16"), "al2": ("sbuf", [128, 256], "bfloat16"),
     "alk": ("sbuf", [128, 16], "float32"), "dif": ("sbuf", [128, 128], "float32"), "tmp": ("sbuf", [128, 128], "float32"),
-    "cnj": ("sbuf", [128, 16], "float32"), "cnt": ("sbuf", [128, 1], "float32"), "cni": ("sbuf", [128, 2], "int32"),
+    "cnj": ("sbuf", [128, 16], "float32"), "cnt": ("sbuf", [128, 1], "float32"), "cnf": ("sbuf", [128, 1], "bfloat16"),
     "pnf": ("sbuf", [128, 1], "float32"), "pend": ("sbuf", [128, 128], "bfloat16"),
     "pi": ("sbuf", [128, 1], "int32"), "pb": ("sbuf", [128, 8], "int32"), "pc": ("sbuf", [128, 16], "float32"),
     "ci": ("sbuf", [128, 144], "float32"), "c16": ("sbuf", [128, 128], "float32"), "cg": ("sbuf", [128, 128], "float32"),
-    "lio": ("sbuf", [128, 176], "float32"), "lst": ("sbuf", [128, 184], "uint16"),
+    "cg8": ("sbuf", [128, 128], "float32"), "c32": ("sbuf", [128, 128], "float32"),
+    "lio": ("sbuf", [128, 80], "float32"), "lst": ("sbuf", [128, 96], "uint16"),
     "idn": ("sbuf", [128, 128], "bfloat16"), "nid": ("sbuf", [128, 128], "bfloat16"), "wd": ("sbuf", [128, 144], "bfloat16"),
-    "nwd": ("sbuf", [128, 144], "bfloat16"),
+    "idf": ("sbuf", [128, 128], "float32"), "nif": ("sbuf", [128, 128], "float32"), "bn": ("sbuf", [128, 128], "bfloat16"),
+    "s8": ("sbuf", [128, 8], "bfloat16"), "ns8": ("sbuf", [128, 8], "bfloat16"), "sj": ("sbuf", [128, 8], "bfloat16"),
+    "cj": ("sbuf", [128, 8], "bfloat16"), "anew": ("sbuf", [128, 256], "float32"), "rev": ("sbuf", [128, 256], "bfloat16"),
+    "blk8": ("sbuf", [128, 128], "bfloat16"), "die": ("sbuf", [128, 128], "float32"), "rse": ("sbuf", [128, 128], "float32"),
     "blk": ("sbuf", [128, 128], "float32"), "dia": ("sbuf", [128, 128], "float32"), "rst": ("sbuf", [128, 128], "float32"),
-    "b1": ("sbuf", [128, 256], "bfloat16"), "b2": ("sbuf", [128, 256], "bfloat16"), "kbig": ("sbuf", [128, 64], "bfloat16"),
-    "one": ("sbuf", [128, 128], "bfloat16"), "m160": ("sbuf", [128, 16], "bfloat16"),
+    "b1": ("sbuf", [128, 256], "bfloat16"), "b2": ("sbuf", [128, 256], "bfloat16"),
+    "one": ("sbuf", [128, 128], "bfloat16"), "m160": ("sbuf", [128, 32], "bfloat16"),
     "inb": ("sbuf", [128, 272], "int32"), "sb": ("sbuf", [128, 256], "int32"), "sg": ("sbuf", [128, 256], "float32"),
-    "ya": ("sbuf", [128, 256], "float32"), "yf": ("sbuf", [128, 272], "float32"), "dup": ("sbuf", [128, 544], "float32"),
+    "yf": ("sbuf", [128, 272], "float32"), "dup": ("sbuf", [128, 544], "float32"),
     "trp": ("sbuf", [128, 544], "float32"), "ztb": ("sbuf", [128, 256], "bfloat16"),
     "nxi": ("sbuf", [128, 256], "int32"), "nxj": ("sbuf", [128, 512], "int32"), "nxh": ("sbuf", [128, 512], "bfloat16"),
-    "fin": ("sbuf", [128, 272], "float32"), "oh1": ("sbuf", [128, 256], "float32"), "oh": ("sbuf", [128, 256], "float32"),
-    "oc": ("sbuf", [128, 16], "float32"), "oz": ("sbuf", [128, 256], "bfloat16"),
+    "oh1": ("sbuf", [128, 256], "float32"), "oh": ("sbuf", [128, 256], "float32"), "ph": ("sbuf", [128, 256], "float32"),
+    "keep": ("sbuf", [128, 256], "float32"), "ohs": ("sbuf", [128, 256], "float32"), "nxr": ("sbuf", [128, 256], "bfloat16"),
+    "oc": ("sbuf", [128, 256], "float32"), "oz": ("sbuf", [128, 256], "bfloat16"),
     "key0": ("psum", [128, 512], "float32"), "key1": ("psum", [128, 512], "float32"),
     "pd0": ("psum", [128, 512], "float32"), "pd1": ("psum", [128, 512], "float32"),
     "pq": ("psum", [128, 512], "float32"), "ps": ("psum", [128, 512], "float32"),
     "pa": ("psum", [128, 512], "float32"), "pn": ("psum", [128, 512], "float32"),
 }
-LOADS = ["ld_mem", "ld_plc", "ld_z", "ld_tab", "ld_nx", "nx_hi", "nx_lo", "st_x", "st_h", "st_c", "st_z"]
-SEMAPHORES = (["cV", "cS", "cP", "cG", "sent"] + LOADS
-              + ["%s%d%d" % (k, t, h) for k in ("az", "af", "bz", "bf", "du") for t in range(1, RO + 1) for h in range(2)])
+STORES = ["st_x", "st_h0", "st_h1", "st_z", "st_c"]
+SEMAPHORES = (["cV", "cS", "cP", "cG", "sent", "ld_m", "ld_c", "ld_z", "ld_t", "ld_nx", "nx_b"] + STORES
+              + ["%s%d%d" % (k, t, h) for k in ("az", "ae", "bz", "be", "du") for t in range(1, RO + 1) for h in range(2)])
 
-L1, L2, LZ, LF1, LF2, LR, LJ = 0, 34, 54, 118, 152, 54, 170
-PAR = dict(cyc=1.04e-3, gat=1.56, sca=3.8, pec=0.55e-3, hop=0.10, remote=2.6, local=2.0, route=ROUTE)
+L1, L2, LZ, LF1, LF2, LJ, LG = 0, 18, 38, 46, 62, 70, 74
 
 
 def A(name, lo=0, hi=None, step=1):
@@ -59,12 +67,24 @@ def IND(win, off):
     return ("*", win, off)
 
 
+def deal(n, total):
+    k = [1] * n
+    while True:
+        i = k.index(min(k))
+        if sum(k) + k[i] > total:
+            return k
+        k[i] *= 2
+
+
 def build(T, topo, rank):
     ops = []
-    visit = [None]
-    CYC, GAT, SCA, PEC, REMOTE, LOCAL, ROUTE = [PAR[k] for k in ("cyc", "gat", "sca", "pec", "remote", "local", "route")]
+    CYC, GAT, SCA, PEC, REMOTE, LOCAL = [CFG[k] for k in ("cyc", "gat", "sca", "pec", "remote", "local")]
     N = len(T.cores)
     me = T.cores[rank]
+    BASE = float(SPARE - 16384)
+
+    def routes(t, h):
+        return CFG["first" if t == 0 else "last" if t == RO - 1 else "route"][h]
 
     def ap(a):
         if not isinstance(a, tuple):
@@ -94,8 +114,7 @@ def build(T, topo, rank):
                 w.append(a[1]); r.append(a[2])
             else:
                 w.append(a)
-        t = visit[0]
-        ops.append(dict(t=t or 0, cls=name if t is None else name[:2] + name[3:], q=q, name=name, fn=fn, rd=r, wr=w, cost=cost, lat=lat, sem=sem, val=val, after=after))
+        ops.append(dict(q=q, name=name, fn=fn, rd=r, wr=w, cost=cost, lat=lat, sem=sem, val=val, after=after))
 
     def vcost(out, ins, both=False):
         if out[0] == "*":
@@ -119,62 +138,93 @@ def build(T, topo, rank):
     def cp(name, out, a):
         add("V", name, lambda g: [g.vector.tensor_copy(ap(out), ap(a))], [a], [out], vcost(out, [a]))
 
-    def scan(name, out, a, b):
-        add("V", name, lambda g: [g.vector.tensor_tensor_scan(ap(out), ap(a), ap(b), 0.0, ALU.mult, ALU.add)], [a, b], [out], vcost(out, [a]))
+    def scan(name, items, op0=ALU.mult, op1=ALU.add):
+        add("V", name, lambda g: [g.vector.tensor_tensor_scan(ap(o), ap(a), ap(b), 0.0, op0, op1) for o, a, b in items],
+            [x for i in items for x in i[1:]], [i[0] for i in items], sum(vcost(o, [a, b]) for o, a, b in items))
+
+    def turn(name, out, a):
+        add("V", name, lambda g: [g.vector.transpose(ap(out), ap(a))], [a], [out], vcost(out, [a]))
 
     def fill(name, out, v):
         add("V", name, lambda g: [g.vector.memset(ap(out), v)], [], [out], vcost(out, [out]))
 
     def act(name, out, a, func, bias=0.0, scale=1.0, acc=None):
         c = 0.065 + width(out) * GAT * CYC if a[0] == "*" else max(64, width(out)) * CYC + 0.03
+        kw = {}
+        if bias != 0.0:
+            kw["bias"] = ap(bias)
+        if scale != 1.0:
+            kw["scale"] = ap(scale)
         if acc is not None:
-            fn = lambda g: [g.scalar.activation(ap(out), ap(a), func, accum_out=ap(acc))]
-        elif bias == 0.0 and scale == 1.0:
-            fn = lambda g: [g.scalar.activation(ap(out), ap(a), func)]
-        else:
-            fn = lambda g: [g.scalar.activation(ap(out), ap(a), func, bias=bias, scale=scale)]
-        add("S", name, fn, [a], [out] + ([acc] if acc else []), c)
+            kw["accum_out"] = ap(acc)
+        add("S", name, lambda g: [g.scalar.activation(ap(out), ap(a), func, **kw)], [a, bias, scale], [out] + ([acc] if acc else []), c)
 
-    def mm(name, items):
+    def mm(name, items, grp=None):
         c = sum(max(64, width(i[2])) * (1 if two(i[2]) else 4) for i in items) * PEC
-        add("P", name, lambda g: [g.tensor.matmul(ap(o), ap(l), ap(r), s, e) for o, l, r, s, e in items],
+        add("P", name, lambda g, close=False: [g.tensor.matmul(ap(o), ap(l), ap(r), s, e or (close and k == len(items) - 1))
+                                               for k, (o, l, r, s, e) in enumerate(items)],
             [x for i in items for x in i[1:3]], [i[0] for i in items], c, lat=0.1)
+        ops[-1]["grp"] = grp
 
-    def iota(name, out, pat, base, ch=0):
+    def iota(name, out, pat, base, ch=0, after=None):
         if SCRATCH[out[0]][2] == "int32":
             fn = lambda g: [g.iota(ap(out), pat, base, ch)]
         else:
             fn = lambda g: [g.iota(ap(out), pat, base, ch, allow_small_or_imprecise_dtypes=True)]
-        add("G", name, fn, [], [out], 0.13 + 2 * width(out) * CYC)
+        add("G", name, fn, [], [out], 0.15 + 2 * width(out) * CYC, after=after)
 
-    def dma(q, name, out, a, rd, wr, lat, sem=None, val=16):
+    def dma(q, name, pairs, rd, wr, lat, after=None):
         eng = (lambda g: g.sync) if q == "Y" else (lambda g: g.scalar)
-        add(q, name, lambda g: [eng(g).dma_start(out, a)], rd, wr, 0.06, lat=lat, sem=sem or name, val=val)
+        add(q, name, lambda g: [eng(g).dma_start(o, a) for o, a in pairs], rd, wr, 0.06 * len(pairs), lat=lat, sem=name, val=16 * len(pairs), after=after)
 
     def sel16(name, out, src):
         mm(name, [(out, A("wd", 15 - p, 143 - p), A(src[0], src[1] + p, src[2], 16), p == 0, p == 15) for p in range(16)])
 
-    def send(name, src, dsts):
+    def mail(r, kind, t, h):
+        s, s1, n1 = 2 * t + h, 2 * t + h + 2, "%d%d" % (t + 1, h)
+        nxt, other = (r + 1) % N, ((r ^ 1) + 1) % N
+        zo = A("zout", 128 * s, 128 * s + 128)
+        out = []
+        if t + 1 == RO:
+            if kind == "late":
+                out.append((zo, r ^ 1, A("pz", 128 * s1, 128 * s1 + 128), "bz" + n1))
+            else:
+                out.append((A("oh", 128 - 128 * h, 256 - 128 * h), r ^ 1, A("ph", 128 - 128 * h, 256 - 128 * h), "be" + n1))
+        elif kind == "late":
+            out.append((A("msg", SLOT * s, SLOT * s + 64), nxt, A("msg", SLOT * s1 + 8, SLOT * s1 + 72), "az" + n1))
+            out.append((zo, nxt, A("zin", 128 * s1, 128 * s1 + 128), "az" + n1))
+            if other != r:
+                out.append((zo, other, A("pz", 128 * s1, 128 * s1 + 128), "bz" + n1))
+        else:
+            src = A("msg", SLOT * s + 64, SLOT * s + 136)
+            out.append((src, nxt, A("msg", SLOT * s1 + 72, SLOT * s1 + SLOT), "ae" + n1))
+            if other != r:
+                out.append((src, other, A("pmsg", 72 * s1, 72 * s1 + 72), "be" + n1))
+        k = deal(len(out), len(topo.engines(T.cores[r], T.cores[out[0][1]])))
+        return [o + (e,) for o, e in zip(out, k)]
+
+    def send(kind, t, h):
+        trs = mail(rank, kind, t, h)
+
         def fn(g):
-            trs = []
-            for i, (r, land, sem) in enumerate(dsts):
-                es = topo.engines(me, T.cores[r])
-                k = len(es) // len(dsts)
+            out, e0 = [], 0
+            for src, r, land, sem, k in trs:
                 rid, pid, _ = topo.addr(T.cores[r])
-                trs.append((rid, pid, sum(1 << e for e in es[i * k:(i + 1) * k]), land, sem))
-            if len(trs) == 1:
-                rid, pid, m, land, sem = trs[0]
+                m = sum(1 << e for e in topo.engines(me, T.cores[r])[e0:e0 + k])
+                e0 += k
+                out.append((rid, pid, m, src, land, sem))
+            if len(out) == 1:
+                rid, pid, m, src, land, sem = out[0]
                 g.remote_dma(ap(land), ap(src), T.sem[sem], T.sem.sent, pid, rid, m)
             else:
                 g.remote_dma_fused([RemoteDMATransfer(dst_ids=[DstId(rid=rid, pnc=pid)], dma_engine_mask=m, remote_sem=T.sem[sem],
-                                                      src=ap(src), dst=ap(land)) for rid, pid, m, land, sem in trs], local_sem=T.sem.sent)
+                                                      src=ap(src), dst=ap(land)) for rid, pid, m, src, land, sem in out], local_sem=T.sem.sent)
             return []
-        k = len(topo.engines(me, T.cores[dsts[0][0]])) // len(dsts)
-        add("G", name, fn, [src], [], 0.5, sem="sent", val=k * len(dsts))
+        add("G", "%s%d%d" % (kind, t, h), fn, [x[0] for x in trs], [], CFG["call"], sem="sent", val=sum(x[4] for x in trs))
 
-    def recv(name, land, src_rank, nwrites, after):
-        k = len(topo.engines(T.cores[src_rank], me)) // nwrites
-        add(None, name, None, [], [land], 0.0, lat=REMOTE, sem=name, val=k, after=after)
+    def recv(kind, t, h, src_rank, sem):
+        mine = [x for x in mail(src_rank, kind, t - 1, h) if x[1] == rank and x[3] == sem]
+        add(None, sem, None, [], [x[2] for x in mine], 0.0, lat=REMOTE, sem=sem, val=sum(x[4] for x in mine), after="%s%d%d" % (kind, t - 1, h))
 
     def lst(lo, n):
         return A("lst", lo, lo + n)
@@ -182,246 +232,302 @@ def build(T, topo, rank):
     def pc(i):
         return A("pc", i, i + 1)
 
-    dma("Y", "ld_mem", T.inb[:, 0:256], T.mem[:], [], [A("inb", 0, 256)], LOCAL)
-    dma("Y", "ld_plc", T.inb[:, 256:272], T.plc[:], [], [A("inb", 256, 272)], LOCAL)
-    dma("S", "ld_z", T.ztb[:], T.zt[:], [], [A("ztb")], LOCAL)
-    dma("S", "ld_tab", T.tab[:, 16:4112], T.xt[:], [], [A("tab", 16, 4112)], LOCAL + 4.0)
-    dma("Y", "ld_nx", T.nxi[:], T.nxt[:], [], [A("nxi")], LOCAL + 4.5)
+    dma("Y", "ld_m", [(T.inb[:, 0:256], T.mem[:])], [], [A("inb", 0, 256)], LOCAL)
+    dma("S", "ld_c", [(T.inb[:, 256:272], T.plc[:])], [], [A("inb", 256, 272)], LOCAL)
+    dma("S", "ld_z", [(T.ztb[:], T.zt[:])], [], [A("ztb")], LOCAL)
+    dma("Y", "ld_t", [(T.tab[:, SPARE:], T.xt[:])], [], [A("tab", SPARE)], LOCAL + CFG["table"], after="ld_m")
+    dma("Y", "ld_nx", [(T.nxi[:], T.nxt[:])], [], [A("nxi")], LOCAL + CFG["table"] + 0.4, after="ld_t")
 
     iota("i_p", A("pi"), [[0, 1]], 0, 1)
-    iota("i_l1", A("lio", L1, L1 + 32), [[-16, 16], [0, 2]], 255)
-    iota("i_l1c", A("lio", L1 + 32, L1 + 34), [[0, 2]], 271)
-    iota("i_lz", A("lio", LZ, LZ + 64), [[-128, 2], [0, 4], [-16, 8]], 255)
-    iota("i_l2", A("lio", L2, L2 + 20), [[256, 2], [2, 10]], -2)
+    iota("i_l1c", A("lio", L1, L1 + 2), [[0, 2]], 143)
+    iota("i_l1", A("lio", L1 + 2, L1 + 18), [[-16, 8], [0, 2]], 127)
+    iota("i_l2", A("lio", L2, L2 + 20), [[256, 2], [2, 10]], 30)
     iota("i_ci", A("ci"), [[1, 144]], 0)
-    iota("i_b2", A("b2"), [[1, 256]], 0)
-    for b in range(2):
-        iota("i_b1%d" % b, A("b1", 128 * b, 128 * b + 128), [[256, 2], [2048, 8], [0, 8]], 16384 * b)
+    iota("i_b2", A("b2"), [[0, 8], [1, 32]], 0)
+    iota("i_b1", A("b1"), [[0, 16], [128, 16]], 0)
     iota("i_c16", A("c16"), [[0, 8], [1, 16]], 0)
     iota("i_cg", A("cg"), [[16, 8], [0, 16]], 0)
-    iota("i_lf1", A("lio", LF1, LF1 + 32), [[136, 2], [1, 8], [0, 2]], 8)
-    iota("i_lf2", A("lio", LF2, LF2 + 16), [[-32, 16]], 495)
-    iota("i_lf2c", A("lio", LF2 + 16, LF2 + 18), [[0, 2]], 527)
-    iota("i_nx0", A("nxb"), [[0, 4112]], 0)
-    ts("p0", A("pb", 0, 1), A("pi"), 7, ALU.bitwise_and)
-    ts("p1", A("pb", 1, 2), A("pi"), 3, ALU.logical_shift_right, 1, ALU.bitwise_and)
-    ts("p2", A("pb", 2, 3), A("pi"), 16, ALU.bitwise_and)
-    ts("p3", A("pb", 3, 4), A("pi"), 15, ALU.bitwise_and)
-    ts("p4", A("pb", 4, 5), A("pi"), 112, ALU.bitwise_and)
-    ts("p5", A("pb", 5, 6), A("pi"), 127, ALU.bitwise_and)
+    iota("i_c32", A("c32"), [[0, 4], [1, 32]], 0)
+    for i in range(4):
+        iota("i_nx%d" % i, A("nxb", 1032 * i, 1032 * i + 1032), [[0, 1032]], 0, after="i_cg")
+    iota("i_rev", A("rev"), [[0, 8], [32, 2], [0, 16]], 0)
+    iota("i_lf1", A("lio", LF1, LF1 + 16), [[1, 8], [0, 2]], 0)
+    iota("i_lf2", A("lio", LF2, LF2 + 8), [[-32, 8]], 239)
+    iota("i_cg8", A("cg8"), [[16, 8], [-1000, 2], [0, 8]], 1000)
+    for i, m in enumerate((7, 8, 16, 15, 112, 127)):
+        ts("p%d" % i, A("pb", i, i + 1), A("pi"), m, ALU.bitwise_and)
     cp("pc", A("pc", 0, 6), A("pb", 0, 6))
-    ts("l1", lst(L1, 34), A("lio", L1, L1 + 34), pc(3), ALU.subtract)
-    ts("lz", lst(LZ, 64), A("lio", LZ, LZ + 64), pc(3), ALU.subtract)
+    ts("l1", lst(L1, 18), A("lio", L1, L1 + 18), pc(3), ALU.subtract)
+    ts("lz", lst(LZ, 8), A("lio", L1 + 2, L1 + 18, 2), pc(3), ALU.subtract)
     ts("p6", pc(6), pc(0), 32.0, ALU.mult, pc(2), ALU.add)
-    ts("l2", lst(L2, 20), A("lio", L2, L2 + 20), pc(6), ALU.add, pc(1), ALU.add)
-    ts("p7", pc(7), pc(2), pc(0), ALU.subtract)
+    ts("p7", pc(7), pc(1), 0.125, ALU.mult, pc(6), ALU.add)
     for h in range(2):
-        ts("l2c%d" % h, lst(L2 + 10 * h, 1), pc(7), 527.0 - 8 * h, ALU.add)
-    ts("lj", lst(LJ, 8), A("ci", 0, 8), 0.0, ALU.mult, pc(0), ALU.add)
+        ts("l2%d" % h, lst(L2 + 10 * h + 1, 9), A("lio", L2 + 10 * h + 1, L2 + 10 * h + 10), pc(7), ALU.add)
+        ts("lc%d" % h, lst(L2 + 10 * h, 1), pc(2), pc(0), ALU.subtract, 15.0 - 8 * h, ALU.add)
+    ts("lj", lst(LJ, 4), A("lio", L1 + 2, L1 + 6), 0.0, ALU.mult, pc(0), ALU.add)
+    cp("lg", lst(LG, 8), A("ci", 0, 8))
+    cp("cj", A("cj"), A("ci", 0, 8))
     ts("idn", A("idn"), A("ci", 0, 128), pc(5), ALU.is_equal)
-    ts("nid", A("nid"), A("idn"), -1.0, ALU.mult)
+    act("nid", A("nid"), A("idn"), AF.Identity, scale=-1.0)
     ts("p8", pc(8), pc(4), 15.0, ALU.add)
-    ts("wd", A("wd"), A("ci"), pc(8), ALU.is_equal, 512.0, ALU.mult)
-    ts("nwd", A("nwd"), A("wd"), -1.0, ALU.mult)
+    ts("wd", A("wd"), A("ci"), pc(8), ALU.is_equal, 256.0, ALU.mult)
+    for name, v in (("s8", 32.0), ("ns8", -32.0), ("sj", 8.0)):
+        ts(name, A(name), A("ci", 0, 128, 16), pc(4), ALU.is_equal, v, ALU.mult)
+    ts("anew", A("anew"), A("b2"), 0.0, ALU.is_equal, 1.0e6, ALU.mult)
     ts("blk", A("blk"), A("cg"), pc(4), ALU.is_equal)
+    act("bn", A("bn"), A("blk"), AF.Copy)
+    ts("blk8", A("blk8"), A("cg8"), pc(4), ALU.is_equal)
     ts("dia", A("dia"), A("c16"), pc(3), ALU.is_equal)
-    ts("rst", A("rst"), A("c16"), pc(3), ALU.not_equal)
-    fill("spare", A("tab", 0, 16), 0.0)
-    fill("kbig", A("kbig"), 512.0)
+    act("rst", A("rst"), A("dia"), AF.Identity, scale=-1.0, bias=1.0)
+    if "2" in CFG["wide"]:
+        ts("die", A("die"), A("c32"), pc(3), ALU.is_equal)
+        act("rse", A("rse"), A("die"), AF.Identity, scale=-1.0, bias=1.0)
+        ts("p10", pc(10), pc(3), 16.0, ALU.add)
+    if set(CFG["xs"] + CFG["cs"]) != {"V"}:
+        act("idf", A("idf"), A("idn"), AF.Copy)
+    if set(CFG["xs"]) != {"V"}:
+        act("nif", A("nif"), A("nid"), AF.Copy)
+    fill("spare", A("tab", 0, SPARE), 0.0)
     fill("one", A("one"), 1.0)
     fill("m160", A("m160"), -160.0)
     ts("p9", pc(9), pc(3), 8.0, ALU.mult)
-    ts("lf1", lst(LF1, 32), A("lio", LF1, LF1 + 32), pc(9), ALU.add)
-    ts("p10", pc(10), pc(1), -128.0, ALU.mult, pc(3), ALU.subtract)
-    ts("p11", pc(11), pc(10), 143.0, ALU.add)
-    ts("lf1d", lst(LF1 + 32, 2), A("ci", 0, 2), 0.0, ALU.mult, pc(11), ALU.add)
-    ts("p12", pc(12), pc(2), pc(3), ALU.subtract)
-    ts("lf2", lst(LF2, 18), A("lio", LF2, LF2 + 18), pc(12), ALU.add)
+    ts("lf1", lst(LF1, 16), A("lio", LF1, LF1 + 16), pc(9), ALU.add)
+    ts("lf2", lst(LF2, 8), A("lio", LF2, LF2 + 8), pc(2), ALU.add, pc(3), ALU.subtract)
 
-    ts("y_s", A("sb"), A("inb", 0, 256), 1, ALU.bitwise_and)
-    ts("y_g", A("sg"), A("sb"), 24577.0, ALU.mult)
-    tt("y_m", A("yf", 0, 256), A("sg"), A("inb", 0, 256), ALU.subtract)
-    ts("y_c", A("yf", 256, 272), A("inb", 256, 272), 28672.0, ALU.add, 2.0, ALU.mult)
-    act("y_d", A("dup"), IND(A("yf"), lst(L1, 34)), AF.Abs, scale=0.5)
-    add("V", "y_t", lambda g: [g.vector.transpose(ap(A("trp")), ap(A("dup")))], [A("dup")], [A("trp")], 544 * CYC)
+    ts("y_c", A("yf", 128, 144), A("inb", 256, 272), 28672.0, ALU.add, 2.0, ALU.mult)
     for h in range(2):
-        act("y_l%d" % h, A("msg", SLOT * h, SLOT * h + SLOT), IND(A("trp"), lst(L2 + 10 * h, 9)), AF.Identity, bias=-6144.0)
-        act("z_l%d" % h, A("zin", 512 * h, 512 * h + 512), IND(A("ztb"), lst(LZ + 32 * h, 32)), AF.Copy)
+        lanes = lambda b: A(b, 128 - 128 * h, 256 - 128 * h)
+        d0, d1 = (0, 288) if h == 0 else (288, 544)
+        ts("y_s%d" % h, lanes("sb"), lanes("inb"), 1, ALU.bitwise_and)
+        ts("y_g%d" % h, lanes("sg"), lanes("sb"), 24577.0, ALU.mult)
+        tt("y_m%d" % h, A("yf", 144 * h, 144 * h + 128), lanes("sg"), lanes("inb"), ALU.subtract)
+        act("y_d%d" % h, A("dup", d0, d1), IND(A("yf", 144 * h, 144 + 128 * h), lst(L1 + 2 * h, 18 - 2 * h)), AF.Abs, scale=0.5)
+        turn("y_t%d" % h, A("trp", d0, d1), A("dup", d0, d1))
+        act("y_l%d" % h, A("msg", SLOT * h, SLOT * h + SLOT), IND(A("trp", 0, d1), lst(L2 + 10 * h, 9)), AF.Identity, bias=-6144.0)
+        act("z_l%d" % h, A("zin", 128 * h, 128 * h + 128), IND(lanes("ztb"), lst(LZ, 8)), AF.Copy)
     ts("nx1", A("nxj", 0, 256), A("nxi"), 4032, ALU.bitwise_and)
     ts("nx2", A("nxj", 256, 512), A("nxi"), 63, ALU.bitwise_and)
     cp("nx3", A("nxh"), A("nxj"))
-    dma("Y", "nx_hi", T.nxb[0:128:16, 16:4112], T.nxh[:, 0:256], [A("nxh")], [A("nxb", 0, 2056)], LOCAL + 0.5)
-    dma("Y", "nx_lo", T.nxb[1:128:16, 16:4112], T.nxh[:, 256:512], [A("nxh")], [A("nxb", 2056, 4112)], LOCAL + 0.5)
+    dma("Y", "nx_b", [(T.nxb[i:128:16, SPARE:], T.nxh[:, 256 * i:256 * i + 256]) for i in range(2)], [A("nxh")], [A("nxb")], LOCAL + 0.5)
 
     prev, part = (rank - 1) % N, rank ^ 1
 
-    def exchange(t, h, zown, own, out):
-        n = "%d%d" % (t, h)
-        src = part if t == RO else prev ^ 1
-        if src == rank:
-            zp, yp = A("zout", 128 * (2 * t - 2 + h), 128 * (2 * t - 1 + h)), A("msg", SLOT * (2 * t - 2 + h) + 72, SLOT * (2 * t - 2 + h) + 136)
-        else:
-            s = 2 * t + h
-            zp, yp = A("pz", 128 * s, 128 * s + 128), A("pmsg", SLOT * s + 72, SLOT * s + 136)
-            w = 1 if t == RO else 2
-            recv("bz" + n, zp, src, w, "sz%d%d" % (t - 1, h))
-            recv("bf" + n, A("pmsg", SLOT * s, SLOT * s + 136), src, w, "sf%d%d" % (t - 1, h))
-        H = lambda b, k=128: A(b, k * h, k * h + k)
+    def alike(n, h, zown, zp, back=None):
         mm("ad" + n, [(A("pa", 0, 128), A("idn"), zown, True, False), (A("pa", 0, 128), A("nid"), zp, False, True)])
-        act("a1" + n, H("al1"), A("pa", 0, 128), AF.Abs)
-        act("a2" + n, H("al2"), H("al1"), AF.Sign, bias=10.5, scale=-1.0)
-        sel16("as" + n, A("pa", 128, 136), H("al2"))
-        ts("ak" + n, H("alk", 8), A("pa", 128, 136), 512.0, ALU.is_ge)
-        tt("df" + n, H("dif", 64), yp, own, ALU.subtract)
-        tt("dm" + n, H("tmp", 64), IND(H("alk", 8), lst(LJ, 4)), H("dif", 64), ALU.mult)
-        tt("sw" + n, out, own, H("tmp", 64), ALU.add)
+        a1, a2 = A("al1", 128 * h, 128 * h + 128), A("al2", 128 * h, 128 * h + 128)
+        act("a1" + n, a1, A("pa", 0, 128), AF.Abs)
+        act("a2" + n, a2, IND(a1, back) if back else a1, AF.Sign, bias=10.5, scale=-1.0)
+        return a2
+
+    def exchange(t, h):
+        n, s, src = "%d%d" % (t, h), 2 * t + h, prev ^ 1
+        own = A("msg", SLOT * s + 80, SLOT * s + SLOT)
+        if src == rank:
+            zp, yp = A("zout", 128 * (s - 2), 128 * (s - 1)), A("msg", SLOT * (s - 2) + 72, SLOT * (s - 2) + 136)
+        else:
+            zp, yp = A("pz", 128 * s, 128 * s + 128), A("pmsg", 72 * s + 8, 72 * s + 72)
+            recv("late", t, h, src, "bz" + n)
+            recv("early", t, h, src, "be" + n)
+        H = lambda b, k=128: A(b, k * h, k * h + k)
+        sel16("as" + n, A("pa", 128, 136), alike(n, h, A("zin", 128 * s, 128 * s + 128), zp))
+        if CFG["xs"][h] == "V":
+            ts("ak" + n, H("alk", 8), A("pa", 128, 136), 256.0, ALU.is_ge)
+            tt("df" + n, H("dif", 64), yp, own, ALU.subtract)
+            tt("dm" + n, H("tmp", 64), IND(H("alk", 8), lst(LJ, 4)), H("dif", 64), ALU.mult)
+            tt("sw" + n, own, own, H("tmp", 64), ALU.add)
+        else:
+            act("ak" + n, H("alk", 8), A("pa", 128, 136), AF.Sign, bias=-128.0)
+            act("ar" + n, H("dif", 64), IND(H("alk", 8), lst(LJ, 4)), AF.Relu)
+            mm("df" + n, [(A("ps", 64, 128), A("idf"), yp, True, False), (A("ps", 64, 128), A("nif"), own, False, True)])
+            tt("dm" + n, A("ps", 128, 192), A("ps", 64, 128), H("dif", 64), ALU.mult)
+            tt("sw" + n, own, A("ps", 128, 192), own, ALU.add)
+
+    def from_table(t, h):
+        return "C" in routes(t, h)
 
     def prep(t, h):
         n, s = "%d%d" % (t, h), 2 * t + h
         m0, z0 = SLOT * s, 512 * s
+        z1 = A("zin", 128 * s, 128 * s + 128)
         if t > 0:
-            w = 1 if ((prev ^ 1) + 1) % N == prev else 2
-            recv("az" + n, A("zin", z0, z0 + 128), prev, w, "sz%d%d" % (t - 1, h))
-            recv("af" + n, A("msg", m0 + 8, m0 + SLOT), prev, w, "sf%d%d" % (t - 1, h))
-            add("Y", "du" + n, lambda g: [g.sync.dma_start(T.zin[:, z0 + 128 * r:z0 + 128 * r + 128], T.zin[:, z0:z0 + 128]) for r in (1, 2, 3)],
-                [A("zin", z0, z0 + 128)], [A("zin", z0 + 128, z0 + 512)], 0.2, lat=LOCAL, sem="du" + n, val=48)
+            recv("late", t, h, prev, "az" + n)
+            recv("early", t, h, prev, "ae" + n)
+        for name, use, out, scale, bias in (("nz", set(routes(t, h)) & set("AB"), A("nz", z0, z0 + 128), -1.0, 0.0),
+                                            ("zb", "D" in routes(t, h) or not from_table(t, h), A("zb", 128 * s, 128 * s + 128), 1.0, 192.0)):
+            if use and CFG["zq"] == "V":
+                ts(name + n, out, z1, scale, ALU.mult, bias, ALU.add)
+            elif use:
+                act(name + n, out, z1, AF.Identity, scale=scale, bias=bias)
+        if set(routes(t, h)) & set("AB"):
+            if t and CFG["dup"][h] == "L":
+                dma("Y", "du" + n, [(T.nz[:, z0 + 128 * r:z0 + 128 * r + 128], T.nz[:, z0:z0 + 128]) for r in (1, 2, 3)],
+                    [A("nz", z0, z0 + 128)], [A("nz", z0 + 128, z0 + 512)], LOCAL + 0.4)
+            else:
+                for i in range(2):
+                    cp("d%d%s" % (i + 1, n), A("nz", z0 + (128 << i), z0 + (256 << i)), A("nz", z0, z0 + (128 << i)))
         c = IND(A("msg", m0 + 8, m0 + 16), lst(LJ, 4))
+        if t and CFG["cs"][h] != "V":
+            act("cr" + n, A("crp", 64 * h, 64 * h + 64), c, AF.Copy)
+            mm("cp" + n, [(A("ps", 0, 64), A("idf"), A("crp", 64 * h, 64 * h + 64), True, True)])
+            c = A("ps", 0, 64)
         for b in range(2):
             if b and t > 0:
-                exchange(t, h, A("zin", z0, z0 + 128), A("msg", m0 + 80, m0 + SLOT), A("msg", m0 + 80, m0 + SLOT))
-            y, o, nb = A("msg", m0 + 16 + 64 * b, m0 + 80 + 64 * b), 256 * h + 128 * b, n + str(b)
-            tt("ta" + nb, A("t32", o, o + 64), c, y, ALU.add)
-            tt("tb" + nb, A("t32", o + 64, o + 128), c, y, ALU.subtract)
-            ts("to" + nb, A("o32", o, o + 128), A("t32", o, o + 128), 16384 | 4095, ALU.bitwise_and)
-            ts("tu" + nb, A("o16", o, o + 128), A("o32", o, o + 128), -16368.0, ALU.add)
+                exchange(t, h)
+            if b and t + 1 < RO:
+                send("early", t, h)
+            y = A("msg", m0 + 16 + 64 * b, m0 + 80 + 64 * b)
+            for kind in range(2):
+                o, nb = 256 * h + 128 * kind + 64 * b, "%s%d%d" % (n, b, kind)
+                tt("ta" + nb, A("t32", o, o + 64), c, y, ALU.subtract if kind else ALU.add)
+                ts("to" + nb, A("o32", o, o + 64), A("t32", o, o + 64), 16384 | 4095, ALU.bitwise_and)
+                ts("tu" + nb, A("o16", o, o + 64), A("o32", o, o + 64), BASE, ALU.add)
 
     nr2 = [0]
 
     def main(t, h):
         n, s = "%d%d" % (t, h), 2 * t + h
-        z4 = A("zin", 512 * s, 512 * s + 512)
+        z1, z4, zb = A("zin", 128 * s, 128 * s + 128), A("nz", 512 * s, 512 * s + 512), A("zb", 128 * s, 128 * s + 128)
         key = "key%d" % h
-        mm("kb" + n, [(A(key, 0, 256), A("idn"), A("b1"), True, False), (A(key, 0, 256), A("idn"), A("b2"), False, False)])
-        neg = []
-        for u in range(8):
-            o = 4096 * h + 512 * u
-            gath = IND(A("tab"), A("o16", 256 * h + 32 * u, 256 * h + 32 * u + 32))
-            gu, au = A("gb", o, o + 512), A("ab", o, o + 512)
-            if ROUTE[h][u] != "S":
-                tt("mg%s%d" % (n, u), gu, gath, z4, ALU.subtract)
-                if ROUTE[h][u] == "V":
-                    act("ma%s%d" % (n, u), au, gu, AF.Abs)
+        mm("kb" + n, [(A(key, 0, 256), A("idn"), A("b2"), True, False), (A(key, 0, 256), A("idn"), A("b1"), False, False)])
+        for w in range(4):
+            base = 128 * (w % 2) + 64 * (w // 2)
+            r2 = routes(t, h)[2 * w:2 * w + 2]
+            G = lambda b, u, k=1: A(b, 4096 * h + 16 * base + 512 * u, 4096 * h + 16 * base + 512 * (u + k))
+            gath = lambda u, k=1: IND(A("tab"), A("o16", 256 * h + base + 32 * u, 256 * h + base + 32 * (u + k)))
+            both = CFG["merge"] and r2 in ("CC", "DD")
+            for u in range(2):
+                nu, r = "%s%d" % (n, 2 * w + u), r2[u]
+                k = 2 if both else 1
+                if r in "AB":
+                    tt("mg" + nu, G("gb", u), gath(u), z4, ALU.add)
+                elif r == "C" and not (both and u):
+                    act("mg" + nu, G("gb", u, k), gath(u, k), AF.Copy)
+                elif not (both and u):
+                    act("mg" + nu, G("ab", u, k), gath(u, k), AF.Identity, bias=192.0)
+                if r == "D":
+                    g0, a0 = G("gb", u)[1], G("ab", u)[1]
+                    scan("md" + nu, [(A("gb", g0 + 128 * i, g0 + 128 * i + 128), A("ab", a0 + 128 * i, a0 + 128 * i + 128), zb) for i in range(4)],
+                         ALU.max, ALU.subtract)
+                if r in "AD":
+                    ts("ma" + nu, G("ab", u), G("gb", u), 0.0, ALU.max, 2.0, ALU.mult)
+                elif r == "B":
+                    act("ma" + nu, G("ab", u), G("gb", u), AF.Abs)
                 else:
-                    ts("ma%s%d" % (n, u), au, gu, 0.0, ALU.max, 2.0, ALU.mult)
-                    if u % 2 == 0 or ROUTE[h][u - 1] != "W":
-                        wide = 2 if u % 2 == 0 and ROUTE[h][u + 1] == "W" else 1
-                        neg.append((u, wide))
-            else:
-                pd = A("pd%d" % (nr2[0] % 2)); nr2[0] += 1
-                act("mg%s%d" % (n, u), gu, gath, AF.Copy)
-                mm("md%s%d" % (n, u), [(pd, A("idn"), gu, True, False), (pd, A("nid"), z4, False, True)])
-                act("ma%s%d" % (n, u), au, pd, AF.Abs)
-            if u % 2:
-                w = u // 2
-                for u0, wide in neg:
-                    o0 = 4096 * h + 512 * u0
-                    mm("mw%s%d" % (n, u0), [(A(key, 32 * u0, 32 * (u0 + wide)), A("nwd", 15 - p, 143 - p),
-                                             A("gb", o0 + p, o0 + 512 * wide, 16), False, False) for p in range(16)])
-                neg.clear()
-                if w == 3 and t > 0:
-                    mm("kp" + n, [(A(key, o1, o1 + 64), A("pend"), A("kbig"), False, False) for o1 in (64, 192)])
-                mm("ms%s%d" % (n, w), [(A(key, 64 * w, 64 * w + 64), A("wd", 15 - p, 143 - p),
-                                        A("ab", o - 512 + p, o + 512, 16), False, w == 3 and p == 15) for p in range(16)])
+                    pd = "pd%d" % (nr2[0] % 2); nr2[0] += 1
+                    mm("md" + nu, [(A(pd), A("idn"), G("gb", u), True, False)]
+                       + [(A(pd, 128 * i, 128 * i + 128), A("nid"), z1, False, i == 3) for i in range(4)])
+                    act("ma" + nu, G("ab", u), A(pd), AF.Abs)
+                for name, b, sel in (("mw", "gb", "ns8"), ("ms", "ab", "s8")):
+                    if name == "ms" or r in "AD":
+                        c0, o = base // 8 + 4 * u, G(b, u)[1]
+                        mm(name + nu, [(A(key, c0 + i, 256, 32), A(b, o + 128 * i, o + 128 * i + 128), A(sel), False, False) for i in range(4)], key + n)
+        if t:
+            mm("kp" + n, [(A(key, 0, 256), A("pend"), A("rev"), False, False)], key + n)
 
     def tail(t, h):
         n, s = "%d%d" % (t, h), 2 * t + h
         m0 = SLOT * s
         H = lambda b, k=128: A(b, k * h, k * h + k)
-        last = lambda b: A(b, 128 * h + 15, 128 * h + 128, 16)
+        last = lambda b, k=16: A(b, 128 * h + k - 1, 128 * h + 128, k)
         key = "key%d" % h
-        add("V", "mn" + n, lambda g: [g.vector.tensor_reduce(ap(A("kf", 8 * h + j, 8 * h + j + 1)), ap(A(key, j, 256, 8)), AX.X, ALU.min) for j in range(8)],
-            [A(key)], [H("kf", 8)], 8 * 64 * CYC)
-        cp("ki" + n, H("ki", 8), H("kf", 8))
-        ts("pt" + n, H("pt32", 8), H("ki", 8), 255, ALU.bitwise_and)
-        cp("pu" + n, H("pt16", 8), H("pt32", 8))
+        scan("mn" + n, [(H("kf", 256), A("anew"), A(key, 0, 256))], ALU.add, ALU.min)
+        cp("ki" + n, H("ki", 8), A("kf", 256 * h + 31, 256 * h + 256, 32))
+        ts("pt" + n, H("pt32", 8), H("ki", 8), 31, ALU.bitwise_and)
+        pos = A(key, 384, 392)
+        tt("bx" + n, H("bx"), IND(H("pt32", 8), lst(LG, 8)), A("dia"), ALU.mult)
+        mm("tr" + n, [(pos, H("bx"), A("sj"), True, False), (pos, A("idn"), A("cj"), False, True)])
+        cp("pu" + n, H("pt16", 8), pos)
+        if not from_table(t, h):
+            ts("pv" + n, H("pd16", 8), pos, 16.0, ALU.mult, pc(3), ALU.add)
         tt("xx" + n, H("xx"), IND(H("o32", 256), H("pt16", 8)), A("dia"), ALU.mult)
-        scan("ff" + n, H("ff"), A("rst"), H("xx"))
-        mm("qr" + n, [(A("pq", 0, 128), A("blk"), H("xx"), True, True)])
-        tt("ne" + n, H("ne"), A("pq", 0, 128), H("ff"), ALU.not_equal)
-        scan("rr" + n, H("rr"), H("ne"), H("xx"))
-        ts("of" + n, A("off16", 16 * h, 16 * h + 16, 2), last("rr"), -16368.0, ALU.add, pc(3), ALU.max)
+        scan("ff" + n, [(H("ff"), A("rst"), H("xx"))])
+        ts("qq" + n, H("q16", 8), last("ff"), BASE, ALU.add)
+        qr = A(key, 256, 384)
+        mm("qr" + n, [(qr, A("blk"), H("xx"), True, True)])
+        tt("ne" + n, H("ne"), qr, H("ff"), ALU.not_equal)
+        scan("rr" + n, [(H("rr"), H("ne"), H("xx"))])
+        wide = int(CFG["wide"][h])
+        if wide == 1:
+            ts("of" + n, A("off16", 16 * h, 16 * h + 16, 2), last("rr"), BASE, ALU.add, pc(3), ALU.max)
+        else:
+            tt("xe" + n, H("xe"), IND(H("o32", 256), H("pt16", 8)), A("die"), ALU.mult)
+            scan("fe" + n, [(H("fe"), A("rse"), H("xe"))])
+            tt("nf" + n, H("nf"), qr, H("fe"), ALU.not_equal)
+            scan("rf" + n, [(H("rf"), H("nf"), H("xe"))])
+            ts("of" + n, A("off16", 16 * h + 1, 16 * h + 8, 2), last("rr", 32), BASE, ALU.add, pc(10), ALU.max)
+            ts("og" + n, A("off16", 16 * h, 16 * h + 8, 2), last("rf", 32), BASE, ALU.add, pc(3), ALU.max)
         zo = A("zout", 128 * s, 128 * s + 128)
-        z1 = A("zin", 512 * s, 512 * s + 128)
-        ts("qq" + n, H("q16", 8), last("ff"), -16368.0, ALU.add)
-        if h == 0:
-            dd = A("ps", 128, 256)
+        z1 = A("zin", 128 * s, 128 * s + 128)
+        if from_table(t, h):
+            dd, ss = A("pq", 0, 128), A("pq", 128, 256)
             act("gq" + n, H("gq"), IND(A("tab"), H("q16", 8)), AF.Copy)
             mm("xz" + n, [(dd, A("idn"), H("gq"), True, False), (dd, A("nid"), z1, False, True),
-                          (A("ps", 0, 128), A("idn"), H("gq"), True, False), (A("ps", 0, 128), A("idn"), z1, False, True)])
+                          (ss, A("idn"), H("gq"), True, False), (ss, A("idn"), z1, False, True)])
             act("zn" + n, zo, dd, AF.Abs)
-            act("hv" + n, H("hv"), A("ps", 0, 128), AF.Identity, bias=159.75, scale=0.5)
-            plus = lambda j: A("m160")
+            act("hv" + n, H("hv"), ss, AF.Identity, bias=159.75, scale=0.5)
+            plus = lambda o, k: A("m160", 0, k)
         else:
-            ts("pv" + n, H("pd16", 8), H("pt32", 8), 16.0, ALU.mult, pc(3), ALU.add)
-            act("zm" + n, A("zm"), z1, AF.Identity, bias=-192.0)
             act("zn" + n, zo, IND(H("gb", 4096), H("pd16", 8)), AF.Abs)
-            act("hv" + n, H("hv"), IND(H("gb", 4096), H("pd16", 8)), AF.Identity, bias=191.75, scale=0.5)
-            plus = lambda j: A("zm", 16 * j, 16 * j + 16)
+            act("hv" + n, H("hv"), IND(H("gb", 4096), H("pd16", 8)), AF.Identity, bias=-192.25, scale=0.5)
+            plus = lambda o, k: A("zb", 128 * s + o, 128 * s + o + k)
         act("ng" + n, H("nxg"), IND(A("nxb"), H("q16", 8)), AF.Copy)
-        sel16("cs" + n, A("pn", 0, 8), H("nxg"))
-        act("cn" + n, A("msg", m0, m0 + 8), A("pn", 0, 8), AF.Identity, bias=22528.0, scale=1.0 / 512)
-        tt("x2" + n, H("x2"), IND(H("t32", 256), H("pt16", 8)), A("dia"), ALU.mult)
-        scan("f2" + n, H("f2"), A("rst"), H("x2"))
-        tt("vn" + n, A("msg", m0 + 8, m0 + 16), last("f2"), A("msg", m0 + 8, m0 + 16), ALU.subtract)
-        s1, n1 = s + 2, "%d%d" % (t + 1, h)
-        dz, df = [], []
         if t + 1 < RO:
-            dz.append(((rank + 1) % N, A("zin", 512 * s1, 512 * s1 + 128), "az" + n1))
-            df.append(((rank + 1) % N, A("msg", SLOT * s1 + 8, SLOT * s1 + SLOT), "af" + n1))
-        other = part if t + 1 == RO else (part + 1) % N
-        if other != rank:
-            dz.append((other, A("pz", 128 * s1, 128 * s1 + 128), "bz" + n1))
-            df.append((other, A("pmsg", SLOT * s1, SLOT * s1 + 136), "bf" + n1))
-        send("sz" + n, zo, dz)
-        send("sf" + n, A("msg", m0, m0 + 136), df)
-        for j in range(8):
-            tt("sc%s%d" % (n, j), IND(A("tab"), A("off16", 16 * h + 2 * j, 16 * h + 2 * j + 1)),
-               A("hv", 128 * h + 16 * j, 128 * h + 16 * j + 16), plus(j), ALU.add)
+            sel16("cs" + n, A("pn", 0, 8), H("nxg"))
+            act("cn" + n, A("msg", m0, m0 + 8), A("pn", 0, 8), AF.Identity, bias=22528.0, scale=1.0 / 256)
+        tt("x2" + n, H("x2"), IND(H("t32", 256), H("pt16", 8)), A("dia"), ALU.mult)
+        scan("f2" + n, [(H("f2"), A("rst"), H("x2"))])
+        tt("vn" + n, A("msg", m0 + 8, m0 + 16), last("f2"), A("msg", m0 + 8, m0 + 16), ALU.subtract)
+        send("late", t, h)
+        k = 16 * wide
+        return lambda: [tt("sc%s%d" % (n, j), IND(A("tab"), A("off16", 16 * h + 2 * j, 16 * h + 2 * j + wide)),
+                           A("hv", 128 * h + k * j, 128 * h + k * j + k), plus(k * j, k), ALU.add) for j in range(8 // wide)]
 
     def penalty(t):
         n = str(t)
-        ts("kc" + n, A("kc"), A("ki"), 64, ALU.bitwise_and)
-        ts("kd" + n, A("kind"), A("kc"), 1.0, ALU.is_ge)
-        mm("c1" + n, [(A("pn", 16, 32), A("one"), A("kind"), True, True)])
-        act("c2" + n, A("cnj"), A("pn", 16, 32), AF.Identity, acc=A("cnt"))
-        cp("c3" + n, A("cni", 0, 1), A("cnt"))
-        ts("c4" + n, A("cni", 1, 2), A("cni", 0, 1), 31, ALU.bitwise_and)
-        cp("c5" + n, A("pnf"), A("cni", 1, 2))
-        add("S", "c6" + n, lambda g: [g.scalar.activation(ap(A("pend")), ap(A("idn")), AF.Identity, scale=ap(A("pnf")))],
-            [A("idn"), A("pnf")], [A("pend")], 128 * CYC + 0.03)
+        ts("kd" + n, A("kind"), A("pt32"), 16.0, ALU.is_ge)
+        mm("c1" + n, [(A("pq", 384, 400), A("one"), A("kind"), True, True)])
+        act("c2" + n, A("cnj"), A("pq", 384, 400), AF.Identity, bias=288.0, acc=A("cnt"))
+        act("c3" + n, A("cnf"), A("cnt"), AF.Identity, bias=-0.484375, scale=1.0 / 32)
+        act("c4" + n, A("pnf"), A("cnf"), AF.Identity, bias=A("cnt"), scale=-32.0)
+        act("c6" + n, A("pend"), A("idn"), AF.Identity, scale=A("pnf"))
+
+    def finish(h):
+        s, n = 2 * (RO - 1) + h, "%d%d" % (RO, h)
+        H = lambda b, k=128: A(b, k * h, k * h + k)
+        lanes = lambda b: A(b, 128 - 128 * h, 256 - 128 * h)
+        pd = "pd%d" % h
+        act("o_d%d" % h, H("dup", 256), IND(A("msg", SLOT * s + 8, SLOT * s + 136), lst(LF1, 16)), AF.Copy)
+        turn("o_t%d" % h, H("trp", 256), H("dup", 256))
+        act("o_h%d" % h, H("oh1"), IND(H("trp", 256), lst(LF2, 8)), AF.Abs, bias=-0.5, scale=2.0)
+        act("o_m%d" % h, lanes("oh"), H("oh1"), AF.Identity, bias=12288.5, scale=-1.0)
+        send("early", RO - 1, h)
+        recv("late", RO, h, part, "bz" + n)
+        recv("early", RO, h, part, "be" + n)
+        a2 = alike(n, h, A("zout", 128 * s, 128 * s + 128), A("pz", 128 * (s + 2), 128 * (s + 3)), lst(LZ, 8))
+        mm("as" + n, [(A("pa", 128, 256), A("blk8"), a2, True, True)])
+        ts("ak" + n, A(pd, 0, 128), A("pa", 128, 256), 1.0, ALU.is_ge)
+        ts("an" + n, A(pd, 128, 256), A("pa", 128, 256), 1.0, ALU.is_lt)
+        tt("o_k%d" % h, H("keep"), A(pd, 128, 256), lanes("oh"), ALU.mult)
+        tt("o_p%d" % h, A(pd, 256, 384), A(pd, 0, 128), lanes("ph"), ALU.mult)
+        tt("o_s%d" % h, lanes("ohs"), A(pd, 256, 384), H("keep"), ALU.add)
+        dma("S", "st_h%d" % h, [(T.yh[:, 128 - 128 * h:256 - 128 * h], T.ohs[:, 128 - 128 * h:256 - 128 * h])], [lanes("ohs")], [], LOCAL)
+        act("o_z%d" % h, lanes("oz"), IND(A("zout", 128 * s, 128 * s + 128), lst(LZ, 8)), AF.Copy)
+        act("o_r%d" % h, H("nxr"), IND(H("nxg"), lst(LZ, 8)), AF.Copy)
+        mm("o_n%d" % h, [(A("pn", 0, 128), A("bn"), H("nxr"), True, True)])
+        act("o_c%d" % h, lanes("oc"), A("pn", 0, 128), AF.Copy)
 
     for t in range(RO):
-        visit[0] = t
-        prep(t, 0); main(t, 0); prep(t, 1); main(t, 1); tail(t, 0); tail(t, 1)
+        prep(t, 0); main(t, 0); prep(t, 1)
+        s0 = tail(t, 0)
+        main(t, 1)
+        s1 = tail(t, 1)
+        s0(); s1()
         if t + 1 < RO:
             penalty(t)
-    visit[0] = None
-
-    dma("Y", "st_x", T.yx[:], T.tab[:, 16:4112], [A("tab")], [], LOCAL + 4.0)
-    for h in range(2):
-        s = 2 * (RO - 1) + h
-        act("fc%d" % h, A("fin", 136 * h, 136 * h + 72), A("msg", SLOT * s, SLOT * s + 72), AF.Copy)
-        exchange(RO, h, A("zout", 128 * s, 128 * s + 128), A("msg", SLOT * s + 72, SLOT * s + 136), A("fin", 136 * h + 72, 136 * h + 136))
-    for h in range(2):
-        act("oz%d" % h, A("oz", 128 * h, 128 * h + 128), IND(A("zout", 1024, 1280), lst(LZ + 32 * h, 8)), AF.Copy)
-    dma("Y", "st_z", T.yz[:], T.oz[:], [A("oz")], [], LOCAL)
-    cp("o_d", A("dup"), IND(A("fin"), lst(LF1, 34)))
-    add("V", "o_t", lambda g: [g.vector.transpose(ap(A("trp")), ap(A("dup")))], [A("dup")], [A("trp")], 544 * CYC)
-    act("o_h", A("oh1"), IND(A("trp"), lst(LF2, 16)), AF.Abs, bias=-0.5, scale=2.0)
-    ts("o_c", A("oc"), IND(A("trp"), lst(LF2 + 16, 1)), -22528.0, ALU.add)
-    ts("o_m", A("oh"), A("oh1"), -1.0, ALU.mult, 12288.5, ALU.add)
-    dma("Y", "st_c", T.yc[:], T.oc[:], [A("oc")], [], LOCAL)
-    dma("S", "st_h", T.yh[:], T.oh[:], [A("oh")], [], LOCAL)
+    dma("Y", "st_x", [(T.yx[:], T.tab[:, SPARE:])], [A("tab")], [], LOCAL + CFG["table"])
+    finish(0); finish(1)
+    dma("Y", "st_z", [(T.yz[:], T.oz[:])], [A("oz")], [], LOCAL)
+    dma("Y", "st_c", [(T.yc[:], T.oc[0:128:16, :])], [A("oc")], [], LOCAL)
     return ops
 
 
@@ -435,11 +541,13 @@ def hazards(ops):
                 psum = SCRATCH[b][0] == "psum"
                 for j, k2, l2, h2 in hist.get(b, ()):
                     same = ops[j]["q"] == o["q"] and o["q"] in ("V", "S", "P", "G") and ops[j]["sem"] is None
+                    clash = l2 < hi and lo < h2 and (kind == "w" or k2 == "w")
+                    if psum and o.get("grp") and ops[j].get("grp") == o["grp"]:
+                        continue
                     if psum:
-                        d[j] = d.get(j, False) or not same
-                    elif l2 < hi and lo < h2 and (kind == "w" or k2 == "w"):
-                        raw = kind == "r"
-                        d[j] = d.get(j, False) or raw or not same or (SAME_QUEUE_WAW and o["q"] != "P")
+                        d[j] = d.get(j, False) or not same or (clash and o["q"] != "P")
+                    elif clash:
+                        d[j] = True
         for kind, regs in (("r", o["rd"]), ("w", o["wr"])):
             for b, lo, hi, _ in regs:
                 hh = hist.setdefault(b, [])
@@ -462,55 +570,54 @@ def schedule(ops):
     pre = [dict(d) for d in deps]
     for i, o in enumerate(ops):
         if o["after"]:
-            pre[i][idx[o["after"]]] = True
+            pre[i][idx[o["after"]]] = o["q"] is None
     succ = [[] for _ in ops]
     for i in range(n):
         for j in pre[i]:
             succ[j].append(i)
     cost = [max(o["cost"], 1e-4) for o in ops]
-    lag = [o["lat"] + PAR["hop"] for o in ops]
+    lag = [o["lat"] + CFG["hop"] for o in ops]
 
     def place(key, back):
         before, behind = (succ, pre) if back else (pre, succ)
         left = [len(b) for b in before]
         ready = [ops[i]["lat"] if back else 0.0 for i in range(n)]
         start = [0.0] * n
-        busy = {}
-        avail = {i: key[i] for i in range(n) if left[i] == 0}
-        while avail:
-            i = min(avail, key=avail.get)
-            del avail[i]
-            st = ready[i]
-            if ops[i]["q"]:
-                b = busy.setdefault(ops[i]["q"], [])
-                k = len(b)
-                while k > 0 and b[k - 1][1] > st:
-                    k -= 1
-                while k < len(b) and b[k][0] < st + cost[i]:
-                    st = max(st, b[k][1])
-                    k += 1
-                b.insert(k, (st, st + cost[i]))
+        free = {o["q"]: 0.0 for o in ops}
+        avail = {q: [i for i in range(n) if ops[i]["q"] == q and not left[i]] for q in free}
+        while any(avail.values()):
+            st, q = min(((max(free[q], min(ready[i] for i in l)), q) for q, l in avail.items() if l), key=lambda x: x[0])
+            i = min((i for i in avail[q] if ready[i] <= st), key=lambda i: key[i])
+            avail[q].remove(i)
             start[i] = st
+            if q:
+                free[q] = st + cost[i]
             for k in behind[i]:
                 gap = (lag[k] if pre[i][k] else 0.0) if back else (lag[i] if pre[k][i] else 0.0)
                 ready[k] = max(ready[k], st + cost[i] + gap)
                 left[k] -= 1
                 if left[k] == 0:
-                    avail[k] = key[k]
+                    avail[ops[k]["q"]].append(k)
         return start, max(start[i] + cost[i] + (0.0 if back else ops[i]["lat"]) for i in range(n))
 
-    def run(plan):
-        if isinstance(plan, str):
-            names = ["period"] + [o["cls"] for o in ops if o["cls"] == o["name"] or o["t"] == 2]
-            plan = dict(zip(names, [0.1 * int(x) for x in plan.split()]))
-        start, total = place([plan.get(o["cls"], 0.0) + plan["period"] * o["t"] for o in ops], False)
-        order = sorted(range(n), key=lambda i: (start[i], i))
-        return {ops[i]["name"]: k for k, i in enumerate(order)}, total, start
+    way = [0.0] * n
+    left = [len(s) for s in succ]
+    todo = [i for i in range(n) if not left[i]]
+    for i in todo:
+        way[i] = cost[i] + max([ops[i]["lat"]] + [way[k] + (lag[i] if pre[k][i] else 0.0) for k in succ[i]])
+        for j in pre[i]:
+            left[j] -= 1
+            if not left[j]:
+                todo.append(j)
+    best = start, total = place([-x for x in way], False)
+    for _ in range(CFG["passes"]):
+        back, _ = place([-(start[i] + cost[i]) for i in range(n)], True)
+        start, total = place([-(back[i] + cost[i]) for i in range(n)], False)
+        if total < best[1]:
+            best = start, total
+    return best
 
-    return run, place
 
-
-PLAN = """233 -8 23 -128 87 5 -204 -327 -103 -103 52 -25 -108 -46 -86 216 214 135 -63 154 268 -145 27 -229 -201 -98 32 -154 -381 -263 -146 -79 -446 -218 -166 -13 -424 -204 -64 4 -86 214 87 117 90 174 -168 148 81 143 -63 -292 -158 24 18 -346 -207 -197 -134 -214 -116 -304 -98 54 159 130 128 178 193 204 45 -108 65 25 -33 55 58 -101 62 71 10 -10 -34 -232 23 22 -24 32 -128 57 83 -234 54 102 -171 77 92 103 118 79 40 127 -32 100 226 100 -93 148 99 119 189 140 173 159 110 164 115 190 -11 75 172 -6 -68 84 103 -35 -5 -60 -99 22 52 83 -12 99 105 97 63 115 200 165 -92 121 147 109 99 108 194 68 174 172 -87 151 46 226 -51 174 226 152 236 -7 78 -112 40 -385 -95 -119 -140 -89 -147 -25 125 163 126 61 72 26 186 131 233 94 -62 274 67 209 211 56 241 249 138 161 255 275 105 224 109 129 234 244 94 81 255 279 250 248 20 -47 -9 149 164 151 102 259 298 281 285 20 267 179 144 134 186 278 289 278 389 369 162 138 438 366 434 1053 834 1346 1177 1289 880 905 1346 1099 931 989 1089 1061 834 962 1202 1402 1280 1289 1206 1536 1250 1157 1337 1247 1600 1415 1128 1081 1170 1199 1184 1181"""
 ORDER = {}
 
 
@@ -519,7 +626,9 @@ def rank_program(g, core, T, topo):
     if rank is None:
         return
     if not ORDER:
-        ORDER.update(schedule(build(T, topo, 0))[0](PLAN)[0])
+        ops = build(T, topo, 0)
+        start = schedule(ops)[0]
+        ORDER.update({ops[i]["name"]: k for k, i in enumerate(sorted(range(len(ops)), key=lambda i: (start[i], i)))})
     ops = build(T, topo, rank)
     deps = hazards(ops)
     queue = {"V": g.vector, "S": g.scalar, "P": g.tensor, "G": g, "Y": g.sync}
@@ -527,7 +636,9 @@ def rank_program(g, core, T, topo):
     known = {q: {} for q in queue}
     done = {}
     sent = 0
-    for i in sorted(range(len(ops)), key=lambda i: ORDER[ops[i]["name"]]):
+    order = sorted(range(len(ops)), key=lambda i: ORDER[ops[i]["name"]])
+    closer = {ops[i]["grp"]: i for i in order if ops[i].get("grp")}
+    for i in order:
         o = ops[i]
         q = o["q"]
         if q is None:
@@ -544,7 +655,7 @@ def rank_program(g, core, T, topo):
                 queue[q].wait_ge(T.sem[sem], val)
                 for s2, v2 in clock.items():
                     kn[s2] = max(kn.get(s2, 0), v2)
-        ins = o["fn"](g)
+        ins = o["fn"](g, True) if closer.get(o.get("grp")) == i else o["fn"](g)
         if o["sem"] == "sent":
             sent += o["val"]
             continue
@@ -563,5 +674,6 @@ def rank_program(g, core, T, topo):
     g.wait_ge(T.sem.sent, sent)
     for q in count:
         g.wait_ge(T.sem["c" + q], count[q])
-    for s in ("st_z", "st_c", "st_h", "st_x"):
-        g.wait_ge(T.sem[s], 16)
+    for o in ops:
+        if o["sem"] in STORES:
+            g.wait_ge(T.sem[o["sem"]], o["val"])

@@ -4,25 +4,30 @@ from concourse.mybir import AluOpType as ALU, ActivationFunctionType as AF
 RO = 5
 SLOT = 144
 SPARE = 32
-CFG = dict(route=("CCAACCAA", "DDADDDDB"), first=("CCAACCAA", "DDADDDDB"), last=("CCAACCAA", "DDADDDDB"),
-           dup="VV", merge=False, zq="V", passes=6, xs="VV", cs="SS", wide="12",
+CFG = dict(route=("CCAADCAA", "DDBDDDDB"), first=("CCAADCAA", "DDBDDDDB"), last=("CCAADCAA", "DDBDDDDB"),
+           dup="VL", cs0="VS", merge="--------", zq="VV", passes=6, xs="SS", cs="VS", wide="12", x2="VS", xe="P", gdma=1.0, acc=0.8,
            cyc=0.95e-3, gat=1.56, sca=3.8, pec=0.5e-3, hop=0.18, call=0.5, remote=2.6, local=2.0, table=3.2)
+CFG.update(seed=3, rounds=1300)
+PACE = [dict(cyc=0.83e-3, pec=0.44e-3, hop=0.2, gat=1.56, sca=3.8, remote=2.3, local=1.9),
+        dict(cyc=1.15e-3, pec=0.6e-3, hop=0.2, gat=1.95, sca=5.0, remote=3.0, local=2.3),
+        dict(cyc=0.87e-3, pec=0.46e-3, hop=0.17, gat=1.2, sca=2.5, remote=3.2, local=2.6),
+        dict(cyc=1.0e-3, pec=0.53e-3, hop=0.23, gat=1.5, sca=4.0, remote=2.7, local=2.1)]
 
 SCRATCH = {
     "tab": ("sbuf", [128, 4096 + SPARE], "bfloat16"), "nxb": ("sbuf", [128, 4096 + SPARE], "bfloat16"),
     "gb": ("sbuf", [128, 8192], "bfloat16"), "ab": ("sbuf", [128, 8192], "bfloat16"),
-    "msg": ("sbuf", [128, SLOT * 10], "float32"), "pmsg": ("sbuf", [128, 72 * 10], "float32"),
+    "msg": ("sbuf", [128, SLOT * 10], "float32"), "pmsg": ("sbuf", [128, 120 * 10], "float32"),
     "nz": ("sbuf", [128, 5120], "bfloat16"), "crp": ("sbuf", [128, 128], "float32"),
     "zin": ("sbuf", [128, 1280], "bfloat16"), "zout": ("sbuf", [128, 1280], "bfloat16"),
     "pz": ("sbuf", [128, 1536], "bfloat16"), "zb": ("sbuf", [128, 1280], "bfloat16"),
     "t32": ("sbuf", [128, 512], "int32"), "o32": ("sbuf", [128, 512], "int32"), "o16": ("sbuf", [128, 512], "uint16"),
     "kf": ("sbuf", [128, 512], "float32"), "ki": ("sbuf", [128, 16], "int32"), "pt32": ("sbuf", [128, 16], "int32"),
-    "pt16": ("sbuf", [128, 16], "uint16"), "pd16": ("sbuf", [128, 16], "uint16"), "q16": ("sbuf", [128, 16], "uint16"),
+    "pt16": ("sbuf", [128, 32], "uint16"), "q16": ("sbuf", [128, 16], "uint16"),
     "bx": ("sbuf", [128, 256], "bfloat16"), "off16": ("sbuf", [128, 32], "uint16"), "kind": ("sbuf", [128, 16], "bfloat16"),
     "xx": ("sbuf", [128, 256], "float32"), "ff": ("sbuf", [128, 256], "float32"), "ne": ("sbuf", [128, 256], "float32"),
     "rr": ("sbuf", [128, 256], "float32"), "x2": ("sbuf", [128, 256], "float32"), "f2": ("sbuf", [128, 256], "float32"),
     "xe": ("sbuf", [128, 256], "float32"), "fe": ("sbuf", [128, 256], "float32"), "nf": ("sbuf", [128, 256], "float32"),
-    "rf": ("sbuf", [128, 256], "float32"),
+    "rf": ("sbuf", [128, 256], "float32"), "g2": ("sbuf", [128, 256], "float32"),
     "gq": ("sbuf", [128, 256], "bfloat16"), "hv": ("sbuf", [128, 256], "bfloat16"),
     "nxg": ("sbuf", [128, 256], "bfloat16"), "al1": ("sbuf", [128, 256], "bfloat16"), "al2": ("sbuf", [128, 256], "bfloat16"),
     "alk": ("sbuf", [128, 16], "float32"), "dif": ("sbuf", [128, 128], "float32"), "tmp": ("sbuf", [128, 128], "float32"),
@@ -34,8 +39,8 @@ SCRATCH = {
     "lio": ("sbuf", [128, 80], "float32"), "lst": ("sbuf", [128, 96], "uint16"),
     "idn": ("sbuf", [128, 128], "bfloat16"), "nid": ("sbuf", [128, 128], "bfloat16"), "wd": ("sbuf", [128, 144], "bfloat16"),
     "idf": ("sbuf", [128, 128], "float32"), "nif": ("sbuf", [128, 128], "float32"), "bn": ("sbuf", [128, 128], "bfloat16"),
-    "s8": ("sbuf", [128, 8], "bfloat16"), "ns8": ("sbuf", [128, 8], "bfloat16"), "sj": ("sbuf", [128, 8], "bfloat16"),
-    "cj": ("sbuf", [128, 8], "bfloat16"), "anew": ("sbuf", [128, 256], "float32"), "rev": ("sbuf", [128, 256], "bfloat16"),
+    "s8": ("sbuf", [128, 8], "bfloat16"), "ns8": ("sbuf", [128, 8], "bfloat16"), "sj": ("sbuf", [128, 16], "bfloat16"),
+    "cj": ("sbuf", [128, 16], "bfloat16"), "anew": ("sbuf", [128, 256], "float32"), "rev": ("sbuf", [128, 256], "bfloat16"),
     "blk8": ("sbuf", [128, 128], "bfloat16"), "die": ("sbuf", [128, 128], "float32"), "rse": ("sbuf", [128, 128], "float32"),
     "blk": ("sbuf", [128, 128], "float32"), "dia": ("sbuf", [128, 128], "float32"), "rst": ("sbuf", [128, 128], "float32"),
     "b1": ("sbuf", [128, 256], "bfloat16"), "b2": ("sbuf", [128, 256], "bfloat16"),
@@ -54,7 +59,8 @@ SCRATCH = {
 }
 STORES = ["st_x", "st_h0", "st_h1", "st_z", "st_c"]
 SEMAPHORES = (["cV", "cS", "cP", "cG", "sent", "ld_m", "ld_c", "ld_z", "ld_t", "ld_nx", "nx_b"] + STORES
-              + ["%s%d%d" % (k, t, h) for k in ("az", "ae", "bz", "be", "du") for t in range(1, RO + 1) for h in range(2)])
+              + ["%s%d%d" % (k, t, h) for k in ("az", "ac", "ae", "bz", "be", "du") for t in range(1, RO + 1) for h in range(2)]
+              + ["fa%d%d" % (h, u) for h in range(2) for u in range(8)])
 
 L1, L2, LZ, LF1, LF2, LJ, LG = 0, 18, 38, 46, 62, 70, 74
 
@@ -76,9 +82,9 @@ def deal(n, total):
         k[i] *= 2
 
 
-def build(T, topo, rank):
+def build(T, topo, rank, pace=CFG):
     ops = []
-    CYC, GAT, SCA, PEC, REMOTE, LOCAL = [CFG[k] for k in ("cyc", "gat", "sca", "pec", "remote", "local")]
+    CYC, GAT, SCA, PEC, REMOTE, LOCAL = [pace[k] for k in ("cyc", "gat", "sca", "pec", "remote", "local")]
     N = len(T.cores)
     me = T.cores[rank]
     BASE = float(SPARE - 16384)
@@ -186,20 +192,21 @@ def build(T, topo, rank):
         zo = A("zout", 128 * s, 128 * s + 128)
         out = []
         if t + 1 == RO:
-            if kind == "late":
+            if kind == "mid":
                 out.append((zo, r ^ 1, A("pz", 128 * s1, 128 * s1 + 128), "bz" + n1))
             else:
                 out.append((A("oh", 128 - 128 * h, 256 - 128 * h), r ^ 1, A("ph", 128 - 128 * h, 256 - 128 * h), "be" + n1))
         elif kind == "late":
-            out.append((A("msg", SLOT * s, SLOT * s + 64), nxt, A("msg", SLOT * s1 + 8, SLOT * s1 + 72), "az" + n1))
+            out.append((A("msg", SLOT * s, SLOT * s + 16), nxt, A("msg", SLOT * s1 + 8, SLOT * s1 + 24), "ac" + n1))
+        elif kind == "mid":
             out.append((zo, nxt, A("zin", 128 * s1, 128 * s1 + 128), "az" + n1))
             if other != r:
                 out.append((zo, other, A("pz", 128 * s1, 128 * s1 + 128), "bz" + n1))
         else:
-            src = A("msg", SLOT * s + 64, SLOT * s + 136)
-            out.append((src, nxt, A("msg", SLOT * s1 + 72, SLOT * s1 + SLOT), "ae" + n1))
+            src = A("msg", SLOT * s + 16, SLOT * s + 136)
+            out.append((src, nxt, A("msg", SLOT * s1 + 24, SLOT * s1 + SLOT), "ae" + n1))
             if other != r:
-                out.append((src, other, A("pmsg", 72 * s1, 72 * s1 + 72), "be" + n1))
+                out.append((src, other, A("pmsg", 120 * s1, 120 * s1 + 120), "be" + n1))
         k = deal(len(out), len(topo.engines(T.cores[r], T.cores[out[0][1]])))
         return [o + (e,) for o, e in zip(out, k)]
 
@@ -235,8 +242,8 @@ def build(T, topo, rank):
     dma("Y", "ld_m", [(T.inb[:, 0:256], T.mem[:])], [], [A("inb", 0, 256)], LOCAL)
     dma("S", "ld_c", [(T.inb[:, 256:272], T.plc[:])], [], [A("inb", 256, 272)], LOCAL)
     dma("S", "ld_z", [(T.ztb[:], T.zt[:])], [], [A("ztb")], LOCAL)
-    dma("Y", "ld_t", [(T.tab[:, SPARE:], T.xt[:])], [], [A("tab", SPARE)], LOCAL + CFG["table"], after="ld_m")
-    dma("Y", "ld_nx", [(T.nxi[:], T.nxt[:])], [], [A("nxi")], LOCAL + CFG["table"] + 0.4, after="ld_t")
+    dma("S", "ld_nx", [(T.nxi[:], T.nxt[:])], [], [A("nxi")], LOCAL + 0.4, after="ld_z")
+    dma("Y", "ld_t", [(T.tab[:, SPARE:], T.xt[:])], [], [A("tab", SPARE)], LOCAL + CFG["table"] + 0.4, after="ld_m")
 
     iota("i_p", A("pi"), [[0, 1]], 0, 1)
     iota("i_l1c", A("lio", L1, L1 + 2), [[0, 2]], 143)
@@ -266,13 +273,14 @@ def build(T, topo, rank):
         ts("lc%d" % h, lst(L2 + 10 * h, 1), pc(2), pc(0), ALU.subtract, 15.0 - 8 * h, ALU.add)
     ts("lj", lst(LJ, 4), A("lio", L1 + 2, L1 + 6), 0.0, ALU.mult, pc(0), ALU.add)
     cp("lg", lst(LG, 8), A("ci", 0, 8))
-    cp("cj", A("cj"), A("ci", 0, 8))
+    cp("cj", A("cj", 0, 8), A("ci", 0, 8))
+    ts("cjp", A("cj", 8, 16), A("ci", 0, 128, 16), pc(3), ALU.add)
     ts("idn", A("idn"), A("ci", 0, 128), pc(5), ALU.is_equal)
     act("nid", A("nid"), A("idn"), AF.Identity, scale=-1.0)
     ts("p8", pc(8), pc(4), 15.0, ALU.add)
     ts("wd", A("wd"), A("ci"), pc(8), ALU.is_equal, 256.0, ALU.mult)
-    for name, v in (("s8", 32.0), ("ns8", -32.0), ("sj", 8.0)):
-        ts(name, A(name), A("ci", 0, 128, 16), pc(4), ALU.is_equal, v, ALU.mult)
+    for name, out, v in (("s8", A("s8"), 32.0), ("ns8", A("ns8"), -32.0), ("sj", A("sj", 0, 8), 8.0), ("sjp", A("sj", 8, 16), 128.0)):
+        ts(name, out, A("ci", 0, 128, 16), pc(4), ALU.is_equal, v, ALU.mult)
     ts("anew", A("anew"), A("b2"), 0.0, ALU.is_equal, 1.0e6, ALU.mult)
     ts("blk", A("blk"), A("cg"), pc(4), ALU.is_equal)
     act("bn", A("bn"), A("blk"), AF.Copy)
@@ -283,6 +291,10 @@ def build(T, topo, rank):
         ts("die", A("die"), A("c32"), pc(3), ALU.is_equal)
         act("rse", A("rse"), A("die"), AF.Identity, scale=-1.0, bias=1.0)
         ts("p10", pc(10), pc(3), 16.0, ALU.add)
+        if CFG["xe"] != "V":
+            act("diep", A("pq", 256, 384), A("die"), AF.Copy)
+    if CFG["x2"] != "VV":
+        act("diap", A("pq", 128, 256), A("dia"), AF.Copy)
     if set(CFG["xs"] + CFG["cs"]) != {"V"}:
         act("idf", A("idf"), A("idn"), AF.Copy)
     if set(CFG["xs"]) != {"V"}:
@@ -325,8 +337,8 @@ def build(T, topo, rank):
         if src == rank:
             zp, yp = A("zout", 128 * (s - 2), 128 * (s - 1)), A("msg", SLOT * (s - 2) + 72, SLOT * (s - 2) + 136)
         else:
-            zp, yp = A("pz", 128 * s, 128 * s + 128), A("pmsg", 72 * s + 8, 72 * s + 72)
-            recv("late", t, h, src, "bz" + n)
+            zp, yp = A("pz", 128 * s, 128 * s + 128), A("pmsg", 120 * s + 56, 120 * s + 120)
+            recv("mid", t, h, src, "bz" + n)
             recv("early", t, h, src, "be" + n)
         H = lambda b, k=128: A(b, k * h, k * h + k)
         sel16("as" + n, A("pa", 128, 136), alike(n, h, A("zin", 128 * s, 128 * s + 128), zp))
@@ -350,23 +362,27 @@ def build(T, topo, rank):
         m0, z0 = SLOT * s, 512 * s
         z1 = A("zin", 128 * s, 128 * s + 128)
         if t > 0:
-            recv("late", t, h, prev, "az" + n)
+            recv("mid", t, h, prev, "az" + n)
+            recv("late", t, h, prev, "ac" + n)
             recv("early", t, h, prev, "ae" + n)
-        for name, use, out, scale, bias in (("nz", set(routes(t, h)) & set("AB"), A("nz", z0, z0 + 128), -1.0, 0.0),
-                                            ("zb", "D" in routes(t, h) or not from_table(t, h), A("zb", 128 * s, 128 * s + 128), 1.0, 192.0)):
-            if use and CFG["zq"] == "V":
+        for name, use, out, scale, bias in (("nz", set(routes(t, h)) & set("ABF"), A("nz", z0, z0 + 128), -1.0, 0.0),
+                                            ("zb", set(routes(t, h)) & set("DE") or not from_table(t, h), A("zb", 128 * s, 128 * s + 128), 1.0, 192.0)):
+            if use and CFG["zq"][h] == "V":
                 ts(name + n, out, z1, scale, ALU.mult, bias, ALU.add)
             elif use:
                 act(name + n, out, z1, AF.Identity, scale=scale, bias=bias)
-        if set(routes(t, h)) & set("AB"):
+        if set(routes(t, h)) & set("ABF"):
             if t and CFG["dup"][h] == "L":
                 dma("Y", "du" + n, [(T.nz[:, z0 + 128 * r:z0 + 128 * r + 128], T.nz[:, z0:z0 + 128]) for r in (1, 2, 3)],
                     [A("nz", z0, z0 + 128)], [A("nz", z0 + 128, z0 + 512)], LOCAL + 0.4)
             else:
                 for i in range(2):
-                    cp("d%d%s" % (i + 1, n), A("nz", z0 + (128 << i), z0 + (256 << i)), A("nz", z0, z0 + (128 << i)))
+                    if t and CFG["dup"][h] == "S":
+                        act("d%d%s" % (i + 1, n), A("nz", z0 + (128 << i), z0 + (256 << i)), A("nz", z0, z0 + (128 << i)), AF.Copy)
+                    else:
+                        cp("d%d%s" % (i + 1, n), A("nz", z0 + (128 << i), z0 + (256 << i)), A("nz", z0, z0 + (128 << i)))
         c = IND(A("msg", m0 + 8, m0 + 16), lst(LJ, 4))
-        if t and CFG["cs"][h] != "V":
+        if CFG["cs" if t else "cs0"][h] != "V":
             act("cr" + n, A("crp", 64 * h, 64 * h + 64), c, AF.Copy)
             mm("cp" + n, [(A("ps", 0, 64), A("idf"), A("crp", 64 * h, 64 * h + 64), True, True)])
             c = A("ps", 0, 64)
@@ -382,7 +398,7 @@ def build(T, topo, rank):
                 ts("to" + nb, A("o32", o, o + 64), A("t32", o, o + 64), 16384 | 4095, ALU.bitwise_and)
                 ts("tu" + nb, A("o16", o, o + 64), A("o32", o, o + 64), BASE, ALU.add)
 
-    nr2 = [0]
+    nr2, uses = [0], {}
 
     def main(t, h):
         n, s = "%d%d" % (t, h), 2 * t + h
@@ -394,31 +410,37 @@ def build(T, topo, rank):
             r2 = routes(t, h)[2 * w:2 * w + 2]
             G = lambda b, u, k=1: A(b, 4096 * h + 16 * base + 512 * u, 4096 * h + 16 * base + 512 * (u + k))
             gath = lambda u, k=1: IND(A("tab"), A("o16", 256 * h + base + 32 * u, 256 * h + base + 32 * (u + k)))
-            both = CFG["merge"] and r2 in ("CC", "DD")
+            both = CFG["merge"][4 * h + w] == "m" and r2 in ("CC", "DD")
             for u in range(2):
                 nu, r = "%s%d" % (n, 2 * w + u), r2[u]
                 k = 2 if both else 1
                 if r in "AB":
                     tt("mg" + nu, G("gb", u), gath(u), z4, ALU.add)
                 elif r == "C" and not (both and u):
-                    act("mg" + nu, G("gb", u, k), gath(u, k), AF.Copy)
+                    act("mg" + nu, G("ab", u, k), gath(u, k), AF.Copy)
+                elif r == "F":
+                    act("mg" + nu, G("gb", u), gath(u), AF.Copy)
+                    sem = "fa%d%d" % (h, 2 * w + u)
+                    uses[sem] = uses.get(sem, 0) + 16
+                    add("G", "md" + nu, lambda g, o=G("gb", u): [g.dma_start(ap(o), ap(z4), accum_op=ALU.add)], [z4, G("gb", u)], [G("gb", u)],
+                        CFG["gdma"], lat=LOCAL + CFG["acc"], sem=sem, val=uses[sem])
                 elif not (both and u):
                     act("mg" + nu, G("ab", u, k), gath(u, k), AF.Identity, bias=192.0)
-                if r == "D":
+                if r in "DE":
                     g0, a0 = G("gb", u)[1], G("ab", u)[1]
                     scan("md" + nu, [(A("gb", g0 + 128 * i, g0 + 128 * i + 128), A("ab", a0 + 128 * i, a0 + 128 * i + 128), zb) for i in range(4)],
                          ALU.max, ALU.subtract)
-                if r in "AD":
+                if r in "ADF":
                     ts("ma" + nu, G("ab", u), G("gb", u), 0.0, ALU.max, 2.0, ALU.mult)
-                elif r == "B":
+                elif r in "BE":
                     act("ma" + nu, G("ab", u), G("gb", u), AF.Abs)
                 else:
                     pd = "pd%d" % (nr2[0] % 2); nr2[0] += 1
-                    mm("md" + nu, [(A(pd), A("idn"), G("gb", u), True, False)]
+                    mm("md" + nu, [(A(pd), A("idn"), G("ab", u), True, False)]
                        + [(A(pd, 128 * i, 128 * i + 128), A("nid"), z1, False, i == 3) for i in range(4)])
-                    act("ma" + nu, G("ab", u), A(pd), AF.Abs)
-                for name, b, sel in (("mw", "gb", "ns8"), ("ms", "ab", "s8")):
-                    if name == "ms" or r in "AD":
+                    act("ma" + nu, G("gb", u), A(pd), AF.Abs)
+                for name, b, sel in (("mw", "gb", "ns8"), ("ms", "gb" if r == "C" else "ab", "s8")):
+                    if name == "ms" or r in "ADF":
                         c0, o = base // 8 + 4 * u, G(b, u)[1]
                         mm(name + nu, [(A(key, c0 + i, 256, 32), A(b, o + 128 * i, o + 128 * i + 128), A(sel), False, False) for i in range(4)], key + n)
         if t:
@@ -433,13 +455,14 @@ def build(T, topo, rank):
         scan("mn" + n, [(H("kf", 256), A("anew"), A(key, 0, 256))], ALU.add, ALU.min)
         cp("ki" + n, H("ki", 8), A("kf", 256 * h + 31, 256 * h + 256, 32))
         ts("pt" + n, H("pt32", 8), H("ki", 8), 31, ALU.bitwise_and)
-        pos = A(key, 384, 392)
+        pos = A(key, 384, 400)
+        pt16, pd16 = A("pt16", 16 * h, 16 * h + 8), A("pt16", 16 * h + 8, 16 * h + 16)
         tt("bx" + n, H("bx"), IND(H("pt32", 8), lst(LG, 8)), A("dia"), ALU.mult)
-        mm("tr" + n, [(pos, H("bx"), A("sj"), True, False), (pos, A("idn"), A("cj"), False, True)])
-        cp("pu" + n, H("pt16", 8), pos)
-        if not from_table(t, h):
-            ts("pv" + n, H("pd16", 8), pos, 16.0, ALU.mult, pc(3), ALU.add)
-        tt("xx" + n, H("xx"), IND(H("o32", 256), H("pt16", 8)), A("dia"), ALU.mult)
+        mm("tr" + n, [(pos, A("idn"), A("cj"), True, False), (pos, H("bx"), A("sj"), False, True)])
+        cp("pu" + n, H("pt16", 16), pos)
+        act("zn" + n, A("zout", 128 * s, 128 * s + 128), IND(H("gb", 4096), pd16), AF.Abs)
+        send("mid", t, h)
+        tt("xx" + n, H("xx"), IND(H("o32", 256), pt16), A("dia"), ALU.mult)
         scan("ff" + n, [(H("ff"), A("rst"), H("xx"))])
         ts("qq" + n, H("q16", 8), last("ff"), BASE, ALU.add)
         qr = A(key, 256, 384)
@@ -450,34 +473,38 @@ def build(T, topo, rank):
         if wide == 1:
             ts("of" + n, A("off16", 16 * h, 16 * h + 16, 2), last("rr"), BASE, ALU.add, pc(3), ALU.max)
         else:
-            tt("xe" + n, H("xe"), IND(H("o32", 256), H("pt16", 8)), A("die"), ALU.mult)
+            if CFG["xe"] == "V":
+                tt("xe" + n, H("xe"), IND(H("o32", 256), pt16), A("die"), ALU.mult)
+            else:
+                tt("xe" + n, H("xe"), A("pq", 256, 384), H("xx"), ALU.mult)
             scan("fe" + n, [(H("fe"), A("rse"), H("xe"))])
             tt("nf" + n, H("nf"), qr, H("fe"), ALU.not_equal)
             scan("rf" + n, [(H("rf"), H("nf"), H("xe"))])
             ts("of" + n, A("off16", 16 * h + 1, 16 * h + 8, 2), last("rr", 32), BASE, ALU.add, pc(10), ALU.max)
             ts("og" + n, A("off16", 16 * h, 16 * h + 8, 2), last("rf", 32), BASE, ALU.add, pc(3), ALU.max)
-        zo = A("zout", 128 * s, 128 * s + 128)
         z1 = A("zin", 128 * s, 128 * s + 128)
         if from_table(t, h):
-            dd, ss = A("pq", 0, 128), A("pq", 128, 256)
+            ss = A("pd0", 0, 128)
             act("gq" + n, H("gq"), IND(A("tab"), H("q16", 8)), AF.Copy)
-            mm("xz" + n, [(dd, A("idn"), H("gq"), True, False), (dd, A("nid"), z1, False, True),
-                          (ss, A("idn"), H("gq"), True, False), (ss, A("idn"), z1, False, True)])
-            act("zn" + n, zo, dd, AF.Abs)
+            mm("xz" + n, [(ss, A("idn"), H("gq"), True, False), (ss, A("idn"), z1, False, True)])
             act("hv" + n, H("hv"), ss, AF.Identity, bias=159.75, scale=0.5)
             plus = lambda o, k: A("m160", 0, k)
         else:
-            act("zn" + n, zo, IND(H("gb", 4096), H("pd16", 8)), AF.Abs)
-            act("hv" + n, H("hv"), IND(H("gb", 4096), H("pd16", 8)), AF.Identity, bias=-192.25, scale=0.5)
+            act("hv" + n, H("hv"), IND(H("gb", 4096), pd16), AF.Identity, bias=-192.25, scale=0.5)
             plus = lambda o, k: A("zb", 128 * s + o, 128 * s + o + k)
         act("ng" + n, H("nxg"), IND(A("nxb"), H("q16", 8)), AF.Copy)
         if t + 1 < RO:
             sel16("cs" + n, A("pn", 0, 8), H("nxg"))
             act("cn" + n, A("msg", m0, m0 + 8), A("pn", 0, 8), AF.Identity, bias=22528.0, scale=1.0 / 256)
-        tt("x2" + n, H("x2"), IND(H("t32", 256), H("pt16", 8)), A("dia"), ALU.mult)
+        if CFG["x2"][h] == "V":
+            tt("x2" + n, H("x2"), IND(H("t32", 256), pt16), A("dia"), ALU.mult)
+        else:
+            act("g2" + n, H("g2"), IND(H("t32", 256), pt16), AF.Copy)
+            tt("x2" + n, H("x2"), A("pq", 128, 256), H("g2"), ALU.mult)
         scan("f2" + n, [(H("f2"), A("rst"), H("x2"))])
         tt("vn" + n, A("msg", m0 + 8, m0 + 16), last("f2"), A("msg", m0 + 8, m0 + 16), ALU.subtract)
-        send("late", t, h)
+        if t + 1 < RO:
+            send("late", t, h)
         k = 16 * wide
         return lambda: [tt("sc%s%d" % (n, j), IND(A("tab"), A("off16", 16 * h + 2 * j, 16 * h + 2 * j + wide)),
                            A("hv", 128 * h + k * j, 128 * h + k * j + k), plus(k * j, k), ALU.add) for j in range(8 // wide)]
@@ -485,8 +512,8 @@ def build(T, topo, rank):
     def penalty(t):
         n = str(t)
         ts("kd" + n, A("kind"), A("pt32"), 16.0, ALU.is_ge)
-        mm("c1" + n, [(A("pq", 384, 400), A("one"), A("kind"), True, True)])
-        act("c2" + n, A("cnj"), A("pq", 384, 400), AF.Identity, bias=288.0, acc=A("cnt"))
+        mm("c1" + n, [(A("pd1", 384, 400), A("one"), A("kind"), True, True)])
+        act("c2" + n, A("cnj"), A("pd1", 384, 400), AF.Identity, bias=288.0, acc=A("cnt"))
         act("c3" + n, A("cnf"), A("cnt"), AF.Identity, bias=-0.484375, scale=1.0 / 32)
         act("c4" + n, A("pnf"), A("cnf"), AF.Identity, bias=A("cnt"), scale=-32.0)
         act("c6" + n, A("pend"), A("idn"), AF.Identity, scale=A("pnf"))
@@ -501,7 +528,7 @@ def build(T, topo, rank):
         act("o_h%d" % h, H("oh1"), IND(H("trp", 256), lst(LF2, 8)), AF.Abs, bias=-0.5, scale=2.0)
         act("o_m%d" % h, lanes("oh"), H("oh1"), AF.Identity, bias=12288.5, scale=-1.0)
         send("early", RO - 1, h)
-        recv("late", RO, h, part, "bz" + n)
+        recv("mid", RO, h, part, "bz" + n)
         recv("early", RO, h, part, "be" + n)
         a2 = alike(n, h, A("zout", 128 * s, 128 * s + 128), A("pz", 128 * (s + 2), 128 * (s + 3)), lst(LZ, 8))
         mm("as" + n, [(A("pa", 128, 256), A("blk8"), a2, True, True)])
@@ -618,6 +645,96 @@ def schedule(ops):
     return best
 
 
+def plan(T, topo):
+    ops = build(T, topo, 0)
+    n = len(ops)
+    idx = {o["name"]: i for i, o in enumerate(ops)}
+    pre = [dict(d) for d in hazards(ops)]
+    for i, o in enumerate(ops):
+        if o["after"]:
+            pre[i][idx[o["after"]]] = o["q"] is None
+    qs = [o["q"] for o in ops]
+    nets = []
+    for p in PACE:
+        os_ = build(T, topo, 0, p)
+        cost, lat = [max(o["cost"], 1e-4) for o in os_], [o["lat"] for o in os_]
+        before = [[(j, lat[j] + p["hop"] if w else 0.0) for j, w in pre[i].items()] for i in range(n)]
+        behind = [[] for _ in ops]
+        for i in range(n):
+            for j, gap in before[i]:
+                behind[j].append((i, gap))
+        nets.append((cost, lat, before, behind))
+
+    def place(net, key, back):
+        cost, lat, before, behind = net
+        if back:
+            before, behind = behind, before
+        left = [len(b) for b in before]
+        ready = list(lat) if back else [0.0] * n
+        start = [0.0] * n
+        free = {q: 0.0 for q in qs}
+        avail = {q: [i for i in range(n) if qs[i] == q and not left[i]] for q in free}
+        for _ in range(n):
+            st, q = 1e9, None
+            for q2, l in avail.items():
+                if l:
+                    t = max(free[q2], min([ready[i] for i in l]))
+                    if t < st:
+                        st, q = t, q2
+            i = min([i for i in avail[q] if ready[i] <= st], key=lambda i: key[i])
+            avail[q].remove(i)
+            start[i] = st
+            st += cost[i]
+            if q:
+                free[q] = st
+            for k, gap in behind[i]:
+                ready[k] = max(ready[k], st + gap)
+                left[k] -= 1
+                if not left[k]:
+                    avail[qs[k]].append(k)
+        return start
+
+    def times(start):
+        order = sorted(range(n), key=lambda i: (start[i], i))
+        out = []
+        for cost, lat, before, _ in nets:
+            end, free = [0.0] * n, {}
+            for i in order:
+                end[i] = free[qs[i]] = max([free.get(qs[i], 0.0) if qs[i] else 0.0] + [end[j] + gap for j, gap in before[i]]) + cost[i]
+            out.append(max(end[i] + lat[i] for i in range(n)))
+        return out
+
+    cost, lat, before, behind = nets[0]
+    way = [0.0] * n
+    left = [len(b) for b in behind]
+    todo = [i for i in range(n) if not left[i]]
+    for i in todo:
+        way[i] = cost[i] + max([lat[i]] + [way[k] + gap for k, gap in behind[i]])
+        for j, _ in before[i]:
+            left[j] -= 1
+            if not left[j]:
+                todo.append(j)
+    best = place(nets[0], [-x for x in way], False)
+    unit = times(best)
+    score = float(len(nets))
+    seed = [CFG["seed"]]
+
+    def draw():
+        seed[0] = (seed[0] * 1103515245 + 12345) % 2147483648
+        return seed[0] / 2147483648.0
+    for r in range(CFG["rounds"]):
+        net, size, mid, span = nets[r % len(nets)], draw() ** 2 * 2, draw() * max(best), 100.0 * draw() ** 2 + 3
+        key = [x + (size * (draw() - 0.5) if abs(x - mid) < span else 0.0) for x in best]
+        if r < 12 or draw() < 0.3:
+            back = place(net, [-x for x in key], True)
+            key = [-(back[i] + net[0][i]) for i in range(n)]
+        start = place(net, key, False)
+        new = sum(a / b for a, b in zip(times(start), unit))
+        if new <= score:
+            best, score = start, new
+    return {ops[i]["name"]: k for k, i in enumerate(sorted(range(n), key=lambda i: (best[i], i)))}, times(best)
+
+
 ORDER = {}
 
 
@@ -626,9 +743,7 @@ def rank_program(g, core, T, topo):
     if rank is None:
         return
     if not ORDER:
-        ops = build(T, topo, 0)
-        start = schedule(ops)[0]
-        ORDER.update({ops[i]["name"]: k for k, i in enumerate(sorted(range(len(ops)), key=lambda i: (start[i], i)))})
+        ORDER.update(plan(T, topo)[0])
     ops = build(T, topo, rank)
     deps = hazards(ops)
     queue = {"V": g.vector, "S": g.scalar, "P": g.tensor, "G": g, "Y": g.sync}

@@ -1,56 +1,68 @@
+import math
 from concourse.bass import DstId, RemoteDMATransfer
 from concourse.mybir import AluOpType as ALU, ActivationFunctionType as AF
 
 RO = 5
-SLOT = 144
-SPARE = 32
-CFG = dict(route=("CCAADCAA", "DDBDDDDB"), first=("CCAADCAA", "DDBDDDDB"), last=("CCAADCAA", "DDBDDDDB"),
-           dup="VL", cs0="VS", merge="--------", zq="VV", passes=6, xs="SS", cs="VS", wide="12", x2="VS", xe="P", gdma=1.0, acc=0.8,
+SLOT = 208
+SPARE = 16384
+PARTS = 2
+SHIFTS = 16 // PARTS
+WORLD = 32 + 2 * PARTS
+KEYS = 8 * WORLD
+
+
+def units(routes):
+    return tuple((r, c, 4) for r, c in zip(routes, (0, 4, 16, 20, 8, 12, 24, 28)))
+
+
+CALLS = (units("CCAADCAA"), units("DDADDDDB"))
+CFG = dict(calls=CALLS, first=CALLS, last=CALLS, cs0="VS", cs="HR", x2="VS", wide="12",
            cyc=0.95e-3, gat=1.56, sca=3.8, pec=0.5e-3, hop=0.18, call=0.5, remote=2.6, local=2.0, table=3.2)
-CFG.update(seed=3, rounds=1300)
+CFG.update(seed=4, rounds=30, swaps=30000, heat=0.002, far=6, free=0.2, copy=500, all=0.8)
 PACE = [dict(cyc=0.83e-3, pec=0.44e-3, hop=0.2, gat=1.56, sca=3.8, remote=2.3, local=1.9),
         dict(cyc=1.15e-3, pec=0.6e-3, hop=0.2, gat=1.95, sca=5.0, remote=3.0, local=2.3),
         dict(cyc=0.87e-3, pec=0.46e-3, hop=0.17, gat=1.2, sca=2.5, remote=3.2, local=2.6),
-        dict(cyc=1.0e-3, pec=0.53e-3, hop=0.23, gat=1.5, sca=4.0, remote=2.7, local=2.1)]
+        dict(cyc=0.9e-3, pec=0.5e-3, hop=0.25, gat=1.3, sca=3.0, remote=4.0, local=3.2),
+        dict(cyc=1.0e-3, pec=0.6e-3, hop=0.3, gat=1.1, sca=2.0, remote=3.4, local=2.4)]
 
 SCRATCH = {
-    "tab": ("sbuf", [128, 4096 + SPARE], "bfloat16"), "nxb": ("sbuf", [128, 4096 + SPARE], "bfloat16"),
+    "tab": ("sbuf", [128, 4096 + SPARE], "bfloat16"), "nxb": ("sbuf", [128, 4096], "int32"),
     "gb": ("sbuf", [128, 8192], "bfloat16"), "ab": ("sbuf", [128, 8192], "bfloat16"),
+    "idw": ("sbuf", [128, 128], "bfloat16"), "idk": ("sbuf", [128, 128], "bfloat16"),
     "msg": ("sbuf", [128, SLOT * 10], "float32"), "pmsg": ("sbuf", [128, 120 * 10], "float32"),
-    "nz": ("sbuf", [128, 5120], "bfloat16"), "crp": ("sbuf", [128, 128], "float32"),
-    "zin": ("sbuf", [128, 1280], "bfloat16"), "zout": ("sbuf", [128, 1280], "bfloat16"),
+    "crp": ("sbuf", [128, 128], "float32"),
+    "zin": ("sbuf", [128, 5120], "bfloat16"), "zout": ("sbuf", [128, 1280], "bfloat16"),
     "pz": ("sbuf", [128, 1536], "bfloat16"), "zb": ("sbuf", [128, 1280], "bfloat16"),
     "t32": ("sbuf", [128, 512], "int32"), "o32": ("sbuf", [128, 512], "int32"), "o16": ("sbuf", [128, 512], "uint16"),
-    "kf": ("sbuf", [128, 512], "float32"), "ki": ("sbuf", [128, 16], "int32"), "pt32": ("sbuf", [128, 16], "int32"),
+    "kf": ("sbuf", [128, 2 * KEYS], "float32"), "quad": ("sbuf", [128, 8], "float32"), "cs": ("sbuf", [128, 128], "float32"), "id8": ("sbuf", [128, 128], "float16"),
     "pt16": ("sbuf", [128, 32], "uint16"), "q16": ("sbuf", [128, 16], "uint16"),
-    "bx": ("sbuf", [128, 256], "bfloat16"), "off16": ("sbuf", [128, 32], "uint16"), "kind": ("sbuf", [128, 16], "bfloat16"),
+    "bx": ("sbuf", [128, 288], "bfloat16"), "off16": ("sbuf", [128, 514], "uint16"),
+    "dim": ("sbuf", [128, 128], "float32"), "cq": ("sbuf", [128, 128], "float16"), "kind": ("sbuf", [128, 72], "bfloat16"),
     "xx": ("sbuf", [128, 256], "float32"), "ff": ("sbuf", [128, 256], "float32"), "ne": ("sbuf", [128, 256], "float32"),
-    "rr": ("sbuf", [128, 256], "float32"), "x2": ("sbuf", [128, 256], "float32"), "f2": ("sbuf", [128, 256], "float32"),
+    "x2": ("sbuf", [128, 256], "float32"), "f2": ("sbuf", [128, 256], "float32"),
     "xe": ("sbuf", [128, 256], "float32"), "fe": ("sbuf", [128, 256], "float32"), "nf": ("sbuf", [128, 256], "float32"),
-    "rf": ("sbuf", [128, 256], "float32"), "g2": ("sbuf", [128, 256], "float32"),
+    "g2": ("sbuf", [128, 256], "float32"),
     "gq": ("sbuf", [128, 256], "bfloat16"), "hv": ("sbuf", [128, 256], "bfloat16"),
-    "nxg": ("sbuf", [128, 256], "bfloat16"), "al1": ("sbuf", [128, 256], "bfloat16"), "al2": ("sbuf", [128, 256], "bfloat16"),
-    "alk": ("sbuf", [128, 16], "float32"), "dif": ("sbuf", [128, 128], "float32"), "tmp": ("sbuf", [128, 128], "float32"),
-    "cnj": ("sbuf", [128, 16], "float32"), "cnt": ("sbuf", [128, 1], "float32"), "cnf": ("sbuf", [128, 1], "bfloat16"),
-    "pnf": ("sbuf", [128, 1], "float32"), "pend": ("sbuf", [128, 128], "bfloat16"),
+    "nxg": ("sbuf", [128, 256], "float16"), "wh": ("sbuf", [128, 144], "float16"), "al1": ("sbuf", [128, 256], "bfloat16"), "al2": ("sbuf", [128, 256], "bfloat16"),
+    "alk": ("sbuf", [128, 16], "float32"), "dif": ("sbuf", [128, 128], "float32"),
+    "cnj": ("sbuf", [128, 72], "float32"), "cnt": ("sbuf", [128, 1], "float32"), "cnf": ("sbuf", [128, 8], "bfloat16"),
     "pi": ("sbuf", [128, 1], "int32"), "pb": ("sbuf", [128, 8], "int32"), "pc": ("sbuf", [128, 16], "float32"),
     "ci": ("sbuf", [128, 144], "float32"), "c16": ("sbuf", [128, 128], "float32"), "cg": ("sbuf", [128, 128], "float32"),
     "cg8": ("sbuf", [128, 128], "float32"), "c32": ("sbuf", [128, 128], "float32"),
     "lio": ("sbuf", [128, 80], "float32"), "lst": ("sbuf", [128, 96], "uint16"),
     "idn": ("sbuf", [128, 128], "bfloat16"), "nid": ("sbuf", [128, 128], "bfloat16"), "wd": ("sbuf", [128, 144], "bfloat16"),
-    "idf": ("sbuf", [128, 128], "float32"), "nif": ("sbuf", [128, 128], "float32"), "bn": ("sbuf", [128, 128], "bfloat16"),
-    "s8": ("sbuf", [128, 8], "bfloat16"), "ns8": ("sbuf", [128, 8], "bfloat16"), "sj": ("sbuf", [128, 16], "bfloat16"),
-    "cj": ("sbuf", [128, 16], "bfloat16"), "anew": ("sbuf", [128, 256], "float32"), "rev": ("sbuf", [128, 256], "bfloat16"),
+    "idf": ("sbuf", [128, 128], "float32"), "nif": ("sbuf", [128, 128], "float32"),
+    "s8": ("sbuf", [128, 8], "bfloat16"), "ns8": ("sbuf", [128, 8], "bfloat16"), "sj": ("sbuf", [128, 256], "bfloat16"),
+    "cj": ("sbuf", [128, 32], "bfloat16"), "anew": ("sbuf", [128, KEYS], "float32"), "tiny": ("sbuf", [128, 8], "float32"),
     "blk8": ("sbuf", [128, 128], "bfloat16"), "die": ("sbuf", [128, 128], "float32"), "rse": ("sbuf", [128, 128], "float32"),
     "blk": ("sbuf", [128, 128], "float32"), "dia": ("sbuf", [128, 128], "float32"), "rst": ("sbuf", [128, 128], "float32"),
-    "b1": ("sbuf", [128, 256], "bfloat16"), "b2": ("sbuf", [128, 256], "bfloat16"),
+    "b1": ("sbuf", [128, KEYS], "bfloat16"), "b2": ("sbuf", [128, KEYS], "bfloat16"),
     "one": ("sbuf", [128, 128], "bfloat16"), "m160": ("sbuf", [128, 32], "bfloat16"),
     "inb": ("sbuf", [128, 272], "int32"), "sb": ("sbuf", [128, 256], "int32"), "sg": ("sbuf", [128, 256], "float32"),
     "yf": ("sbuf", [128, 272], "float32"), "dup": ("sbuf", [128, 544], "float32"),
     "trp": ("sbuf", [128, 544], "float32"), "ztb": ("sbuf", [128, 256], "bfloat16"),
-    "nxi": ("sbuf", [128, 256], "int32"), "nxj": ("sbuf", [128, 512], "int32"), "nxh": ("sbuf", [128, 512], "bfloat16"),
     "oh1": ("sbuf", [128, 256], "float32"), "oh": ("sbuf", [128, 256], "float32"), "ph": ("sbuf", [128, 256], "float32"),
-    "keep": ("sbuf", [128, 256], "float32"), "ohs": ("sbuf", [128, 256], "float32"), "nxr": ("sbuf", [128, 256], "bfloat16"),
+    "keep": ("sbuf", [128, 256], "float32"), "ohs": ("sbuf", [128, 256], "float32"), "nxr": ("sbuf", [128, 256], "float32"),
     "oc": ("sbuf", [128, 256], "float32"), "oz": ("sbuf", [128, 256], "bfloat16"),
     "key0": ("psum", [128, 512], "float32"), "key1": ("psum", [128, 512], "float32"),
     "pd0": ("psum", [128, 512], "float32"), "pd1": ("psum", [128, 512], "float32"),
@@ -58,11 +70,10 @@ SCRATCH = {
     "pa": ("psum", [128, 512], "float32"), "pn": ("psum", [128, 512], "float32"),
 }
 STORES = ["st_x", "st_h0", "st_h1", "st_z", "st_c"]
-SEMAPHORES = (["cV", "cS", "cP", "cG", "sent", "ld_m", "ld_c", "ld_z", "ld_t", "ld_nx", "nx_b"] + STORES
-              + ["%s%d%d" % (k, t, h) for k in ("az", "ac", "ae", "bz", "be", "du") for t in range(1, RO + 1) for h in range(2)]
-              + ["fa%d%d" % (h, u) for h in range(2) for u in range(8)])
+SEMAPHORES = (["cV", "cS", "cP", "cG", "sent", "ld_m", "ld_c", "ld_z", "ld_t", "ld_nx"] + STORES
+              + ["%s%d%d" % (k, t, h) for k in ("az", "ac", "ae", "bz", "be", "du") for t in range(RO + 1) for h in range(2)])
 
-L1, L2, LZ, LF1, LF2, LJ, LG = 0, 18, 38, 46, 62, 70, 74
+L1, L2, LZ, LF1, LF2, LJ = 0, 18, 38, 46, 62, 70
 
 
 def A(name, lo=0, hi=None, step=1):
@@ -83,14 +94,17 @@ def deal(n, total):
 
 
 def build(T, topo, rank, pace=CFG):
-    ops = []
+    ops, visits = [], []
     CYC, GAT, SCA, PEC, REMOTE, LOCAL = [pace[k] for k in ("cyc", "gat", "sca", "pec", "remote", "local")]
     N = len(T.cores)
     me = T.cores[rank]
-    BASE = float(SPARE - 16384)
+    BASE = -float(SPARE)
+
+    def calls(t, h):
+        return CFG["first" if t == 0 else "last" if t == RO - 1 else "calls"][h]
 
     def routes(t, h):
-        return CFG["first" if t == 0 else "last" if t == RO - 1 else "route"][h]
+        return set(c[0] for c in calls(t, h))
 
     def ap(a):
         if not isinstance(a, tuple):
@@ -110,7 +124,7 @@ def build(T, topo, rank, pace=CFG):
         return 16 * width(a[2]) if a[0] == "*" else len(range(a[1], a[2], a[3]))
 
     def two(a):
-        return SCRATCH[a[0]][2] in ("bfloat16", "uint16")
+        return SCRATCH[a[0]][2] in ("bfloat16", "uint16", "float16")
 
     def add(q, name, fn, rd, wr, cost, lat=0.0, sem=None, val=0, after=None):
         r = regs(rd)
@@ -120,7 +134,9 @@ def build(T, topo, rank, pace=CFG):
                 w.append(a[1]); r.append(a[2])
             else:
                 w.append(a)
-        ops.append(dict(q=q, name=name, fn=fn, rd=r, wr=w, cost=cost, lat=lat, sem=sem, val=val, after=after))
+        k = min(i for i in range(2, len(name) + 1) if name[i:i + 1] in "0123456789")
+        role = (name[:k] + name[k + 1:], int(name[k])) if visits else None
+        ops.append(dict(q=q, name=name, fn=fn, rd=r, wr=w, cost=cost, lat=lat, sem=sem, val=val, after=after, role=role))
 
     def vcost(out, ins, both=False):
         if out[0] == "*":
@@ -165,6 +181,12 @@ def build(T, topo, rank, pace=CFG):
             kw["accum_out"] = ap(acc)
         add("S", name, lambda g: [g.scalar.activation(ap(out), ap(a), func, **kw)], [a, bias, scale], [out] + ([acc] if acc else []), c)
 
+    def shift(eng, name, out, a, by):
+        if eng == "V":
+            ts(name, out, a, by, ALU.add)
+        else:
+            act(name, out, a, AF.Identity, bias=by)
+
     def mm(name, items, grp=None):
         c = sum(max(64, width(i[2])) * (1 if two(i[2]) else 4) for i in items) * PEC
         add("P", name, lambda g, close=False: [g.tensor.matmul(ap(o), ap(l), ap(r), s, e or (close and k == len(items) - 1))
@@ -183,8 +205,14 @@ def build(T, topo, rank, pace=CFG):
         eng = (lambda g: g.sync) if q == "Y" else (lambda g: g.scalar)
         add(q, name, lambda g: [eng(g).dma_start(o, a) for o, a in pairs], rd, wr, 0.06 * len(pairs), lat=lat, sem=name, val=16 * len(pairs), after=after)
 
-    def sel16(name, out, src):
-        mm(name, [(out, A("wd", 15 - p, 143 - p), A(src[0], src[1] + p, src[2], 16), p == 0, p == 15) for p in range(16)])
+    def sel16(name, out, src, w="wd"):
+        mm(name, [(out, A(w, 15 - p, 143 - p), A(src[0], src[1] + p, src[2], 16), p == 0, p == 15) for p in range(16)])
+
+    def msg(s, lo, hi):
+        return A("msg", SLOT * s + 64 + lo, SLOT * s + 64 + hi)
+
+    def zin(s, k=1):
+        return A("zin", 512 * s, 512 * s + 128 * k)
 
     def mail(r, kind, t, h):
         s, s1, n1 = 2 * t + h, 2 * t + h + 2, "%d%d" % (t + 1, h)
@@ -197,14 +225,15 @@ def build(T, topo, rank, pace=CFG):
             else:
                 out.append((A("oh", 128 - 128 * h, 256 - 128 * h), r ^ 1, A("ph", 128 - 128 * h, 256 - 128 * h), "be" + n1))
         elif kind == "late":
-            out.append((A("msg", SLOT * s, SLOT * s + 16), nxt, A("msg", SLOT * s1 + 8, SLOT * s1 + 24), "ac" + n1))
+            k = -64 if CFG["cs"][h] == "R" else 0
+            out.append((msg(s, k, 16), nxt, msg(s1, k + 8, 24), "ac" + n1))
         elif kind == "mid":
-            out.append((zo, nxt, A("zin", 128 * s1, 128 * s1 + 128), "az" + n1))
+            out.append((zo, nxt, zin(s1), "az" + n1))
             if other != r:
                 out.append((zo, other, A("pz", 128 * s1, 128 * s1 + 128), "bz" + n1))
         else:
-            src = A("msg", SLOT * s + 16, SLOT * s + 136)
-            out.append((src, nxt, A("msg", SLOT * s1 + 24, SLOT * s1 + SLOT), "ae" + n1))
+            src = msg(s, 16, 136)
+            out.append((src, nxt, msg(s1, 24, 144), "ae" + n1))
             if other != r:
                 out.append((src, other, A("pmsg", 120 * s1, 120 * s1 + 120), "be" + n1))
         k = deal(len(out), len(topo.engines(T.cores[r], T.cores[out[0][1]])))
@@ -239,31 +268,30 @@ def build(T, topo, rank, pace=CFG):
     def pc(i):
         return A("pc", i, i + 1)
 
-    dma("Y", "ld_m", [(T.inb[:, 0:256], T.mem[:])], [], [A("inb", 0, 256)], LOCAL)
+    dma("Y", "ld_m", [(T.inb[:, 0:256], T.mem[:])], [], [A("inb", 0, 256)], LOCAL + 0.2)
     dma("S", "ld_c", [(T.inb[:, 256:272], T.plc[:])], [], [A("inb", 256, 272)], LOCAL)
-    dma("S", "ld_z", [(T.ztb[:], T.zt[:])], [], [A("ztb")], LOCAL)
-    dma("S", "ld_nx", [(T.nxi[:], T.nxt[:])], [], [A("nxi")], LOCAL + 0.4, after="ld_z")
-    dma("Y", "ld_t", [(T.tab[:, SPARE:], T.xt[:])], [], [A("tab", SPARE)], LOCAL + CFG["table"] + 0.4, after="ld_m")
+    dma("Y", "ld_z", [(T.ztb[:], T.zt[:])], [], [A("ztb")], LOCAL + 0.3, after="ld_m")
+    dma("Y", "ld_t", [(T.tab[:, SPARE:], T.xt[:])], [], [A("tab", SPARE)], LOCAL + CFG["table"] + 0.3, after="ld_z")
 
     iota("i_p", A("pi"), [[0, 1]], 0, 1)
     iota("i_l1c", A("lio", L1, L1 + 2), [[0, 2]], 143)
     iota("i_l1", A("lio", L1 + 2, L1 + 18), [[-16, 8], [0, 2]], 127)
     iota("i_l2", A("lio", L2, L2 + 20), [[256, 2], [2, 10]], 30)
     iota("i_ci", A("ci"), [[1, 144]], 0)
-    iota("i_b2", A("b2"), [[0, 8], [1, 32]], 0)
-    iota("i_b1", A("b1"), [[0, 16], [128, 16]], 0)
+    iota("i_b2", A("b2"), [[0, 8], [2, WORLD]], -31)
+    iota("i_cs", A("cs", 0, 8 * SHIFTS), [[16, 8], [1, SHIFTS]], 0)
     iota("i_c16", A("c16"), [[0, 8], [1, 16]], 0)
     iota("i_cg", A("cg"), [[16, 8], [0, 16]], 0)
     iota("i_c32", A("c32"), [[0, 4], [1, 32]], 0)
     for i in range(4):
-        iota("i_nx%d" % i, A("nxb", 1032 * i, 1032 * i + 1032), [[0, 1032]], 0, after="i_cg")
-    iota("i_rev", A("rev"), [[0, 8], [32, 2], [0, 16]], 0)
+        iota("i_nx%d" % i, A("nxb", 1024 * i, 1024 * i + 1024), [[0, 1024]], 0, after="i_cg")
     iota("i_lf1", A("lio", LF1, LF1 + 16), [[1, 8], [0, 2]], 0)
     iota("i_lf2", A("lio", LF2, LF2 + 8), [[-32, 8]], 239)
     iota("i_cg8", A("cg8"), [[16, 8], [-1000, 2], [0, 8]], 1000)
-    for i, m in enumerate((7, 8, 16, 15, 112, 127)):
-        ts("p%d" % i, A("pb", i, i + 1), A("pi"), m, ALU.bitwise_and)
+    for i, m in enumerate((7, 8, 16, 15, 112, 127, SHIFTS - 1, 16 - SHIFTS)):
+        ts("p%d" % (i + 14 * (i > 5)), A("pb", i, i + 1), A("pi"), m, ALU.bitwise_and)
     cp("pc", A("pc", 0, 6), A("pb", 0, 6))
+    cp("pd", A("pc", 12, 14), A("pb", 6, 8))
     ts("l1", lst(L1, 18), A("lio", L1, L1 + 18), pc(3), ALU.subtract)
     ts("lz", lst(LZ, 8), A("lio", L1 + 2, L1 + 18, 2), pc(3), ALU.subtract)
     ts("p6", pc(6), pc(0), 32.0, ALU.mult, pc(2), ALU.add)
@@ -272,41 +300,54 @@ def build(T, topo, rank, pace=CFG):
         ts("l2%d" % h, lst(L2 + 10 * h + 1, 9), A("lio", L2 + 10 * h + 1, L2 + 10 * h + 10), pc(7), ALU.add)
         ts("lc%d" % h, lst(L2 + 10 * h, 1), pc(2), pc(0), ALU.subtract, 15.0 - 8 * h, ALU.add)
     ts("lj", lst(LJ, 4), A("lio", L1 + 2, L1 + 6), 0.0, ALU.mult, pc(0), ALU.add)
-    cp("lg", lst(LG, 8), A("ci", 0, 8))
-    cp("cj", A("cj", 0, 8), A("ci", 0, 8))
+    ts("cj", A("cj", 0, 8), A("ci", 0, 8), 124.0, ALU.add)
     ts("cjp", A("cj", 8, 16), A("ci", 0, 128, 16), pc(3), ALU.add)
+    ts("cjq", A("cj", 16, 32), A("ci", 0, 16), 8.0, ALU.is_ge, 1984.0, ALU.mult)
     ts("idn", A("idn"), A("ci", 0, 128), pc(5), ALU.is_equal)
     act("nid", A("nid"), A("idn"), AF.Identity, scale=-1.0)
     ts("p8", pc(8), pc(4), 15.0, ALU.add)
     ts("wd", A("wd"), A("ci"), pc(8), ALU.is_equal, 256.0, ALU.mult)
-    for name, out, v in (("s8", A("s8"), 32.0), ("ns8", A("ns8"), -32.0), ("sj", A("sj", 0, 8), 8.0), ("sjp", A("sj", 8, 16), 128.0)):
-        ts(name, out, A("ci", 0, 128, 16), pc(4), ALU.is_equal, v, ALU.mult)
-    ts("anew", A("anew"), A("b2"), 0.0, ALU.is_equal, 1.0e6, ALU.mult)
+    ts("s8", A("s8"), A("ci", 0, 128, 16), pc(4), ALU.is_equal, 64.0, ALU.mult)
+    act("ns8", A("ns8"), A("s8"), AF.Identity, scale=-1.0)
+    ts("pa", pc(11), pc(12), pc(4), ALU.add)
+    ts("sj0", A("sj", 0, 8 * SHIFTS), A("cs", 0, 8 * SHIFTS), pc(11), ALU.is_equal, 4.0, ALU.mult)
+    act("sj1", A("sj", 8 * SHIFTS, 16 * SHIFTS), A("sj", 0, 8 * SHIFTS), AF.Identity, scale=16.0)
+    for i in range(2):
+        ts("ps%d" % i, A("quad", 4 * i, 4 * i + PARTS), A("ci", 0, 16, SHIFTS), pc(13), ALU.is_equal, (3.0 - 6 * i) * 2 ** 28, ALU.mult)
+    fill("one", A("one"), 1.0)
+    act("anew", A("anew"), A("b2"), AF.Relu, scale=-1.0e6, bias=-30.0e6)
+    for r in range(PARTS):
+        for i in range(2):
+            act("up%d%d" % (r, i), A("anew", 32 + 2 * r + i, KEYS, WORLD), A("one", 0, 8), AF.Identity, scale=A("quad", 4 * i + r, 4 * i + r + 1))
+    act("b1", A("b1"), A("b2"), AF.Sign)
+    act("idk", A("idk"), A("idn"), AF.Identity, scale=129.0)
+    act("idw", A("idw"), A("idn"), AF.Identity, scale=-2048.0)
+    fill("bx", A("bx"), 0.0)
     ts("blk", A("blk"), A("cg"), pc(4), ALU.is_equal)
-    act("bn", A("bn"), A("blk"), AF.Copy)
+    act("wh", A("wh"), A("wd"), AF.Identity, scale=1.0 / 256)
     ts("blk8", A("blk8"), A("cg8"), pc(4), ALU.is_equal)
     ts("dia", A("dia"), A("c16"), pc(3), ALU.is_equal)
     act("rst", A("rst"), A("dia"), AF.Identity, scale=-1.0, bias=1.0)
-    if "2" in CFG["wide"]:
-        ts("die", A("die"), A("c32"), pc(3), ALU.is_equal)
-        act("rse", A("rse"), A("die"), AF.Identity, scale=-1.0, bias=1.0)
-        ts("p10", pc(10), pc(3), 16.0, ALU.add)
-        if CFG["xe"] != "V":
-            act("diep", A("pq", 256, 384), A("die"), AF.Copy)
-    if CFG["x2"] != "VV":
-        act("diap", A("pq", 128, 256), A("dia"), AF.Copy)
-    if set(CFG["xs"] + CFG["cs"]) != {"V"}:
-        act("idf", A("idf"), A("idn"), AF.Copy)
-    if set(CFG["xs"]) != {"V"}:
-        act("nif", A("nif"), A("nid"), AF.Copy)
-    fill("spare", A("tab", 0, SPARE), 0.0)
-    fill("one", A("one"), 1.0)
+    ts("die", A("die"), A("c32"), pc(3), ALU.is_equal)
+    act("rse", A("rse"), A("die"), AF.Identity, scale=-1.0, bias=1.0)
+    ts("p10", pc(10), pc(3), 16.0, ALU.add)
+    act("diep", A("pq", 256, 384), A("die"), AF.Identity, scale=32768.0, bias=pc(3))
+    act("dim", A("dim"), A("dia"), AF.Identity, scale=32768.0, bias=pc(10))
+    act("cq", A("cq"), A("c16"), AF.Identity, bias=-360.0)
+    act("id8", A("id8"), A("idn"), AF.Copy)
+    fill("b0a", A("b1", 32, KEYS, WORLD), -2.0 ** 20)
+    for i in range(1, 2 * PARTS):
+        act("b0%d" % i, A("b1", 32 + i, KEYS, WORLD), A("b1", 32, KEYS, WORLD), AF.Copy)
+    act("diap", A("pq", 128, 256), A("dia"), AF.Copy)
+    act("idf", A("idf"), A("idn"), AF.Copy)
+    act("nif", A("nif"), A("nid"), AF.Copy)
     fill("m160", A("m160"), -160.0)
+    fill("tiny", A("tiny"), -1.0 / 2048)
     ts("p9", pc(9), pc(3), 8.0, ALU.mult)
     ts("lf1", lst(LF1, 16), A("lio", LF1, LF1 + 16), pc(9), ALU.add)
     ts("lf2", lst(LF2, 8), A("lio", LF2, LF2 + 8), pc(2), ALU.add, pc(3), ALU.subtract)
 
-    ts("y_c", A("yf", 128, 144), A("inb", 256, 272), 28672.0, ALU.add, 2.0, ALU.mult)
+    act("y_c", A("yf", 128, 144), A("inb", 256, 272), AF.Identity, scale=2.0, bias=2 * 28672.0)
     for h in range(2):
         lanes = lambda b: A(b, 128 - 128 * h, 256 - 128 * h)
         d0, d1 = (0, 288) if h == 0 else (288, 544)
@@ -315,12 +356,9 @@ def build(T, topo, rank, pace=CFG):
         tt("y_m%d" % h, A("yf", 144 * h, 144 * h + 128), lanes("sg"), lanes("inb"), ALU.subtract)
         act("y_d%d" % h, A("dup", d0, d1), IND(A("yf", 144 * h, 144 + 128 * h), lst(L1 + 2 * h, 18 - 2 * h)), AF.Abs, scale=0.5)
         turn("y_t%d" % h, A("trp", d0, d1), A("dup", d0, d1))
-        act("y_l%d" % h, A("msg", SLOT * h, SLOT * h + SLOT), IND(A("trp", 0, d1), lst(L2 + 10 * h, 9)), AF.Identity, bias=-6144.0)
-        act("z_l%d" % h, A("zin", 128 * h, 128 * h + 128), IND(lanes("ztb"), lst(LZ, 8)), AF.Copy)
-    ts("nx1", A("nxj", 0, 256), A("nxi"), 4032, ALU.bitwise_and)
-    ts("nx2", A("nxj", 256, 512), A("nxi"), 63, ALU.bitwise_and)
-    cp("nx3", A("nxh"), A("nxj"))
-    dma("Y", "nx_b", [(T.nxb[i:128:16, SPARE:], T.nxh[:, 256 * i:256 * i + 256]) for i in range(2)], [A("nxh")], [A("nxb")], LOCAL + 0.5)
+        act("y_l%d" % h, msg(h, 0, 144), IND(A("trp", 0, d1), lst(L2 + 10 * h, 9)), AF.Identity, bias=-6144.0)
+        act("z_l%d" % h, zin(h), IND(lanes("ztb"), lst(LZ, 8)), AF.Copy)
+    dma("Y", "ld_nx", [(T.nxb[0:128:16, :], T.nxt[:])], [], [A("nxb")], LOCAL + 0.5, after="ld_t")
 
     prev, part = (rank - 1) % N, rank ^ 1
 
@@ -333,60 +371,44 @@ def build(T, topo, rank, pace=CFG):
 
     def exchange(t, h):
         n, s, src = "%d%d" % (t, h), 2 * t + h, prev ^ 1
-        own = A("msg", SLOT * s + 80, SLOT * s + SLOT)
+        own = msg(s, 80, 144)
         if src == rank:
-            zp, yp = A("zout", 128 * (s - 2), 128 * (s - 1)), A("msg", SLOT * (s - 2) + 72, SLOT * (s - 2) + 136)
+            zp, yp = A("zout", 128 * (s - 2), 128 * (s - 1)), msg(s - 2, 72, 136)
         else:
             zp, yp = A("pz", 128 * s, 128 * s + 128), A("pmsg", 120 * s + 56, 120 * s + 120)
             recv("mid", t, h, src, "bz" + n)
             recv("early", t, h, src, "be" + n)
         H = lambda b, k=128: A(b, k * h, k * h + k)
-        sel16("as" + n, A("pa", 128, 136), alike(n, h, A("zin", 128 * s, 128 * s + 128), zp))
-        if CFG["xs"][h] == "V":
-            ts("ak" + n, H("alk", 8), A("pa", 128, 136), 256.0, ALU.is_ge)
-            tt("df" + n, H("dif", 64), yp, own, ALU.subtract)
-            tt("dm" + n, H("tmp", 64), IND(H("alk", 8), lst(LJ, 4)), H("dif", 64), ALU.mult)
-            tt("sw" + n, own, own, H("tmp", 64), ALU.add)
-        else:
-            act("ak" + n, H("alk", 8), A("pa", 128, 136), AF.Sign, bias=-128.0)
-            act("ar" + n, H("dif", 64), IND(H("alk", 8), lst(LJ, 4)), AF.Relu)
-            mm("df" + n, [(A("ps", 64, 128), A("idf"), yp, True, False), (A("ps", 64, 128), A("nif"), own, False, True)])
-            tt("dm" + n, A("ps", 128, 192), A("ps", 64, 128), H("dif", 64), ALU.mult)
-            tt("sw" + n, own, A("ps", 128, 192), own, ALU.add)
-
-    def from_table(t, h):
-        return "C" in routes(t, h)
+        sel16("as" + n, A("pa", 128, 136), alike(n, h, zin(s), zp))
+        act("ak" + n, H("alk", 8), A("pa", 128, 136), AF.Sign, bias=-128.0)
+        act("ar" + n, H("dif", 64), IND(H("alk", 8), lst(LJ, 4)), AF.Relu)
+        mm("df" + n, [(A("ps", 64, 128), A("idf"), yp, True, False), (A("ps", 64, 128), A("nif"), own, False, True)])
+        tt("dm" + n, A("ps", 128, 192), A("ps", 64, 128), H("dif", 64), ALU.mult)
+        tt("sw" + n, own, A("ps", 128, 192), own, ALU.add)
 
     def prep(t, h):
         n, s = "%d%d" % (t, h), 2 * t + h
-        m0, z0 = SLOT * s, 512 * s
-        z1 = A("zin", 128 * s, 128 * s + 128)
+        m0, z0 = SLOT * s + 64, 512 * s
         if t > 0:
             recv("mid", t, h, prev, "az" + n)
             recv("late", t, h, prev, "ac" + n)
             recv("early", t, h, prev, "ae" + n)
-        for name, use, out, scale, bias in (("nz", set(routes(t, h)) & set("ABF"), A("nz", z0, z0 + 128), -1.0, 0.0),
-                                            ("zb", set(routes(t, h)) & set("DE") or not from_table(t, h), A("zb", 128 * s, 128 * s + 128), 1.0, 192.0)):
-            if use and CFG["zq"][h] == "V":
-                ts(name + n, out, z1, scale, ALU.mult, bias, ALU.add)
-            elif use:
-                act(name + n, out, z1, AF.Identity, scale=scale, bias=bias)
-        if set(routes(t, h)) & set("ABF"):
-            if t and CFG["dup"][h] == "L":
-                dma("Y", "du" + n, [(T.nz[:, z0 + 128 * r:z0 + 128 * r + 128], T.nz[:, z0:z0 + 128]) for r in (1, 2, 3)],
-                    [A("nz", z0, z0 + 128)], [A("nz", z0 + 128, z0 + 512)], LOCAL + 0.4)
-            else:
-                for i in range(2):
-                    if t and CFG["dup"][h] == "S":
-                        act("d%d%s" % (i + 1, n), A("nz", z0 + (128 << i), z0 + (256 << i)), A("nz", z0, z0 + (128 << i)), AF.Copy)
-                    else:
-                        cp("d%d%s" % (i + 1, n), A("nz", z0 + (128 << i), z0 + (256 << i)), A("nz", z0, z0 + (128 << i)))
+        shift("V" if t else "S", "zb" + n, A("zb", 128 * s, 128 * s + 128), zin(s), 192.0)
+        if t:
+            dma("Y", "du" + n, [(T.zin[:, z0 + 128 * r:z0 + 128 * r + 128], T.zin[:, z0:z0 + 128]) for r in range(1, 4)],
+                [zin(s)], [A("zin", z0 + 128, z0 + 512)], LOCAL + 0.4)
+        else:
+            for i in range(2):
+                act("d%d%s" % (i + 1, n), A("zin", z0 + (128 << i), z0 + (256 << i)), A("zin", z0, z0 + (128 << i)), AF.Copy)
         c = IND(A("msg", m0 + 8, m0 + 16), lst(LJ, 4))
-        if CFG["cs" if t else "cs0"][h] != "V":
-            act("cr" + n, A("crp", 64 * h, 64 * h + 64), c, AF.Copy)
-            mm("cp" + n, [(A("ps", 0, 64), A("idf"), A("crp", 64 * h, 64 * h + 64), True, True)])
-            c = A("ps", 0, 64)
         for b in range(2):
+            if CFG["cs" if t else "cs0"][h] == "SH"[b]:
+                act("cr" + n, A("crp", 64 * h, 64 * h + 64), c, AF.Copy)
+                mm("cp" + n, [(A("ps", 0, 64), A("idf"), A("crp", 64 * h, 64 * h + 64), True, True)])
+                c = A("ps", 0, 64)
+            if t and CFG["cs"][h] == "R" and not b:
+                mm("cp" + n, [(A("ps", 0, 64), A("idf"), msg(s, -56, 8), True, True)])
+                c = A("ps", 0, 64)
             if b and t > 0:
                 exchange(t, h)
             if b and t + 1 < RO:
@@ -398,132 +420,121 @@ def build(T, topo, rank, pace=CFG):
                 ts("to" + nb, A("o32", o, o + 64), A("t32", o, o + 64), 16384 | 4095, ALU.bitwise_and)
                 ts("tu" + nb, A("o16", o, o + 64), A("o32", o, o + 64), BASE, ALU.add)
 
-    nr2, uses = [0], {}
+    nr2 = [0]
 
     def main(t, h):
-        n, s = "%d%d" % (t, h), 2 * t + h
-        z1, z4, zb = A("zin", 128 * s, 128 * s + 128), A("nz", 512 * s, 512 * s + 512), A("zb", 128 * s, 128 * s + 128)
-        key = "key%d" % h
-        mm("kb" + n, [(A(key, 0, 256), A("idn"), A("b2"), True, False), (A(key, 0, 256), A("idn"), A("b1"), False, False)])
-        for w in range(4):
-            base = 128 * (w % 2) + 64 * (w // 2)
-            r2 = routes(t, h)[2 * w:2 * w + 2]
-            G = lambda b, u, k=1: A(b, 4096 * h + 16 * base + 512 * u, 4096 * h + 16 * base + 512 * (u + k))
-            gath = lambda u, k=1: IND(A("tab"), A("o16", 256 * h + base + 32 * u, 256 * h + base + 32 * (u + k)))
-            both = CFG["merge"][4 * h + w] == "m" and r2 in ("CC", "DD")
-            for u in range(2):
-                nu, r = "%s%d" % (n, 2 * w + u), r2[u]
-                k = 2 if both else 1
-                if r in "AB":
-                    tt("mg" + nu, G("gb", u), gath(u), z4, ALU.add)
-                elif r == "C" and not (both and u):
-                    act("mg" + nu, G("ab", u, k), gath(u, k), AF.Copy)
-                elif r == "F":
-                    act("mg" + nu, G("gb", u), gath(u), AF.Copy)
-                    sem = "fa%d%d" % (h, 2 * w + u)
-                    uses[sem] = uses.get(sem, 0) + 16
-                    add("G", "md" + nu, lambda g, o=G("gb", u): [g.dma_start(ap(o), ap(z4), accum_op=ALU.add)], [z4, G("gb", u)], [G("gb", u)],
-                        CFG["gdma"], lat=LOCAL + CFG["acc"], sem=sem, val=uses[sem])
-                elif not (both and u):
-                    act("mg" + nu, G("ab", u, k), gath(u, k), AF.Identity, bias=192.0)
-                if r in "DE":
-                    g0, a0 = G("gb", u)[1], G("ab", u)[1]
-                    scan("md" + nu, [(A("gb", g0 + 128 * i, g0 + 128 * i + 128), A("ab", a0 + 128 * i, a0 + 128 * i + 128), zb) for i in range(4)],
-                         ALU.max, ALU.subtract)
-                if r in "ADF":
-                    ts("ma" + nu, G("ab", u), G("gb", u), 0.0, ALU.max, 2.0, ALU.mult)
-                elif r in "BE":
-                    act("ma" + nu, G("ab", u), G("gb", u), AF.Abs)
+        n, s, key = "%d%d" % (t, h), 2 * t + h, "key%d" % h
+        z1, zb = zin(s), A("zb", 128 * s, 128 * s + 128)
+        mm("kb" + n, [(A(key, 0, KEYS), A(w), A(b), b == "b2", False) for w, b in (("idk", "b2"), ("idw", "b1"))])
+        col = lambda c: A(key, c, KEYS, WORLD)
+        for u, (r, c0, m) in enumerate(calls(t, h)):
+            nu = "%s%x" % (n, u)
+            gath = IND(A("tab", SPARE), A("o16", 256 * h + 8 * c0, 256 * h + 8 * (c0 + m)))
+            o = 4096 * h + 128 * c0
+            G = lambda b, i=0, k=m: A(b, o + 128 * i, o + 128 * (i + k))
+            if r in "AB":
+                tt("mg" + nu, G("gb"), gath, zin(s, m), ALU.subtract)
+            elif r == "C":
+                act("mg" + nu, G("ab"), gath, AF.Copy)
+            else:
+                act("mg" + nu, G("ab"), gath, AF.Identity, bias=192.0)
+            for i0 in range(0, m, 4):
+                k, nv = min(4, m - i0), nu + ("b" if i0 else "")
+                if r == "D":
+                    scan("md" + nv, [(G("gb", i, 1), G("ab", i, 1), zb) for i in range(i0, i0 + k)], ALU.max, ALU.subtract)
+                if r in "AD":
+                    ts("ma" + nv, G("ab", i0, k), G("gb", i0, k), 0.0, ALU.max, 2.0, ALU.mult)
+                elif r == "B":
+                    act("ma" + nv, G("ab", i0, k), G("gb", i0, k), AF.Abs)
                 else:
                     pd = "pd%d" % (nr2[0] % 2); nr2[0] += 1
-                    mm("md" + nu, [(A(pd), A("idn"), G("ab", u), True, False)]
-                       + [(A(pd, 128 * i, 128 * i + 128), A("nid"), z1, False, i == 3) for i in range(4)])
-                    act("ma" + nu, G("gb", u), A(pd), AF.Abs)
+                    mm("md" + nv, [(A(pd, 0, 128 * k), A("idn"), G("ab", i0, k), True, False)]
+                       + [(A(pd, 128 * i, 128 * i + 128), A("nid"), z1, False, i == k - 1) for i in range(k)])
+                    act("ma" + nv, G("gb", i0, k), A(pd, 0, 128 * k), AF.Abs)
                 for name, b, sel in (("mw", "gb", "ns8"), ("ms", "gb" if r == "C" else "ab", "s8")):
-                    if name == "ms" or r in "ADF":
-                        c0, o = base // 8 + 4 * u, G(b, u)[1]
-                        mm(name + nu, [(A(key, c0 + i, 256, 32), A(b, o + 128 * i, o + 128 * i + 128), A(sel), False, False) for i in range(4)], key + n)
-        if t:
-            mm("kp" + n, [(A(key, 0, 256), A("pend"), A("rev"), False, False)], key + n)
+                    if name == "ms" or r in "AD":
+                        mm(name + nv, [(col(c0 + i), G(b, i, 1), A(sel), False, False) for i in range(i0, i0 + k)], key + n)
 
     def tail(t, h):
         n, s = "%d%d" % (t, h), 2 * t + h
-        m0 = SLOT * s
+        m0 = SLOT * s + 64
         H = lambda b, k=128: A(b, k * h, k * h + k)
         last = lambda b, k=16: A(b, 128 * h + k - 1, 128 * h + 128, k)
         key = "key%d" % h
-        scan("mn" + n, [(H("kf", 256), A("anew"), A(key, 0, 256))], ALU.add, ALU.min)
-        cp("ki" + n, H("ki", 8), A("kf", 256 * h + 31, 256 * h + 256, 32))
-        ts("pt" + n, H("pt32", 8), H("ki", 8), 31, ALU.bitwise_and)
-        pos = A(key, 384, 400)
+        scan("mn" + n, [(H("kf", KEYS), A("anew"), A(key, 0, KEYS))], ALU.add, ALU.min)
+        for r in range(PARTS):
+            at = lambda c: A("kf", KEYS * h + c + 2 * r, KEYS * h + KEYS, WORLD)
+            o = 144 * h + SHIFTS * (r + 1) - 1
+            tt("pt%s%d" % (n, r), A("bx", o, o + 128, 16), at(31), at(33), ALU.subtract)
+        pos = A(key, 448, 464)
         pt16, pd16 = A("pt16", 16 * h, 16 * h + 8), A("pt16", 16 * h + 8, 16 * h + 16)
-        tt("bx" + n, H("bx"), IND(H("pt32", 8), lst(LG, 8)), A("dia"), ALU.mult)
-        mm("tr" + n, [(pos, A("idn"), A("cj"), True, False), (pos, H("bx"), A("sj"), False, True)])
+        mm("tq" + n, [(pos, A("idn"), A("cj", 0, 16), True, False), (pos, A("idn"), A("cj", 16, 32), False, False)])
+        o = 144 * h + SHIFTS - 1
+        mm("tr" + n, [(pos, A("bx", o - a, o + 128 - a), A("sj", a, 16 * SHIFTS, SHIFTS), False, a == SHIFTS - 1) for a in range(SHIFTS)])
         cp("pu" + n, H("pt16", 16), pos)
-        act("zn" + n, A("zout", 128 * s, 128 * s + 128), IND(H("gb", 4096), pd16), AF.Abs)
+        zo, z1 = A("zout", 128 * s, 128 * s + 128), zin(s)
+        plus = lambda o, k: A("m160", 0, k)
+        act("zn" + n, zo, IND(H("gb", 4096), pd16), AF.Abs)
         send("mid", t, h)
-        tt("xx" + n, H("xx"), IND(H("o32", 256), pt16), A("dia"), ALU.mult)
-        scan("ff" + n, [(H("ff"), A("rst"), H("xx"))])
+        tt("xx" + n, H("xx"), IND(H("o32", 256), pt16), A("dim"), ALU.min)
+        scan("ff" + n, [(H("ff"), A("rst"), H("xx"))], ALU.mult, ALU.max)
         ts("qq" + n, H("q16", 8), last("ff"), BASE, ALU.add)
-        qr = A(key, 256, 384)
-        mm("qr" + n, [(qr, A("blk"), H("xx"), True, True)])
+        qr = A(key, KEYS, KEYS + 128)
+        mm("qc" + n, [(qr, A("id8"), A("cq"), True, False)])
+        mm("qr" + n, [(qr, A("blk"), H("xx"), False, True)])
         tt("ne" + n, H("ne"), qr, H("ff"), ALU.not_equal)
-        scan("rr" + n, [(H("rr"), H("ne"), H("xx"))])
-        wide = int(CFG["wide"][h])
-        if wide == 1:
-            ts("of" + n, A("off16", 16 * h, 16 * h + 16, 2), last("rr"), BASE, ALU.add, pc(3), ALU.max)
-        else:
-            if CFG["xe"] == "V":
-                tt("xe" + n, H("xe"), IND(H("o32", 256), pt16), A("die"), ALU.mult)
-            else:
-                tt("xe" + n, H("xe"), A("pq", 256, 384), H("xx"), ALU.mult)
-            scan("fe" + n, [(H("fe"), A("rse"), H("xe"))])
+        wide, o0 = int(CFG["wide"][h]), 256 * h
+        scan("rr" + n, [(A("off16", o0 + 1, o0 + 1 + 128 * wide, wide), H("ne"), H("xx"))], ALU.mult, ALU.max)
+        if wide == 2:
+            tt("xe" + n, H("xe"), A("pq", 256, 384), H("xx"), ALU.min)
+            scan("fe" + n, [(H("fe"), A("rse"), H("xe"))], ALU.mult, ALU.max)
             tt("nf" + n, H("nf"), qr, H("fe"), ALU.not_equal)
-            scan("rf" + n, [(H("rf"), H("nf"), H("xe"))])
-            ts("of" + n, A("off16", 16 * h + 1, 16 * h + 8, 2), last("rr", 32), BASE, ALU.add, pc(10), ALU.max)
-            ts("og" + n, A("off16", 16 * h, 16 * h + 8, 2), last("rf", 32), BASE, ALU.add, pc(3), ALU.max)
-        z1 = A("zin", 128 * s, 128 * s + 128)
-        if from_table(t, h):
-            ss = A("pd0", 0, 128)
-            act("gq" + n, H("gq"), IND(A("tab"), H("q16", 8)), AF.Copy)
+            scan("rf" + n, [(A("off16", o0, o0 + 256, 2), H("nf"), H("xe"))], ALU.mult, ALU.max)
+        offs = lambda j: A("off16", o0 + 16 * j + 16, o0 + 16 * j + 17) if wide == 1 else A("off16", o0 + 64 * j + 62, o0 + 64 * j + 64)
+        if t + 1 < RO:
+            act("ng" + n, H("nxg"), IND(A("nxb"), H("q16", 8)), AF.Identity, bias=-2048.0)
+            sel16("cs" + n, A("pn", 0, 8), H("nxg"), "wh")
+            act("cn" + n, A("msg", m0, m0 + 8), A("pn", 0, 8), AF.Identity, bias=22528.0 + 16 * 2048)
+            if CFG["cs"][h] == "R":
+                act("cw" + n, msg(s, -64, 0), IND(msg(s, 0, 8), lst(LJ, 4)), AF.Copy)
+        else:
+            act("ng" + n, H("nxr"), IND(A("nxb"), H("q16", 8)), AF.Copy)
+        if "C" in routes(t, h):
+            ss = A("pd0", 128, 256)
+            act("gq" + n, H("gq"), IND(A("tab", SPARE), H("q16", 8)), AF.Copy)
             mm("xz" + n, [(ss, A("idn"), H("gq"), True, False), (ss, A("idn"), z1, False, True)])
             act("hv" + n, H("hv"), ss, AF.Identity, bias=159.75, scale=0.5)
-            plus = lambda o, k: A("m160", 0, k)
         else:
             act("hv" + n, H("hv"), IND(H("gb", 4096), pd16), AF.Identity, bias=-192.25, scale=0.5)
             plus = lambda o, k: A("zb", 128 * s + o, 128 * s + o + k)
-        act("ng" + n, H("nxg"), IND(A("nxb"), H("q16", 8)), AF.Copy)
-        if t + 1 < RO:
-            sel16("cs" + n, A("pn", 0, 8), H("nxg"))
-            act("cn" + n, A("msg", m0, m0 + 8), A("pn", 0, 8), AF.Identity, bias=22528.0, scale=1.0 / 256)
         if CFG["x2"][h] == "V":
             tt("x2" + n, H("x2"), IND(H("t32", 256), pt16), A("dia"), ALU.mult)
         else:
             act("g2" + n, H("g2"), IND(H("t32", 256), pt16), AF.Copy)
             tt("x2" + n, H("x2"), A("pq", 128, 256), H("g2"), ALU.mult)
-        scan("f2" + n, [(H("f2"), A("rst"), H("x2"))])
+        scan("f2" + n, [(H("f2"), A("rst"), H("x2"))], ALU.mult, ALU.max)
         tt("vn" + n, A("msg", m0 + 8, m0 + 16), last("f2"), A("msg", m0 + 8, m0 + 16), ALU.subtract)
         if t + 1 < RO:
             send("late", t, h)
         k = 16 * wide
-        return lambda: [tt("sc%s%d" % (n, j), IND(A("tab"), A("off16", 16 * h + 2 * j, 16 * h + 2 * j + wide)),
+        return lambda: [tt("sc%s%d" % (n, j), IND(A("tab"), offs(j)),
                            A("hv", 128 * h + k * j, 128 * h + k * j + k), plus(k * j, k), ALU.add) for j in range(8 // wide)]
 
     def penalty(t):
         n = str(t)
-        ts("kd" + n, A("kind"), A("pt32"), 16.0, ALU.is_ge)
-        mm("c1" + n, [(A("pd1", 384, 400), A("one"), A("kind"), True, True)])
-        act("c2" + n, A("cnj"), A("pd1", 384, 400), AF.Identity, bias=288.0, acc=A("cnt"))
-        act("c3" + n, A("cnf"), A("cnt"), AF.Identity, bias=-0.484375, scale=1.0 / 32)
-        act("c4" + n, A("pnf"), A("cnf"), AF.Identity, bias=A("cnt"), scale=-32.0)
-        act("c6" + n, A("pend"), A("idn"), AF.Identity, scale=A("pnf"))
+        k = 18 * PARTS
+        ts("kd" + n, A("kind", 0, k), A("bx", SHIFTS - 1, 288, SHIFTS), 1.0, ALU.is_ge)
+        mm("c1" + n, [(A("pd1", 384, 384 + k), A("one"), A("kind", 0, k), True, True)])
+        act("c2" + n, A("cnj", 0, k), A("pd1", 384, 384 + k), AF.Identity, bias=-64.0 * 4608 / k, scale=-64.0, acc=A("cnt"))
+        act("c3" + n, A("cnf"), A("tiny"), AF.Identity, bias=-0.484375, scale=A("cnt"))
+        act("c4" + n, A("anew", 16, KEYS, WORLD), A("cnf"), AF.Identity, bias=A("cnt"), scale=2048.0)
 
     def finish(h):
         s, n = 2 * (RO - 1) + h, "%d%d" % (RO, h)
         H = lambda b, k=128: A(b, k * h, k * h + k)
         lanes = lambda b: A(b, 128 - 128 * h, 256 - 128 * h)
         pd = "pd%d" % h
-        act("o_d%d" % h, H("dup", 256), IND(A("msg", SLOT * s + 8, SLOT * s + 136), lst(LF1, 16)), AF.Copy)
+        act("o_d%d" % h, H("dup", 256), IND(msg(s, 8, 136), lst(LF1, 16)), AF.Copy)
         turn("o_t%d" % h, H("trp", 256), H("dup", 256))
         act("o_h%d" % h, H("oh1"), IND(H("trp", 256), lst(LF2, 8)), AF.Abs, bias=-0.5, scale=2.0)
         act("o_m%d" % h, lanes("oh"), H("oh1"), AF.Identity, bias=12288.5, scale=-1.0)
@@ -539,10 +550,9 @@ def build(T, topo, rank, pace=CFG):
         tt("o_s%d" % h, lanes("ohs"), A(pd, 256, 384), H("keep"), ALU.add)
         dma("S", "st_h%d" % h, [(T.yh[:, 128 - 128 * h:256 - 128 * h], T.ohs[:, 128 - 128 * h:256 - 128 * h])], [lanes("ohs")], [], LOCAL)
         act("o_z%d" % h, lanes("oz"), IND(A("zout", 128 * s, 128 * s + 128), lst(LZ, 8)), AF.Copy)
-        act("o_r%d" % h, H("nxr"), IND(H("nxg"), lst(LZ, 8)), AF.Copy)
-        mm("o_n%d" % h, [(A("pn", 0, 128), A("bn"), H("nxr"), True, True)])
-        act("o_c%d" % h, lanes("oc"), A("pn", 0, 128), AF.Copy)
+        act("o_c%d" % h, lanes("oc"), IND(H("nxr"), lst(LZ, 8)), AF.Copy)
 
+    visits.append(True)
     for t in range(RO):
         prep(t, 0); main(t, 0); prep(t, 1)
         s0 = tail(t, 0)
@@ -551,7 +561,8 @@ def build(T, topo, rank, pace=CFG):
         s0(); s1()
         if t + 1 < RO:
             penalty(t)
-    dma("Y", "st_x", [(T.yx[:], T.tab[:, SPARE:])], [A("tab")], [], LOCAL + CFG["table"])
+    visits.pop()
+    dma("Y", "st_x", [(T.yx[:], T.tab[:, SPARE:])], [A("tab", SPARE)], [], LOCAL + CFG["table"])
     finish(0); finish(1)
     dma("Y", "st_z", [(T.yz[:], T.oz[:])], [A("oz")], [], LOCAL)
     dma("Y", "st_c", [(T.yc[:], T.oc[0:128:16, :])], [A("oc")], [], LOCAL)
@@ -564,11 +575,11 @@ def hazards(ops):
     for i, o in enumerate(ops):
         d = {}
         for kind, regs in (("r", o["rd"]), ("w", o["wr"])):
-            for b, lo, hi, _ in regs:
+            for b, lo, hi, st in regs:
                 psum = SCRATCH[b][0] == "psum"
-                for j, k2, l2, h2 in hist.get(b, ()):
+                for j, k2, l2, h2, s2 in hist.get(b, ()):
                     same = ops[j]["q"] == o["q"] and o["q"] in ("V", "S", "P", "G") and ops[j]["sem"] is None
-                    clash = l2 < hi and lo < h2 and (kind == "w" or k2 == "w")
+                    clash = l2 < hi and lo < h2 and (kind == "w" or k2 == "w") and not (st == s2 and (lo - l2) % st)
                     if psum and o.get("grp") and ops[j].get("grp") == o["grp"]:
                         continue
                     if psum:
@@ -576,73 +587,16 @@ def hazards(ops):
                     elif clash:
                         d[j] = True
         for kind, regs in (("r", o["rd"]), ("w", o["wr"])):
-            for b, lo, hi, _ in regs:
+            for b, lo, hi, st in regs:
                 hh = hist.setdefault(b, [])
-                if kind == "w" or SCRATCH[b][0] == "psum":
-                    q = o["q"]
-                    if SCRATCH[b][0] == "psum":
-                        hh[:] = [e for e in hh if ops[e[0]]["q"] == q]
-                    else:
-                        hh[:] = [e for e in hh if not (lo <= e[2] and e[3] <= hi) or e[0] == i]
-                hh.append((i, kind, lo, hi))
+                if SCRATCH[b][0] == "psum":
+                    hh[:] = [e for e in hh if ops[e[0]]["q"] == o["q"]]
+                elif kind == "w":
+                    hh[:] = [e for e in hh if not (lo <= e[2] and e[3] <= hi and (st == 1 or (st == e[4] and (lo - e[2]) % st == 0))) or e[0] == i]
+                hh.append((i, kind, lo, hi, st))
         d.pop(i, None)
         deps.append(d)
     return deps
-
-
-def schedule(ops):
-    deps = hazards(ops)
-    idx = {o["name"]: i for i, o in enumerate(ops)}
-    n = len(ops)
-    pre = [dict(d) for d in deps]
-    for i, o in enumerate(ops):
-        if o["after"]:
-            pre[i][idx[o["after"]]] = o["q"] is None
-    succ = [[] for _ in ops]
-    for i in range(n):
-        for j in pre[i]:
-            succ[j].append(i)
-    cost = [max(o["cost"], 1e-4) for o in ops]
-    lag = [o["lat"] + CFG["hop"] for o in ops]
-
-    def place(key, back):
-        before, behind = (succ, pre) if back else (pre, succ)
-        left = [len(b) for b in before]
-        ready = [ops[i]["lat"] if back else 0.0 for i in range(n)]
-        start = [0.0] * n
-        free = {o["q"]: 0.0 for o in ops}
-        avail = {q: [i for i in range(n) if ops[i]["q"] == q and not left[i]] for q in free}
-        while any(avail.values()):
-            st, q = min(((max(free[q], min(ready[i] for i in l)), q) for q, l in avail.items() if l), key=lambda x: x[0])
-            i = min((i for i in avail[q] if ready[i] <= st), key=lambda i: key[i])
-            avail[q].remove(i)
-            start[i] = st
-            if q:
-                free[q] = st + cost[i]
-            for k in behind[i]:
-                gap = (lag[k] if pre[i][k] else 0.0) if back else (lag[i] if pre[k][i] else 0.0)
-                ready[k] = max(ready[k], st + cost[i] + gap)
-                left[k] -= 1
-                if left[k] == 0:
-                    avail[ops[k]["q"]].append(k)
-        return start, max(start[i] + cost[i] + (0.0 if back else ops[i]["lat"]) for i in range(n))
-
-    way = [0.0] * n
-    left = [len(s) for s in succ]
-    todo = [i for i in range(n) if not left[i]]
-    for i in todo:
-        way[i] = cost[i] + max([ops[i]["lat"]] + [way[k] + (lag[i] if pre[k][i] else 0.0) for k in succ[i]])
-        for j in pre[i]:
-            left[j] -= 1
-            if not left[j]:
-                todo.append(j)
-    best = start, total = place([-x for x in way], False)
-    for _ in range(CFG["passes"]):
-        back, _ = place([-(start[i] + cost[i]) for i in range(n)], True)
-        start, total = place([-(back[i] + cost[i]) for i in range(n)], False)
-        if total < best[1]:
-            best = start, total
-    return best
 
 
 def plan(T, topo):
@@ -653,6 +607,18 @@ def plan(T, topo):
     for i, o in enumerate(ops):
         if o["after"]:
             pre[i][idx[o["after"]]] = o["q"] is None
+    seen = {}
+
+    def waited(i):
+        if i not in seen:
+            through = 0
+            for j in pre[i]:
+                through |= waited(j)
+            seen[i] = through | sum(1 << j for j, w in pre[i].items() if w)
+            pre[i] = {j: w for j, w in pre[i].items() if not through >> j & 1}
+        return seen[i]
+    for i in range(n):
+        waited(i)
     qs = [o["q"] for o in ops]
     nets = []
     for p in PACE:
@@ -714,7 +680,7 @@ def plan(T, topo):
             left[j] -= 1
             if not left[j]:
                 todo.append(j)
-    best = place(nets[0], [-x for x in way], False)
+    best = place(nets[0], [max(way) - x for x in way], False)
     unit = times(best)
     score = float(len(nets))
     seed = [CFG["seed"]]
@@ -732,7 +698,105 @@ def plan(T, topo):
         new = sum(a / b for a, b in zip(times(start), unit))
         if new <= score:
             best, score = start, new
-    return {ops[i]["name"]: k for k, i in enumerate(sorted(range(n), key=lambda i: (best[i], i)))}, times(best)
+
+    twin = {o["role"]: i for i, o in enumerate(ops) if o["role"]}
+    succ = [[k for k, _ in b] for b in nets[0][3]]
+    qi = [" VSPGY".index(q or " ") for q in qs]
+
+    def run(order, net, trace=False):
+        cost, lat, before, _ = net
+        end, free, top, why, last, at = [0.0] * n, [0.0] * 6, 0.0, {}, [None] * 6, None
+        for i in order:
+            q = qi[i]
+            s, w = free[q], -1
+            for j, gap in before[i]:
+                if end[j] + gap >= s:
+                    s, w = end[j] + gap, j
+            s += cost[i]
+            end[i] = s
+            if q:
+                free[q] = s
+            if trace:
+                why[i], last[q] = (w, last[q]), i
+            if s + lat[i] > top:
+                top, at = s + lat[i], i
+        if trace is None:
+            return end
+        if not trace:
+            return top
+        arcs = []
+        while at is not None:
+            w, front = why[at]
+            if w < 0 and front is not None and qi[at]:
+                arcs.append((front, at))
+            at = w if w >= 0 else front if qi[at] else None
+        return arcs
+
+    order = kept = sorted(range(n), key=lambda i: (best[i], i))
+    now = [run(order, net) / u for net, u in zip(nets, unit)]
+    low, arcs = sum(now), None
+    def alike(order, model, visits):
+        end = run(order, nets[0], None)
+        at = [end[twin["sc13", t]] for t in range(RO)]
+        key = end[:]
+        for i, o in enumerate(ops):
+            if o["role"] and o["role"][1] in visits and (o["role"][0], model) in twin:
+                t = o["role"][1]
+                key[i] = end[twin[o["role"][0], model]] - at[model] + at[t]
+        for i in order:
+            key[i] = max([key[i]] + [key[j] + 1e-6 for j in pre[i]])
+        return sorted(order, key=lambda i: key[i])
+
+    for r in range(CFG["swaps"]):
+        if r % CFG["copy"] == CFG["copy"] // 2:
+            for model in range(1, RO):
+                for visits in (range(1, RO - 1), range(1, RO), range(RO)):
+                    new = alike(order, model, visits)
+                    got = [run(new, net) / u for net, u in zip(nets, unit)]
+                    if sum(got) < sum(now):
+                        order, now, arcs = new, got, None
+        if arcs is None:
+            arcs = [run(order, net, True) for net in nets]
+            key, place_in, line = [0.0] * n, [0] * n, [[] for _ in range(6)]
+            for k, i in enumerate(order):
+                key[i], place_in[i] = k, len(line[qi[i]])
+                line[qi[i]].append(i)
+        first = int(draw() * len(nets))
+        a, b = arcs[first][int(draw() * len(arcs[first]))]
+        free = draw() < CFG["free"]
+        if free:
+            l = line[1 + int(draw() * 3)]
+            k = 1 + int(draw() * (len(l) - 1))
+            a, b = l[k - 1], l[k]
+        far, l = int(draw() ** 2 * CFG["far"]), line[qi[a]]
+        if free or draw() < 0.5:
+            pairs, d = [(b, l[max(0, place_in[a] - far)])], -0.5
+        else:
+            pairs, d = [(a, l[min(len(l) - 1, place_in[b] + far)])], 0.5
+        x, y = ops[pairs[0][0]]["role"], ops[pairs[0][1]]["role"]
+        if x and y and draw() < CFG["all"]:
+            pairs = [(twin[x[0], x[1] + e], twin[y[0], y[1] + e]) for e in range(-RO, RO) if (x[0], x[1] + e) in twin and (y[0], y[1] + e) in twin]
+        k2 = key[:]
+        for i, j in pairs:
+            if (key[j] - k2[i]) * d < 0:
+                continue
+            k2[i], todo = key[j] + d, [i]
+            for i in todo:
+                for j in pre[i] if d < 0 else succ[i]:
+                    if (k2[j] - k2[i]) * d <= 0:
+                        k2[j] = k2[i] + d / 64
+                        todo.append(j)
+        new, room, got = sorted(order, key=lambda i: k2[i]), -CFG["heat"] * (1 - r / CFG["swaps"]) ** 2 * math.log(draw() + 1e-9), now[:]
+        for m in range(len(nets)):
+            m = (m + first) % len(nets)
+            got[m] = run(new, nets[m]) / unit[m]
+            if sum(got) > sum(now) + room + 0.004:
+                break
+        if sum(got) <= sum(now) + room:
+            order, now, arcs = new, got, None
+            if sum(now) < low:
+                low, kept = sum(now), order
+    return {ops[i]["name"]: k for k, i in enumerate(kept)}, [max(e + x for e, x in zip(run(kept, net, None), net[1])) for net in nets]
 
 
 ORDER = {}

import math
from concourse.bass import DstId, RemoteDMATransfer
from concourse.mybir import AluOpType as ALU, ActivationFunctionType as AF

RO = 5
SLOT = 208
SPARE = 16384
PARTS = 2
SHIFTS = 16 // PARTS
WORLD = 32 + 2 * PARTS
KEYS = 8 * WORLD


def units(routes):
    return tuple((r, c, 4) for r, c in zip(routes, (0, 4, 16, 20, 8, 12, 24, 28)))


CALLS = (units("CCAADCAA"), units("DDADDDDB"))
CFG = dict(calls=CALLS, first=CALLS, last=CALLS, cs0="VS", cs="HR", x2="VS", wide="12",
           cyc=0.95e-3, gat=1.56, sca=3.8, pec=0.5e-3, hop=0.18, call=0.5, remote=2.6, local=2.0, table=3.2)
CFG.update(seed=4, rounds=30, swaps=30000, heat=0.002, far=6, free=0.2, copy=500, all=0.8)
PACE = [dict(cyc=0.83e-3, pec=0.44e-3, hop=0.2, gat=1.56, sca=3.8, remote=2.3, local=1.9),
        dict(cyc=1.15e-3, pec=0.6e-3, hop=0.2, gat=1.95, sca=5.0, remote=3.0, local=2.3),
        dict(cyc=0.87e-3, pec=0.46e-3, hop=0.17, gat=1.2, sca=2.5, remote=3.2, local=2.6),
        dict(cyc=0.9e-3, pec=0.5e-3, hop=0.25, gat=1.3, sca=3.0, remote=4.0, local=3.2),
        dict(cyc=1.0e-3, pec=0.6e-3, hop=0.3, gat=1.1, sca=2.0, remote=3.4, local=2.4)]

SCRATCH = {
    "tab": ("sbuf", [128, 4096 + SPARE], "bfloat16"), "nxb": ("sbuf", [128, 4096], "int32"),
    "gb": ("sbuf", [128, 8192], "bfloat16"), "ab": ("sbuf", [128, 8192], "bfloat16"),
    "idw": ("sbuf", [128, 128], "bfloat16"), "idk": ("sbuf", [128, 128], "bfloat16"),
    "msg": ("sbuf", [128, SLOT * 10], "float32"), "pmsg": ("sbuf", [128, 120 * 10], "float32"),
    "crp": ("sbuf", [128, 128], "float32"),
    "zin": ("sbuf", [128, 5120], "bfloat16"), "zout": ("sbuf", [128, 1280], "bfloat16"),
    "pz": ("sbuf", [128, 1536], "bfloat16"), "zb": ("sbuf", [128, 1280], "bfloat16"),
    "t32": ("sbuf", [128, 512], "int32"), "o32": ("sbuf", [128, 512], "int32"), "o16": ("sbuf", [128, 512], "uint16"),
    "kf": ("sbuf", [128, 2 * KEYS], "float32"), "quad": ("sbuf", [128, 8], "float32"), "cs": ("sbuf", [128, 128], "float32"), "id8": ("sbuf", [128, 128], "float16"),
    "pt16": ("sbuf", [128, 32], "uint16"), "q16": ("sbuf", [128, 16], "uint16"),
    "bx": ("sbuf", [128, 288], "bfloat16"), "off16": ("sbuf", [128, 514], "uint16"),
    "dim": ("sbuf", [128, 128], "float32"), "cq": ("sbuf", [128, 128], "float16"), "kind": ("sbuf", [128, 72], "bfloat16"),
    "xx": ("sbuf", [128, 256], "float32"), "ff": ("sbuf", [128, 256], "float32"), "ne": ("sbuf", [128, 256], "float32"),
    "x2": ("sbuf", [128, 256], "float32"), "f2": ("sbuf", [128, 256], "float32"),
    "xe": ("sbuf", [128, 256], "float32"), "fe": ("sbuf", [128, 256], "float32"), "nf": ("sbuf", [128, 256], "float32"),
    "g2": ("sbuf", [128, 256], "float32"),
    "gq": ("sbuf", [128, 256], "bfloat16"), "hv": ("sbuf", [128, 256], "bfloat16"),
    "nxg": ("sbuf", [128, 256], "float16"), "wh": ("sbuf", [128, 144], "float16"), "al1": ("sbuf", [128, 256], "bfloat16"), "al2": ("sbuf", [128, 256], "bfloat16"),
    "alk": ("sbuf", [128, 16], "float32"), "dif": ("sbuf", [128, 128], "float32"),
    "cnj": ("sbuf", [128, 72], "float32"), "cnt": ("sbuf", [128, 1], "float32"), "cnf": ("sbuf", [128, 8], "bfloat16"),
    "pi": ("sbuf", [128, 1], "int32"), "pb": ("sbuf", [128, 8], "int32"), "pc": ("sbuf", [128, 16], "float32"),
    "ci": ("sbuf", [128, 144], "float32"), "c16": ("sbuf", [128, 128], "float32"), "cg": ("sbuf", [128, 128], "float32"),
    "cg8": ("sbuf", [128, 128], "float32"), "c32": ("sbuf", [128, 128], "float32"),
    "lio": ("sbuf", [128, 80], "float32"), "lst": ("sbuf", [128, 96], "uint16"),
    "idn": ("sbuf", [128, 128], "bfloat16"), "nid": ("sbuf", [128, 128], "bfloat16"), "wd": ("sbuf", [128, 144], "bfloat16"),
    "idf": ("sbuf", [128, 128], "float32"), "nif": ("sbuf", [128, 128], "float32"),
    "s8": ("sbuf", [128, 8], "bfloat16"), "ns8": ("sbuf", [128, 8], "bfloat16"), "sj": ("sbuf", [128, 256], "bfloat16"),
    "cj": ("sbuf", [128, 32], "bfloat16"), "anew": ("sbuf", [128, KEYS], "float32"), "tiny": ("sbuf", [128, 8], "float32"),
    "blk8": ("sbuf", [128, 128], "bfloat16"), "die": ("sbuf", [128, 128], "float32"), "rse": ("sbuf", [128, 128], "float32"),
    "blk": ("sbuf", [128, 128], "float32"), "dia": ("sbuf", [128, 128], "float32"), "rst": ("sbuf", [128, 128], "float32"),
    "b1": ("sbuf", [128, KEYS], "bfloat16"), "b2": ("sbuf", [128, KEYS], "bfloat16"),
    "one": ("sbuf", [128, 128], "bfloat16"), "m160": ("sbuf", [128, 32], "bfloat16"),
    "inb": ("sbuf", [128, 272], "int32"), "sb": ("sbuf", [128, 256], "int32"), "sg": ("sbuf", [128, 256], "float32"),
    "yf": ("sbuf", [128, 272], "float32"), "dup": ("sbuf", [128, 544], "float32"),
    "trp": ("sbuf", [128, 544], "float32"), "ztb": ("sbuf", [128, 256], "bfloat16"),
    "oh1": ("sbuf", [128, 256], "float32"), "oh": ("sbuf", [128, 256], "float32"), "ph": ("sbuf", [128, 256], "float32"),
    "keep": ("sbuf", [128, 256], "float32"), "ohs": ("sbuf", [128, 256], "float32"), "nxr": ("sbuf", [128, 256], "float32"),
    "oc": ("sbuf", [128, 256], "float32"), "oz": ("sbuf", [128, 256], "bfloat16"),
    "key0": ("psum", [128, 512], "float32"), "key1": ("psum", [128, 512], "float32"),
    "pd0": ("psum", [128, 512], "float32"), "pd1": ("psum", [128, 512], "float32"),
    "pq": ("psum", [128, 512], "float32"), "ps": ("psum", [128, 512], "float32"),
    "pa": ("psum", [128, 512], "float32"), "pn": ("psum", [128, 512], "float32"),
}
STORES = ["st_x", "st_h0", "st_h1", "st_z", "st_c"]
SEMAPHORES = (["cV", "cS", "cP", "cG", "sent", "ld_m", "ld_c", "ld_z", "ld_t", "ld_nx"] + STORES
              + ["%s%d%d" % (k, t, h) for k in ("az", "ac", "ae", "bz", "be", "du") for t in range(RO + 1) for h in range(2)])

L1, L2, LZ, LF1, LF2, LJ = 0, 18, 38, 46, 62, 70


def A(name, lo=0, hi=None, step=1):
    return (name, lo, SCRATCH[name][1][1] if hi is None else hi, step)


def IND(win, off):
    return ("*", win, off)


def deal(n, total):
    k = [1] * n
    while True:
        i = k.index(min(k))
        if sum(k) + k[i] > total:
            return k
        k[i] *= 2


def build(T, topo, rank, pace=CFG):
    ops, visits = [], []
    CYC, GAT, SCA, PEC, REMOTE, LOCAL = [pace[k] for k in ("cyc", "gat", "sca", "pec", "remote", "local")]
    N = len(T.cores)
    me = T.cores[rank]
    BASE = -float(SPARE)

    def calls(t, h):
        return CFG["first" if t == 0 else "last" if t == RO - 1 else "calls"][h]

    def routes(t, h):
        return set(c[0] for c in calls(t, h))

    def ap(a):
        if not isinstance(a, tuple):
            return a
        if a[0] == "*":
            return ap(a[1]).indirect(ap(a[2]))
        return T[a[0]][:, a[1]:a[2]:a[3]] if a[3] != 1 else T[a[0]][:, a[1]:a[2]]

    def regs(xs):
        out = []
        for a in xs:
            if isinstance(a, tuple):
                out += [a[1], a[2]] if a[0] == "*" else [a]
        return out

    def width(a):
        return 16 * width(a[2]) if a[0] == "*" else len(range(a[1], a[2], a[3]))

    def two(a):
        return SCRATCH[a[0]][2] in ("bfloat16", "uint16", "float16")

    def add(q, name, fn, rd, wr, cost, lat=0.0, sem=None, val=0, after=None):
        r = regs(rd)
        w = []
        for a in wr:
            if a[0] == "*":
                w.append(a[1]); r.append(a[2])
            else:
                w.append(a)
        k = min(i for i in range(2, len(name) + 1) if name[i:i + 1] in "0123456789")
        role = (name[:k] + name[k + 1:], int(name[k])) if visits else None
        ops.append(dict(q=q, name=name, fn=fn, rd=r, wr=w, cost=cost, lat=lat, sem=sem, val=val, after=after, role=role))

    def vcost(out, ins, both=False):
        if out[0] == "*":
            return 0.05 + width(out) * SCA * CYC
        if ins[0][0] == "*":
            return 0.05 + width(out) * GAT * CYC
        f = 2.0 if both else (0.5 if two(out) and all(two(a) for a in ins) else 1.0)
        return max(64, width(ins[0]) * f) * CYC

    def tt(name, out, a, b, op):
        both = a[0] == "*" or (SCRATCH[a[0]][0] == "sbuf" and SCRATCH[b[0]][0] == "sbuf")
        add("V", name, lambda g: [g.vector.tensor_tensor(ap(out), ap(a), ap(b), op)], [a, b], [out], vcost(out, [a, b], both))

    def ts(name, out, a, s1, op0, s2=None, op1=None):
        if op1 is None:
            fn = lambda g: [g.vector.tensor_scalar(ap(out), ap(a), ap(s1), None, op0)]
        else:
            fn = lambda g: [g.vector.tensor_scalar(ap(out), ap(a), ap(s1), ap(s2), op0, op1)]
        add("V", name, fn, [a, s1, s2], [out], vcost(out, [a]))

    def cp(name, out, a):
        add("V", name, lambda g: [g.vector.tensor_copy(ap(out), ap(a))], [a], [out], vcost(out, [a]))

    def scan(name, items, op0=ALU.mult, op1=ALU.add):
        add("V", name, lambda g: [g.vector.tensor_tensor_scan(ap(o), ap(a), ap(b), 0.0, op0, op1) for o, a, b in items],
            [x for i in items for x in i[1:]], [i[0] for i in items], sum(vcost(o, [a, b]) for o, a, b in items))

    def turn(name, out, a):
        add("V", name, lambda g: [g.vector.transpose(ap(out), ap(a))], [a], [out], vcost(out, [a]))

    def fill(name, out, v):
        add("V", name, lambda g: [g.vector.memset(ap(out), v)], [], [out], vcost(out, [out]))

    def act(name, out, a, func, bias=0.0, scale=1.0, acc=None):
        c = 0.065 + width(out) * GAT * CYC if a[0] == "*" else max(64, width(out)) * CYC + 0.03
        kw = {}
        if bias != 0.0:
            kw["bias"] = ap(bias)
        if scale != 1.0:
            kw["scale"] = ap(scale)
        if acc is not None:
            kw["accum_out"] = ap(acc)
        add("S", name, lambda g: [g.scalar.activation(ap(out), ap(a), func, **kw)], [a, bias, scale], [out] + ([acc] if acc else []), c)

    def shift(eng, name, out, a, by):
        if eng == "V":
            ts(name, out, a, by, ALU.add)
        else:
            act(name, out, a, AF.Identity, bias=by)

    def mm(name, items, grp=None):
        c = sum(max(64, width(i[2])) * (1 if two(i[2]) else 4) for i in items) * PEC
        add("P", name, lambda g, close=False: [g.tensor.matmul(ap(o), ap(l), ap(r), s, e or (close and k == len(items) - 1))
                                               for k, (o, l, r, s, e) in enumerate(items)],
            [x for i in items for x in i[1:3]], [i[0] for i in items], c, lat=0.1)
        ops[-1]["grp"] = grp

    def iota(name, out, pat, base, ch=0, after=None):
        if SCRATCH[out[0]][2] == "int32":
            fn = lambda g: [g.iota(ap(out), pat, base, ch)]
        else:
            fn = lambda g: [g.iota(ap(out), pat, base, ch, allow_small_or_imprecise_dtypes=True)]
        add("G", name, fn, [], [out], 0.15 + 2 * width(out) * CYC, after=after)

    def dma(q, name, pairs, rd, wr, lat, after=None):
        eng = (lambda g: g.sync) if q == "Y" else (lambda g: g.scalar)
        add(q, name, lambda g: [eng(g).dma_start(o, a) for o, a in pairs], rd, wr, 0.06 * len(pairs), lat=lat, sem=name, val=16 * len(pairs), after=after)

    def sel16(name, out, src, w="wd"):
        mm(name, [(out, A(w, 15 - p, 143 - p), A(src[0], src[1] + p, src[2], 16), p == 0, p == 15) for p in range(16)])

    def msg(s, lo, hi):
        return A("msg", SLOT * s + 64 + lo, SLOT * s + 64 + hi)

    def zin(s, k=1):
        return A("zin", 512 * s, 512 * s + 128 * k)

    def mail(r, kind, t, h):
        s, s1, n1 = 2 * t + h, 2 * t + h + 2, "%d%d" % (t + 1, h)
        nxt, other = (r + 1) % N, ((r ^ 1) + 1) % N
        zo = A("zout", 128 * s, 128 * s + 128)
        out = []
        if t + 1 == RO:
            if kind == "mid":
                out.append((zo, r ^ 1, A("pz", 128 * s1, 128 * s1 + 128), "bz" + n1))
            else:
                out.append((A("oh", 128 - 128 * h, 256 - 128 * h), r ^ 1, A("ph", 128 - 128 * h, 256 - 128 * h), "be" + n1))
        elif kind == "late":
            k = -64 if CFG["cs"][h] == "R" else 0
            out.append((msg(s, k, 16), nxt, msg(s1, k + 8, 24), "ac" + n1))
        elif kind == "mid":
            out.append((zo, nxt, zin(s1), "az" + n1))
            if other != r:
                out.append((zo, other, A("pz", 128 * s1, 128 * s1 + 128), "bz" + n1))
        else:
            src = msg(s, 16, 136)
            out.append((src, nxt, msg(s1, 24, 144), "ae" + n1))
            if other != r:
                out.append((src, other, A("pmsg", 120 * s1, 120 * s1 + 120), "be" + n1))
        k = deal(len(out), len(topo.engines(T.cores[r], T.cores[out[0][1]])))
        return [o + (e,) for o, e in zip(out, k)]

    def send(kind, t, h):
        trs = mail(rank, kind, t, h)

        def fn(g):
            out, e0 = [], 0
            for src, r, land, sem, k in trs:
                rid, pid, _ = topo.addr(T.cores[r])
                m = sum(1 << e for e in topo.engines(me, T.cores[r])[e0:e0 + k])
                e0 += k
                out.append((rid, pid, m, src, land, sem))
            if len(out) == 1:
                rid, pid, m, src, land, sem = out[0]
                g.remote_dma(ap(land), ap(src), T.sem[sem], T.sem.sent, pid, rid, m)
            else:
                g.remote_dma_fused([RemoteDMATransfer(dst_ids=[DstId(rid=rid, pnc=pid)], dma_engine_mask=m, remote_sem=T.sem[sem],
                                                      src=ap(src), dst=ap(land)) for rid, pid, m, src, land, sem in out], local_sem=T.sem.sent)
            return []
        add("G", "%s%d%d" % (kind, t, h), fn, [x[0] for x in trs], [], CFG["call"], sem="sent", val=sum(x[4] for x in trs))

    def recv(kind, t, h, src_rank, sem):
        mine = [x for x in mail(src_rank, kind, t - 1, h) if x[1] == rank and x[3] == sem]
        add(None, sem, None, [], [x[2] for x in mine], 0.0, lat=REMOTE, sem=sem, val=sum(x[4] for x in mine), after="%s%d%d" % (kind, t - 1, h))

    def lst(lo, n):
        return A("lst", lo, lo + n)

    def pc(i):
        return A("pc", i, i + 1)

    dma("Y", "ld_m", [(T.inb[:, 0:256], T.mem[:])], [], [A("inb", 0, 256)], LOCAL + 0.2)
    dma("S", "ld_c", [(T.inb[:, 256:272], T.plc[:])], [], [A("inb", 256, 272)], LOCAL)
    dma("Y", "ld_z", [(T.ztb[:], T.zt[:])], [], [A("ztb")], LOCAL + 0.3, after="ld_m")
    dma("Y", "ld_t", [(T.tab[:, SPARE:], T.xt[:])], [], [A("tab", SPARE)], LOCAL + CFG["table"] + 0.3, after="ld_z")

    iota("i_p", A("pi"), [[0, 1]], 0, 1)
    iota("i_l1c", A("lio", L1, L1 + 2), [[0, 2]], 143)
    iota("i_l1", A("lio", L1 + 2, L1 + 18), [[-16, 8], [0, 2]], 127)
    iota("i_l2", A("lio", L2, L2 + 20), [[256, 2], [2, 10]], 30)
    iota("i_ci", A("ci"), [[1, 144]], 0)
    iota("i_b2", A("b2"), [[0, 8], [2, WORLD]], -31)
    iota("i_cs", A("cs", 0, 8 * SHIFTS), [[16, 8], [1, SHIFTS]], 0)
    iota("i_c16", A("c16"), [[0, 8], [1, 16]], 0)
    iota("i_cg", A("cg"), [[16, 8], [0, 16]], 0)
    iota("i_c32", A("c32"), [[0, 4], [1, 32]], 0)
    for i in range(4):
        iota("i_nx%d" % i, A("nxb", 1024 * i, 1024 * i + 1024), [[0, 1024]], 0, after="i_cg")
    iota("i_lf1", A("lio", LF1, LF1 + 16), [[1, 8], [0, 2]], 0)
    iota("i_lf2", A("lio", LF2, LF2 + 8), [[-32, 8]], 239)
    iota("i_cg8", A("cg8"), [[16, 8], [-1000, 2], [0, 8]], 1000)
    for i, m in enumerate((7, 8, 16, 15, 112, 127, SHIFTS - 1, 16 - SHIFTS)):
        ts("p%d" % (i + 14 * (i > 5)), A("pb", i, i + 1), A("pi"), m, ALU.bitwise_and)
    cp("pc", A("pc", 0, 6), A("pb", 0, 6))
    cp("pd", A("pc", 12, 14), A("pb", 6, 8))
    ts("l1", lst(L1, 18), A("lio", L1, L1 + 18), pc(3), ALU.subtract)
    ts("lz", lst(LZ, 8), A("lio", L1 + 2, L1 + 18, 2), pc(3), ALU.subtract)
    ts("p6", pc(6), pc(0), 32.0, ALU.mult, pc(2), ALU.add)
    ts("p7", pc(7), pc(1), 0.125, ALU.mult, pc(6), ALU.add)
    for h in range(2):
        ts("l2%d" % h, lst(L2 + 10 * h + 1, 9), A("lio", L2 + 10 * h + 1, L2 + 10 * h + 10), pc(7), ALU.add)
        ts("lc%d" % h, lst(L2 + 10 * h, 1), pc(2), pc(0), ALU.subtract, 15.0 - 8 * h, ALU.add)
    ts("lj", lst(LJ, 4), A("lio", L1 + 2, L1 + 6), 0.0, ALU.mult, pc(0), ALU.add)
    ts("cj", A("cj", 0, 8), A("ci", 0, 8), 124.0, ALU.add)
    ts("cjp", A("cj", 8, 16), A("ci", 0, 128, 16), pc(3), ALU.add)
    ts("cjq", A("cj", 16, 32), A("ci", 0, 16), 8.0, ALU.is_ge, 1984.0, ALU.mult)
    ts("idn", A("idn"), A("ci", 0, 128), pc(5), ALU.is_equal)
    act("nid", A("nid"), A("idn"), AF.Identity, scale=-1.0)
    ts("p8", pc(8), pc(4), 15.0, ALU.add)
    ts("wd", A("wd"), A("ci"), pc(8), ALU.is_equal, 256.0, ALU.mult)
    ts("s8", A("s8"), A("ci", 0, 128, 16), pc(4), ALU.is_equal, 64.0, ALU.mult)
    act("ns8", A("ns8"), A("s8"), AF.Identity, scale=-1.0)
    ts("pa", pc(11), pc(12), pc(4), ALU.add)
    ts("sj0", A("sj", 0, 8 * SHIFTS), A("cs", 0, 8 * SHIFTS), pc(11), ALU.is_equal, 4.0, ALU.mult)
    act("sj1", A("sj", 8 * SHIFTS, 16 * SHIFTS), A("sj", 0, 8 * SHIFTS), AF.Identity, scale=16.0)
    for i in range(2):
        ts("ps%d" % i, A("quad", 4 * i, 4 * i + PARTS), A("ci", 0, 16, SHIFTS), pc(13), ALU.is_equal, (3.0 - 6 * i) * 2 ** 28, ALU.mult)
    fill("one", A("one"), 1.0)
    act("anew", A("anew"), A("b2"), AF.Relu, scale=-1.0e6, bias=-30.0e6)
    for r in range(PARTS):
        for i in range(2):
            act("up%d%d" % (r, i), A("anew", 32 + 2 * r + i, KEYS, WORLD), A("one", 0, 8), AF.Identity, scale=A("quad", 4 * i + r, 4 * i + r + 1))
    act("b1", A("b1"), A("b2"), AF.Sign)
    act("idk", A("idk"), A("idn"), AF.Identity, scale=129.0)
    act("idw", A("idw"), A("idn"), AF.Identity, scale=-2048.0)
    fill("bx", A("bx"), 0.0)
    ts("blk", A("blk"), A("cg"), pc(4), ALU.is_equal)
    act("wh", A("wh"), A("wd"), AF.Identity, scale=1.0 / 256)
    ts("blk8", A("blk8"), A("cg8"), pc(4), ALU.is_equal)
    ts("dia", A("dia"), A("c16"), pc(3), ALU.is_equal)
    act("rst", A("rst"), A("dia"), AF.Identity, scale=-1.0, bias=1.0)
    ts("die", A("die"), A("c32"), pc(3), ALU.is_equal)
    act("rse", A("rse"), A("die"), AF.Identity, scale=-1.0, bias=1.0)
    ts("p10", pc(10), pc(3), 16.0, ALU.add)
    act("diep", A("pq", 256, 384), A("die"), AF.Identity, scale=32768.0, bias=pc(3))
    act("dim", A("dim"), A("dia"), AF.Identity, scale=32768.0, bias=pc(10))
    act("cq", A("cq"), A("c16"), AF.Identity, bias=-360.0)
    act("id8", A("id8"), A("idn"), AF.Copy)
    fill("b0a", A("b1", 32, KEYS, WORLD), -2.0 ** 20)
    for i in range(1, 2 * PARTS):
        act("b0%d" % i, A("b1", 32 + i, KEYS, WORLD), A("b1", 32, KEYS, WORLD), AF.Copy)
    act("diap", A("pq", 128, 256), A("dia"), AF.Copy)
    act("idf", A("idf"), A("idn"), AF.Copy)
    act("nif", A("nif"), A("nid"), AF.Copy)
    fill("m160", A("m160"), -160.0)
    fill("tiny", A("tiny"), -1.0 / 2048)
    ts("p9", pc(9), pc(3), 8.0, ALU.mult)
    ts("lf1", lst(LF1, 16), A("lio", LF1, LF1 + 16), pc(9), ALU.add)
    ts("lf2", lst(LF2, 8), A("lio", LF2, LF2 + 8), pc(2), ALU.add, pc(3), ALU.subtract)

    act("y_c", A("yf", 128, 144), A("inb", 256, 272), AF.Identity, scale=2.0, bias=2 * 28672.0)
    for h in range(2):
        lanes = lambda b: A(b, 128 - 128 * h, 256 - 128 * h)
        d0, d1 = (0, 288) if h == 0 else (288, 544)
        ts("y_s%d" % h, lanes("sb"), lanes("inb"), 1, ALU.bitwise_and)
        ts("y_g%d" % h, lanes("sg"), lanes("sb"), 24577.0, ALU.mult)
        tt("y_m%d" % h, A("yf", 144 * h, 144 * h + 128), lanes("sg"), lanes("inb"), ALU.subtract)
        act("y_d%d" % h, A("dup", d0, d1), IND(A("yf", 144 * h, 144 + 128 * h), lst(L1 + 2 * h, 18 - 2 * h)), AF.Abs, scale=0.5)
        turn("y_t%d" % h, A("trp", d0, d1), A("dup", d0, d1))
        act("y_l%d" % h, msg(h, 0, 144), IND(A("trp", 0, d1), lst(L2 + 10 * h, 9)), AF.Identity, bias=-6144.0)
        act("z_l%d" % h, zin(h), IND(lanes("ztb"), lst(LZ, 8)), AF.Copy)
    dma("Y", "ld_nx", [(T.nxb[0:128:16, :], T.nxt[:])], [], [A("nxb")], LOCAL + 0.5, after="ld_t")

    prev, part = (rank - 1) % N, rank ^ 1

    def alike(n, h, zown, zp, back=None):
        mm("ad" + n, [(A("pa", 0, 128), A("idn"), zown, True, False), (A("pa", 0, 128), A("nid"), zp, False, True)])
        a1, a2 = A("al1", 128 * h, 128 * h + 128), A("al2", 128 * h, 128 * h + 128)
        act("a1" + n, a1, A("pa", 0, 128), AF.Abs)
        act("a2" + n, a2, IND(a1, back) if back else a1, AF.Sign, bias=10.5, scale=-1.0)
        return a2

    def exchange(t, h):
        n, s, src = "%d%d" % (t, h), 2 * t + h, prev ^ 1
        own = msg(s, 80, 144)
        if src == rank:
            zp, yp = A("zout", 128 * (s - 2), 128 * (s - 1)), msg(s - 2, 72, 136)
        else:
            zp, yp = A("pz", 128 * s, 128 * s + 128), A("pmsg", 120 * s + 56, 120 * s + 120)
            recv("mid", t, h, src, "bz" + n)
            recv("early", t, h, src, "be" + n)
        H = lambda b, k=128: A(b, k * h, k * h + k)
        sel16("as" + n, A("pa", 128, 136), alike(n, h, zin(s), zp))
        act("ak" + n, H("alk", 8), A("pa", 128, 136), AF.Sign, bias=-128.0)
        act("ar" + n, H("dif", 64), IND(H("alk", 8), lst(LJ, 4)), AF.Relu)
        mm("df" + n, [(A("ps", 64, 128), A("idf"), yp, True, False), (A("ps", 64, 128), A("nif"), own, False, True)])
        tt("dm" + n, A("ps", 128, 192), A("ps", 64, 128), H("dif", 64), ALU.mult)
        tt("sw" + n, own, A("ps", 128, 192), own, ALU.add)

    def prep(t, h):
        n, s = "%d%d" % (t, h), 2 * t + h
        m0, z0 = SLOT * s + 64, 512 * s
        if t > 0:
            recv("mid", t, h, prev, "az" + n)
            recv("late", t, h, prev, "ac" + n)
            recv("early", t, h, prev, "ae" + n)
        shift("V" if t else "S", "zb" + n, A("zb", 128 * s, 128 * s + 128), zin(s), 192.0)
        if t:
            dma("Y", "du" + n, [(T.zin[:, z0 + 128 * r:z0 + 128 * r + 128], T.zin[:, z0:z0 + 128]) for r in range(1, 4)],
                [zin(s)], [A("zin", z0 + 128, z0 + 512)], LOCAL + 0.4)
        else:
            for i in range(2):
                act("d%d%s" % (i + 1, n), A("zin", z0 + (128 << i), z0 + (256 << i)), A("zin", z0, z0 + (128 << i)), AF.Copy)
        c = IND(A("msg", m0 + 8, m0 + 16), lst(LJ, 4))
        for b in range(2):
            if CFG["cs" if t else "cs0"][h] == "SH"[b]:
                act("cr" + n, A("crp", 64 * h, 64 * h + 64), c, AF.Copy)
                mm("cp" + n, [(A("ps", 0, 64), A("idf"), A("crp", 64 * h, 64 * h + 64), True, True)])
                c = A("ps", 0, 64)
            if t and CFG["cs"][h] == "R" and not b:
                mm("cp" + n, [(A("ps", 0, 64), A("idf"), msg(s, -56, 8), True, True)])
                c = A("ps", 0, 64)
            if b and t > 0:
                exchange(t, h)
            if b and t + 1 < RO:
                send("early", t, h)
            y = A("msg", m0 + 16 + 64 * b, m0 + 80 + 64 * b)
            for kind in range(2):
                o, nb = 256 * h + 128 * kind + 64 * b, "%s%d%d" % (n, b, kind)
                tt("ta" + nb, A("t32", o, o + 64), c, y, ALU.subtract if kind else ALU.add)
                ts("to" + nb, A("o32", o, o + 64), A("t32", o, o + 64), 16384 | 4095, ALU.bitwise_and)
                ts("tu" + nb, A("o16", o, o + 64), A("o32", o, o + 64), BASE, ALU.add)

    nr2 = [0]

    def main(t, h):
        n, s, key = "%d%d" % (t, h), 2 * t + h, "key%d" % h
        z1, zb = zin(s), A("zb", 128 * s, 128 * s + 128)
        mm("kb" + n, [(A(key, 0, KEYS), A(w), A(b), b == "b2", False) for w, b in (("idk", "b2"), ("idw", "b1"))])
        col = lambda c: A(key, c, KEYS, WORLD)
        for u, (r, c0, m) in enumerate(calls(t, h)):
            nu = "%s%x" % (n, u)
            gath = IND(A("tab", SPARE), A("o16", 256 * h + 8 * c0, 256 * h + 8 * (c0 + m)))
            o = 4096 * h + 128 * c0
            G = lambda b, i=0, k=m: A(b, o + 128 * i, o + 128 * (i + k))
            if r in "AB":
                tt("mg" + nu, G("gb"), gath, zin(s, m), ALU.subtract)
            elif r == "C":
                act("mg" + nu, G("ab"), gath, AF.Copy)
            else:
                act("mg" + nu, G("ab"), gath, AF.Identity, bias=192.0)
            for i0 in range(0, m, 4):
                k, nv = min(4, m - i0), nu + ("b" if i0 else "")
                if r == "D":
                    scan("md" + nv, [(G("gb", i, 1), G("ab", i, 1), zb) for i in range(i0, i0 + k)], ALU.max, ALU.subtract)
                if r in "AD":
                    ts("ma" + nv, G("ab", i0, k), G("gb", i0, k), 0.0, ALU.max, 2.0, ALU.mult)
                elif r == "B":
                    act("ma" + nv, G("ab", i0, k), G("gb", i0, k), AF.Abs)
                else:
                    pd = "pd%d" % (nr2[0] % 2); nr2[0] += 1
                    mm("md" + nv, [(A(pd, 0, 128 * k), A("idn"), G("ab", i0, k), True, False)]
                       + [(A(pd, 128 * i, 128 * i + 128), A("nid"), z1, False, i == k - 1) for i in range(k)])
                    act("ma" + nv, G("gb", i0, k), A(pd, 0, 128 * k), AF.Abs)
                for name, b, sel in (("mw", "gb", "ns8"), ("ms", "gb" if r == "C" else "ab", "s8")):
                    if name == "ms" or r in "AD":
                        mm(name + nv, [(col(c0 + i), G(b, i, 1), A(sel), False, False) for i in range(i0, i0 + k)], key + n)

    def tail(t, h):
        n, s = "%d%d" % (t, h), 2 * t + h
        m0 = SLOT * s + 64
        H = lambda b, k=128: A(b, k * h, k * h + k)
        last = lambda b, k=16: A(b, 128 * h + k - 1, 128 * h + 128, k)
        key = "key%d" % h
        scan("mn" + n, [(H("kf", KEYS), A("anew"), A(key, 0, KEYS))], ALU.add, ALU.min)
        for r in range(PARTS):
            at = lambda c: A("kf", KEYS * h + c + 2 * r, KEYS * h + KEYS, WORLD)
            o = 144 * h + SHIFTS * (r + 1) - 1
            tt("pt%s%d" % (n, r), A("bx", o, o + 128, 16), at(31), at(33), ALU.subtract)
        pos = A(key, 448, 464)
        pt16, pd16 = A("pt16", 16 * h, 16 * h + 8), A("pt16", 16 * h + 8, 16 * h + 16)
        mm("tq" + n, [(pos, A("idn"), A("cj", 0, 16), True, False), (pos, A("idn"), A("cj", 16, 32), False, False)])
        o = 144 * h + SHIFTS - 1
        mm("tr" + n, [(pos, A("bx", o - a, o + 128 - a), A("sj", a, 16 * SHIFTS, SHIFTS), False, a == SHIFTS - 1) for a in range(SHIFTS)])
        cp("pu" + n, H("pt16", 16), pos)
        zo, z1 = A("zout", 128 * s, 128 * s + 128), zin(s)
        plus = lambda o, k: A("m160", 0, k)
        act("zn" + n, zo, IND(H("gb", 4096), pd16), AF.Abs)
        send("mid", t, h)
        tt("xx" + n, H("xx"), IND(H("o32", 256), pt16), A("dim"), ALU.min)
        scan("ff" + n, [(H("ff"), A("rst"), H("xx"))], ALU.mult, ALU.max)
        ts("qq" + n, H("q16", 8), last("ff"), BASE, ALU.add)
        qr = A(key, KEYS, KEYS + 128)
        mm("qc" + n, [(qr, A("id8"), A("cq"), True, False)])
        mm("qr" + n, [(qr, A("blk"), H("xx"), False, True)])
        tt("ne" + n, H("ne"), qr, H("ff"), ALU.not_equal)
        wide, o0 = int(CFG["wide"][h]), 256 * h
        scan("rr" + n, [(A("off16", o0 + 1, o0 + 1 + 128 * wide, wide), H("ne"), H("xx"))], ALU.mult, ALU.max)
        if wide == 2:
            tt("xe" + n, H("xe"), A("pq", 256, 384), H("xx"), ALU.min)
            scan("fe" + n, [(H("fe"), A("rse"), H("xe"))], ALU.mult, ALU.max)
            tt("nf" + n, H("nf"), qr, H("fe"), ALU.not_equal)
            scan("rf" + n, [(A("off16", o0, o0 + 256, 2), H("nf"), H("xe"))], ALU.mult, ALU.max)
        offs = lambda j: A("off16", o0 + 16 * j + 16, o0 + 16 * j + 17) if wide == 1 else A("off16", o0 + 64 * j + 62, o0 + 64 * j + 64)
        if t + 1 < RO:
            act("ng" + n, H("nxg"), IND(A("nxb"), H("q16", 8)), AF.Identity, bias=-2048.0)
            sel16("cs" + n, A("pn", 0, 8), H("nxg"), "wh")
            act("cn" + n, A("msg", m0, m0 + 8), A("pn", 0, 8), AF.Identity, bias=22528.0 + 16 * 2048)
            if CFG["cs"][h] == "R":
                act("cw" + n, msg(s, -64, 0), IND(msg(s, 0, 8), lst(LJ, 4)), AF.Copy)
        else:
            act("ng" + n, H("nxr"), IND(A("nxb"), H("q16", 8)), AF.Copy)
        if "C" in routes(t, h):
            ss = A("pd0", 128, 256)
            act("gq" + n, H("gq"), IND(A("tab", SPARE), H("q16", 8)), AF.Copy)
            mm("xz" + n, [(ss, A("idn"), H("gq"), True, False), (ss, A("idn"), z1, False, True)])
            act("hv" + n, H("hv"), ss, AF.Identity, bias=159.75, scale=0.5)
        else:
            act("hv" + n, H("hv"), IND(H("gb", 4096), pd16), AF.Identity, bias=-192.25, scale=0.5)
            plus = lambda o, k: A("zb", 128 * s + o, 128 * s + o + k)
        if CFG["x2"][h] == "V":
            tt("x2" + n, H("x2"), IND(H("t32", 256), pt16), A("dia"), ALU.mult)
        else:
            act("g2" + n, H("g2"), IND(H("t32", 256), pt16), AF.Copy)
            tt("x2" + n, H("x2"), A("pq", 128, 256), H("g2"), ALU.mult)
        scan("f2" + n, [(H("f2"), A("rst"), H("x2"))], ALU.mult, ALU.max)
        tt("vn" + n, A("msg", m0 + 8, m0 + 16), last("f2"), A("msg", m0 + 8, m0 + 16), ALU.subtract)
        if t + 1 < RO:
            send("late", t, h)
        k = 16 * wide
        return lambda: [tt("sc%s%d" % (n, j), IND(A("tab"), offs(j)),
                           A("hv", 128 * h + k * j, 128 * h + k * j + k), plus(k * j, k), ALU.add) for j in range(8 // wide)]

    def penalty(t):
        n = str(t)
        k = 18 * PARTS
        ts("kd" + n, A("kind", 0, k), A("bx", SHIFTS - 1, 288, SHIFTS), 1.0, ALU.is_ge)
        mm("c1" + n, [(A("pd1", 384, 384 + k), A("one"), A("kind", 0, k), True, True)])
        act("c2" + n, A("cnj", 0, k), A("pd1", 384, 384 + k), AF.Identity, bias=-64.0 * 4608 / k, scale=-64.0, acc=A("cnt"))
        act("c3" + n, A("cnf"), A("tiny"), AF.Identity, bias=-0.484375, scale=A("cnt"))
        act("c4" + n, A("anew", 16, KEYS, WORLD), A("cnf"), AF.Identity, bias=A("cnt"), scale=2048.0)

    def finish(h):
        s, n = 2 * (RO - 1) + h, "%d%d" % (RO, h)
        H = lambda b, k=128: A(b, k * h, k * h + k)
        lanes = lambda b: A(b, 128 - 128 * h, 256 - 128 * h)
        pd = "pd%d" % h
        act("o_d%d" % h, H("dup", 256), IND(msg(s, 8, 136), lst(LF1, 16)), AF.Copy)
        turn("o_t%d" % h, H("trp", 256), H("dup", 256))
        act("o_h%d" % h, H("oh1"), IND(H("trp", 256), lst(LF2, 8)), AF.Abs, bias=-0.5, scale=2.0)
        act("o_m%d" % h, lanes("oh"), H("oh1"), AF.Identity, bias=12288.5, scale=-1.0)
        send("early", RO - 1, h)
        recv("mid", RO, h, part, "bz" + n)
        recv("early", RO, h, part, "be" + n)
        a2 = alike(n, h, A("zout", 128 * s, 128 * s + 128), A("pz", 128 * (s + 2), 128 * (s + 3)), lst(LZ, 8))
        mm("as" + n, [(A("pa", 128, 256), A("blk8"), a2, True, True)])
        ts("ak" + n, A(pd, 0, 128), A("pa", 128, 256), 1.0, ALU.is_ge)
        ts("an" + n, A(pd, 128, 256), A("pa", 128, 256), 1.0, ALU.is_lt)
        tt("o_k%d" % h, H("keep"), A(pd, 128, 256), lanes("oh"), ALU.mult)
        tt("o_p%d" % h, A(pd, 256, 384), A(pd, 0, 128), lanes("ph"), ALU.mult)
        tt("o_s%d" % h, lanes("ohs"), A(pd, 256, 384), H("keep"), ALU.add)
        dma("S", "st_h%d" % h, [(T.yh[:, 128 - 128 * h:256 - 128 * h], T.ohs[:, 128 - 128 * h:256 - 128 * h])], [lanes("ohs")], [], LOCAL)
        act("o_z%d" % h, lanes("oz"), IND(A("zout", 128 * s, 128 * s + 128), lst(LZ, 8)), AF.Copy)
        act("o_c%d" % h, lanes("oc"), IND(H("nxr"), lst(LZ, 8)), AF.Copy)

    visits.append(True)
    for t in range(RO):
        prep(t, 0); main(t, 0); prep(t, 1)
        s0 = tail(t, 0)
        main(t, 1)
        s1 = tail(t, 1)
        s0(); s1()
        if t + 1 < RO:
            penalty(t)
    visits.pop()
    dma("Y", "st_x", [(T.yx[:], T.tab[:, SPARE:])], [A("tab", SPARE)], [], LOCAL + CFG["table"])
    finish(0); finish(1)
    dma("Y", "st_z", [(T.yz[:], T.oz[:])], [A("oz")], [], LOCAL)
    dma("Y", "st_c", [(T.yc[:], T.oc[0:128:16, :])], [A("oc")], [], LOCAL)
    return ops


def hazards(ops):
    hist = {}
    deps = []
    for i, o in enumerate(ops):
        d = {}
        for kind, regs in (("r", o["rd"]), ("w", o["wr"])):
            for b, lo, hi, st in regs:
                psum = SCRATCH[b][0] == "psum"
                for j, k2, l2, h2, s2 in hist.get(b, ()):
                    same = ops[j]["q"] == o["q"] and o["q"] in ("V", "S", "P", "G") and ops[j]["sem"] is None
                    clash = l2 < hi and lo < h2 and (kind == "w" or k2 == "w") and not (st == s2 and (lo - l2) % st)
                    if psum and o.get("grp") and ops[j].get("grp") == o["grp"]:
                        continue
                    if psum:
                        d[j] = d.get(j, False) or not same or (clash and o["q"] != "P")
                    elif clash:
                        d[j] = True
        for kind, regs in (("r", o["rd"]), ("w", o["wr"])):
            for b, lo, hi, st in regs:
                hh = hist.setdefault(b, [])
                if SCRATCH[b][0] == "psum":
                    hh[:] = [e for e in hh if ops[e[0]]["q"] == o["q"]]
                elif kind == "w":
                    hh[:] = [e for e in hh if not (lo <= e[2] and e[3] <= hi and (st == 1 or (st == e[4] and (lo - e[2]) % st == 0))) or e[0] == i]
                hh.append((i, kind, lo, hi, st))
        d.pop(i, None)
        deps.append(d)
    return deps


def plan(T, topo):
    ops = build(T, topo, 0)
    n = len(ops)
    idx = {o["name"]: i for i, o in enumerate(ops)}
    pre = [dict(d) for d in hazards(ops)]
    for i, o in enumerate(ops):
        if o["after"]:
            pre[i][idx[o["after"]]] = o["q"] is None
    seen = {}

    def waited(i):
        if i not in seen:
            through = 0
            for j in pre[i]:
                through |= waited(j)
            seen[i] = through | sum(1 << j for j, w in pre[i].items() if w)
            pre[i] = {j: w for j, w in pre[i].items() if not through >> j & 1}
        return seen[i]
    for i in range(n):
        waited(i)
    qs = [o["q"] for o in ops]
    nets = []
    for p in PACE:
        os_ = build(T, topo, 0, p)
        cost, lat = [max(o["cost"], 1e-4) for o in os_], [o["lat"] for o in os_]
        before = [[(j, lat[j] + p["hop"] if w else 0.0) for j, w in pre[i].items()] for i in range(n)]
        behind = [[] for _ in ops]
        for i in range(n):
            for j, gap in before[i]:
                behind[j].append((i, gap))
        nets.append((cost, lat, before, behind))

    def place(net, key, back):
        cost, lat, before, behind = net
        if back:
            before, behind = behind, before
        left = [len(b) for b in before]
        ready = list(lat) if back else [0.0] * n
        start = [0.0] * n
        free = {q: 0.0 for q in qs}
        avail = {q: [i for i in range(n) if qs[i] == q and not left[i]] for q in free}
        for _ in range(n):
            st, q = 1e9, None
            for q2, l in avail.items():
                if l:
                    t = max(free[q2], min([ready[i] for i in l]))
                    if t < st:
                        st, q = t, q2
            i = min([i for i in avail[q] if ready[i] <= st], key=lambda i: key[i])
            avail[q].remove(i)
            start[i] = st
            st += cost[i]
            if q:
                free[q] = st
            for k, gap in behind[i]:
                ready[k] = max(ready[k], st + gap)
                left[k] -= 1
                if not left[k]:
                    avail[qs[k]].append(k)
        return start

    def times(start):
        order = sorted(range(n), key=lambda i: (start[i], i))
        out = []
        for cost, lat, before, _ in nets:
            end, free = [0.0] * n, {}
            for i in order:
                end[i] = free[qs[i]] = max([free.get(qs[i], 0.0) if qs[i] else 0.0] + [end[j] + gap for j, gap in before[i]]) + cost[i]
            out.append(max(end[i] + lat[i] for i in range(n)))
        return out

    cost, lat, before, behind = nets[0]
    way = [0.0] * n
    left = [len(b) for b in behind]
    todo = [i for i in range(n) if not left[i]]
    for i in todo:
        way[i] = cost[i] + max([lat[i]] + [way[k] + gap for k, gap in behind[i]])
        for j, _ in before[i]:
            left[j] -= 1
            if not left[j]:
                todo.append(j)
    best = place(nets[0], [max(way) - x for x in way], False)
    unit = times(best)
    score = float(len(nets))
    seed = [CFG["seed"]]

    def draw():
        seed[0] = (seed[0] * 1103515245 + 12345) % 2147483648
        return seed[0] / 2147483648.0
    for r in range(CFG["rounds"]):
        net, size, mid, span = nets[r % len(nets)], draw() ** 2 * 2, draw() * max(best), 100.0 * draw() ** 2 + 3
        key = [x + (size * (draw() - 0.5) if abs(x - mid) < span else 0.0) for x in best]
        if r < 12 or draw() < 0.3:
            back = place(net, [-x for x in key], True)
            key = [-(back[i] + net[0][i]) for i in range(n)]
        start = place(net, key, False)
        new = sum(a / b for a, b in zip(times(start), unit))
        if new <= score:
            best, score = start, new

    twin = {o["role"]: i for i, o in enumerate(ops) if o["role"]}
    succ = [[k for k, _ in b] for b in nets[0][3]]
    qi = [" VSPGY".index(q or " ") for q in qs]

    def run(order, net, trace=False):
        cost, lat, before, _ = net
        end, free, top, why, last, at = [0.0] * n, [0.0] * 6, 0.0, {}, [None] * 6, None
        for i in order:
            q = qi[i]
            s, w = free[q], -1
            for j, gap in before[i]:
                if end[j] + gap >= s:
                    s, w = end[j] + gap, j
            s += cost[i]
            end[i] = s
            if q:
                free[q] = s
            if trace:
                why[i], last[q] = (w, last[q]), i
            if s + lat[i] > top:
                top, at = s + lat[i], i
        if trace is None:
            return end
        if not trace:
            return top
        arcs = []
        while at is not None:
            w, front = why[at]
            if w < 0 and front is not None and qi[at]:
                arcs.append((front, at))
            at = w if w >= 0 else front if qi[at] else None
        return arcs

    order = kept = sorted(range(n), key=lambda i: (best[i], i))
    now = [run(order, net) / u for net, u in zip(nets, unit)]
    low, arcs = sum(now), None
    def alike(order, model, visits):
        end = run(order, nets[0], None)
        at = [end[twin["sc13", t]] for t in range(RO)]
        key = end[:]
        for i, o in enumerate(ops):
            if o["role"] and o["role"][1] in visits and (o["role"][0], model) in twin:
                t = o["role"][1]
                key[i] = end[twin[o["role"][0], model]] - at[model] + at[t]
        for i in order:
            key[i] = max([key[i]] + [key[j] + 1e-6 for j in pre[i]])
        return sorted(order, key=lambda i: key[i])

    for r in range(CFG["swaps"]):
        if r % CFG["copy"] == CFG["copy"] // 2:
            for model in range(1, RO):
                for visits in (range(1, RO - 1), range(1, RO), range(RO)):
                    new = alike(order, model, visits)
                    got = [run(new, net) / u for net, u in zip(nets, unit)]
                    if sum(got) < sum(now):
                        order, now, arcs = new, got, None
        if arcs is None:
            arcs = [run(order, net, True) for net in nets]
            key, place_in, line = [0.0] * n, [0] * n, [[] for _ in range(6)]
            for k, i in enumerate(order):
                key[i], place_in[i] = k, len(line[qi[i]])
                line[qi[i]].append(i)
        first = int(draw() * len(nets))
        a, b = arcs[first][int(draw() * len(arcs[first]))]
        free = draw() < CFG["free"]
        if free:
            l = line[1 + int(draw() * 3)]
            k = 1 + int(draw() * (len(l) - 1))
            a, b = l[k - 1], l[k]
        far, l = int(draw() ** 2 * CFG["far"]), line[qi[a]]
        if free or draw() < 0.5:
            pairs, d = [(b, l[max(0, place_in[a] - far)])], -0.5
        else:
            pairs, d = [(a, l[min(len(l) - 1, place_in[b] + far)])], 0.5
        x, y = ops[pairs[0][0]]["role"], ops[pairs[0][1]]["role"]
        if x and y and draw() < CFG["all"]:
            pairs = [(twin[x[0], x[1] + e], twin[y[0], y[1] + e]) for e in range(-RO, RO) if (x[0], x[1] + e) in twin and (y[0], y[1] + e) in twin]
        k2 = key[:]
        for i, j in pairs:
            if (key[j] - k2[i]) * d < 0:
                continue
            k2[i], todo = key[j] + d, [i]
            for i in todo:
                for j in pre[i] if d < 0 else succ[i]:
                    if (k2[j] - k2[i]) * d <= 0:
                        k2[j] = k2[i] + d / 64
                        todo.append(j)
        new, room, got = sorted(order, key=lambda i: k2[i]), -CFG["heat"] * (1 - r / CFG["swaps"]) ** 2 * math.log(draw() + 1e-9), now[:]
        for m in range(len(nets)):
            m = (m + first) % len(nets)
            got[m] = run(new, nets[m]) / unit[m]
            if sum(got) > sum(now) + room + 0.004:
                break
        if sum(got) <= sum(now) + room:
            order, now, arcs = new, got, None
            if sum(now) < low:
                low, kept = sum(now), order
    return {ops[i]["name"]: k for k, i in enumerate(kept)}, [max(e + x for e, x in zip(run(kept, net, None), net[1])) for net in nets]


ORDER = {}


def rank_program(g, core, T, topo):
    rank = T.rank_of(core)
    if rank is None:
        return
    if not ORDER:
        ORDER.update(plan(T, topo)[0])
    ops = build(T, topo, rank)
    deps = hazards(ops)
    queue = {"V": g.vector, "S": g.scalar, "P": g.tensor, "G": g, "Y": g.sync}
    count = {"V": 0, "S": 0, "P": 0, "G": 0}
    known = {q: {} for q in queue}
    done = {}
    sent = 0
    order = sorted(range(len(ops)), key=lambda i: ORDER[ops[i]["name"]])
    closer = {ops[i]["grp"]: i for i in order if ops[i].get("grp")}
    for i in order:
        o = ops[i]
        q = o["q"]
        if q is None:
            done[i] = (o["sem"], o["val"], {o["sem"]: o["val"]})
            continue
        kn = known[q]
        need = sorted((done[j] for j, w in deps[i].items() if w), key=lambda d: -len(d[2]))
        want = {}
        for sem, val, clock in need:
            if kn.get(sem, 0) < val:
                want[sem] = max(want.get(sem, 0), val)
        for sem, val, clock in need:
            if want.get(sem) == val and kn.get(sem, 0) < val:
                queue[q].wait_ge(T.sem[sem], val)
                for s2, v2 in clock.items():
                    kn[s2] = max(kn.get(s2, 0), v2)
        ins = o["fn"](g, True) if closer.get(o.get("grp")) == i else o["fn"](g)
        if o["sem"] == "sent":
            sent += o["val"]
            continue
        if o["sem"]:
            for x in ins:
                x.then_inc(T.sem[o["sem"]], 16)
            sem, val = o["sem"], o["val"]
        else:
            for x in ins:
                x.then_inc(T.sem["c" + q], 1)
            count[q] += len(ins)
            sem, val = "c" + q, count[q]
        clock = dict(kn)
        clock[sem] = val
        done[i] = (sem, val, clock)
    g.wait_ge(T.sem.sent, sent)
    for q in count:
        g.wait_ge(T.sem["c" + q], count[q])
    for o in ops:
        if o["sem"] in STORES:
            g.wait_ge(T.sem[o["sem"]], o["val"])
